import numpy as np
import ml_dtypes


def mxq(x, axis, fmt="e4m3"):
    dtype, down = {"e4m3": (ml_dtypes.float8_e4m3fn, 7), "e5m2": (ml_dtypes.float8_e5m2, 14)}[fmt]
    v = np.moveaxis(np.asarray(x, np.float32).astype(ml_dtypes.bfloat16).astype(np.float64), axis, -1)
    blocks = v.reshape(v.shape[:-1] + (-1, 32))
    amax = np.abs(blocks).max(-1, keepdims=True)
    byte = np.maximum(np.where(amax > 0, np.frexp(amax)[1] - 1 + 127, 0) - down, 1)
    scale = np.exp2(byte - 127.0)
    codes = (blocks / scale).astype(np.float32).astype(dtype).astype(np.float64)
    return np.moveaxis((codes * scale).reshape(v.shape), -1, axis)


WIDE = False


def mx_kscale(k):
    if not WIDE:
        return np.ones(k)
    levels = np.array([24, -24, 12, -12, 0])
    if k % 512:
        return np.exp2(np.random.permutation(np.resize(levels, k // 32))).repeat(32)
    a = np.empty((k // 512, 16))
    for p in range(k // 512):
        a[p, :8] = np.random.permutation(np.resize(levels, 8))
        for g in range(8):
            far = levels[np.abs(levels - a[p, g]) >= 10]
            a[p, g + 8] = far[np.random.randint(len(far))]
    return np.exp2(a.ravel()).repeat(32)


def f64(x):
    return np.asarray(x).astype(np.float64)


def striped(idx):
    return np.tile(idx.reshape(-1, 16).T, (8, 1)).astype(np.uint16)


def unstriped(offs):
    return offs[:16].T.reshape(-1).astype(np.int64)


E2M1 = np.array([0.0, 0.5, 1.0, 1.5, 2.0, 3.0, 4.0, 6.0, -0.0, -0.5, -1.0, -1.5, -2.0, -3.0, -4.0, -6.0])


def pack_weight(w, fmt):
    k, n = w.shape
    w = f64(np.asarray(w, np.float32).astype(ml_dtypes.bfloat16)).reshape(k // 32, 32, n)
    amax = np.abs(w).max(1)
    if fmt == "e4m3":
        byte = np.frexp(amax)[1] - 1 + 127 - 7
    else:
        mant, ex = np.frexp(amax / 6.0)
        byte = np.where(mant > 0.5, ex, ex - 1) + 127
    byte = np.clip(np.where(amax > 0, byte, 1), 1, 254)
    scaled = (w * np.exp2(127.0 - byte)[:, None, :]).reshape(k, n).astype(np.float32)
    by_word = np.ascontiguousarray(scaled.reshape(k // 512, 128, 4, n).transpose(0, 1, 3, 2))
    if fmt == "e4m3":
        words = by_word.astype(ml_dtypes.float8_e4m3fn).view(np.uint8)
    else:
        c = by_word.astype(ml_dtypes.float4_e2m1fn).view(np.uint8) & 0xF
        words = (c[..., 0::2] | (c[..., 1::2] << 4)).reshape(k // 512, 128, 2 * n)
    return np.ascontiguousarray(words), np.ascontiguousarray(byte.astype(np.uint8).reshape(k // 512, 16, n))


def unpack_weight(words, scales, fmt):
    g, _, n = scales.shape
    words = np.ascontiguousarray(words).reshape(g, 128, n, -1)
    if fmt == "e4m3":
        vals = words.view(ml_dtypes.float8_e4m3fn).astype(np.float64)
    else:
        nib = np.empty((g, 128, n, 4), np.uint8)
        nib[..., 0::2] = words & 0xF
        nib[..., 1::2] = words >> 4
        vals = E2M1[nib]
    vals = vals * np.repeat(np.exp2(scales.astype(np.float64) - 127.0), 8, axis=1)[..., None]
    return vals.transpose(0, 1, 3, 2).reshape(g * 512, n)


def pack_table4(v):
    words, scales = pack_weight(v, "e2m1")
    g, t = words.shape[0] // 2, v.shape[1]
    return np.ascontiguousarray(words.reshape(g, 2, 128, t, 2).transpose(0, 2, 3, 1, 4).reshape(g, 128, t, 4)), scales


def unpack_table4(words, scales):
    g, _, t, _ = words.shape
    return unpack_weight(words.reshape(g, 128, t, 2, 2).transpose(0, 3, 1, 2, 4).reshape(2 * g, 128, 2 * t), scales, "e2m1")


K, F, N, T, J = 1024, 1024, 256, 4096, 1024


def setup_inputs():
    n = np.random.standard_normal
    s = mx_kscale(K)[:, None]
    u = mx_kscale(F)[:, None]
    p_tab = pack_table4(n((K, T)) * s)
    p_co = pack_weight(n((K, F)) / np.sqrt(K) / s, "e4m3")
    p_si = pack_weight(n((K, F)) / np.sqrt(K) / s, "e4m3")
    return {
        "tab_words": p_tab[0],
        "tab_scales": p_tab[1],
        "co_words": p_co[0],
        "co_scales": p_co[1],
        "si_words": p_si[0],
        "si_scales": p_si[1],
        "gn": (np.random.uniform(0.5, 2.0, F) * u[:, 0]).astype(np.float32),
        "fb": (np.abs(n((F, N))) / F / u).astype(np.float32),
        "ts": np.tile(np.exp(0.5 * n(T)), (128, 1)).astype(np.float32),
        "offs": striped(np.random.permutation(T)[:J]),
    }


def reference(tab_words, tab_scales, co_words, co_scales, si_words, si_scales, gn, fb, ts, offs):
    idx = unstriped(offs)
    tab_ = unpack_table4(tab_words, tab_scales)[:, idx]
    co_ = unpack_weight(co_words, co_scales, "e4m3")
    si_ = unpack_weight(si_words, si_scales, "e4m3")
    re = co_.T @ tab_
    im = si_.T @ tab_
    h = f64(gn)[:, None] * ((re) ** 2 + (im) ** 2)
    h_ = mxq(h, 0, "e4m3")
    fb_ = mxq(f64(fb), 0, "e4m3")
    y = fb_.T @ h_
    return y * f64(ts)[0, idx][None, :]

@@ -1,0 +1,231 @@
+from contextlib import ExitStack
+
+import concourse.mybir as mybir
+from concourse.masks import make_identity
+
+K, F, N, T, J = 1024, 1024, 256, 4096, 1024
+FLOPS = 2 * (2 * K * F * J + F * N * J)
+
+F32 = mybir.dt.float32
+BF16 = mybir.dt.bfloat16
+I32 = mybir.dt.int32
+U32 = mybir.dt.uint32
+U16 = mybir.dt.uint16
+U8 = mybir.dt.uint8
+FP8X4 = mybir.dt.float8_e4m3fn_x4
+FP4X4 = mybir.dt.float4_e2m1fn_x4
+ALU = mybir.AluOpType
+ACT = mybir.ActivationFunctionType
+
+P = 128
+W = 512
+HALVES = J // W
+GROUPS = F // 512
+PASSES = K // 512
+
+
+def tile_list_meltab_gain_kernel(
+    tc, tab_words, tab_scales, co_words, co_scales, si_words, si_scales, gn, fb, ts, offs, out
+):
+    nc = tc.nc
+    w_words = (co_words, si_words)
+    w_scales = (co_scales, si_scales)
+
+    with ExitStack() as ctx:
+        keep = ctx.enter_context(tc.tile_pool(name="keep", bufs=1))
+        ring = ctx.enter_context(tc.tile_pool(name="ring", bufs=4))
+        psum = ctx.enter_context(tc.psum_pool(name="psum", bufs=8))
+
+        offsets = keep.tile([P, J // 16], U16, name="offsets")
+        tab = keep.tile([P, T], I32, name="tab", align_bytes=64)
+        tab_sc = keep.tile([P, T], U8, name="tab_sc", align_bytes=64)
+        picked_sc = keep.tile([P, J], U8, name="picked_sc", tag="slot_c", align_bytes=64)
+        v_sc = keep.tile([P, PASSES, J], U8, name="v_sc", align_bytes=64)
+        w_sc_raw = keep.tile([P, 2, PASSES, F], U8, name="w_sc_raw", align_bytes=64)
+        w_sc = keep.tile([P, 2, PASSES, F], U8, name="w_sc", align_bytes=64)
+        gn_rows = keep.tile([P, P], F32, name="gn_rows")
+        ident = keep.tile([P, P], F32, name="ident")
+        w_raw = {}
+        w_q = {}
+        for g in range(GROUPS):
+            for w in range(2):
+                w_q[w, g] = keep.tile([P, PASSES, 4, P], I32, name="w_q%d%d" % (w, g), align_bytes=64)
+
+        nc.vector.memset(w_sc_raw[:].rearrange("p w a f -> p (w a f)").bitcast(I32), 0)
+        nc.vector.memset(tab_sc[32:64, :].bitcast(I32), 0)
+        nc.vector.memset(tab_sc[64:128, :].bitcast(I32), 0)
+        nc.vector.memset(v_sc[:].rearrange("p a j -> p (a j)").bitcast(I32), 0)
+        nc.gpsimd.memset(gn_rows[:], 0.0)
+
+        nc.sync.dma_start(offsets[:], offs)
+        nc.sync.dma_start(tab_sc[0:32, :].bitcast(I32), tab_scales.rearrange("a q t -> (a q) t").bitcast(I32))
+        nc.sync.dma_start(tab[:], tab_words.rearrange("e p t b -> p (e t b)").bitcast(I32))
+        for w in range(2):
+            rows = w_scales[w].bitcast(I32).rearrange("a (u r) f -> r u a f", r=4)
+            for r in range(4):
+                nc.scalar.dma_start(w_sc_raw[r:P:32, w, :, :].bitcast(I32), rows[r])
+        gn_by_tile = gn.rearrange("(g q t r) -> g t q r", g=GROUPS, t=4, r=8)
+        for g in range(GROUPS):
+            nc.gpsimd.dma_start(gn_rows[4 * g : 4 * g + 4, :].rearrange("t (q r) -> t q r", r=8), gn_by_tile[g])
+        make_identity(nc, ident[:])
+
+        def load_weight(w, g, tag):
+            w_raw[w, g] = keep.tile([P, PASSES, W], I32, name="w_raw%d%d" % (w, g), tag=tag, align_bytes=64)
+            words = w_words[w].rearrange("a p f b -> p a (f b)").bitcast(I32)
+            nc.sync.dma_start(w_raw[w, g][:], words[:, :, g * W : (g + 1) * W])
+
+        load_weight(0, 0, "slot_d")
+        load_weight(1, 0, "slot_e")
+
+        nc.vector.tensor_copy(picked_sc[:], tab_sc[:].indirect(offsets[:]))
+        for a in range(PASSES):
+            for r in range(4):
+                nc.scalar.dma_start(v_sc[r:P:32, a, :].bitcast(I32), picked_sc[16 * a + r : 16 * a + 16 : 4, :].bitcast(I32))
+
+        gn_t = psum.tile([P, P], F32, name="bank")
+        nc.tensor.transpose(gn_t[:], gn_rows[:], ident[:])
+        two_pos = keep.tile([P, 8], F32, name="two_pos")
+        sign = keep.tile([P, 8], F32, name="sign")
+        gn_abs = keep.tile([P, 8], F32, name="gn_abs")
+        root = keep.tile([P, 8], F32, name="root")
+        nc.scalar.activation(gn_abs[:], gn_t[:, 0:8], ACT.Abs)
+        nc.scalar.activation(root[:], gn_abs[:], ACT.Sqrt)
+        nc.vector.tensor_scalar(two_pos[:], gn_t[:, 0:8], 0.0, 2.0, ALU.is_ge, ALU.mult)
+        nc.vector.tensor_scalar_add(sign[:], two_pos[:], -1.0)
+
+        nc.vector.tensor_copy(
+            w_sc[:].rearrange("p w a f -> p (w a f)").bitcast(I32).rearrange("p (x t q e) -> p t x q e", t=4, q=16, e=2),
+            w_sc_raw[:].rearrange("p w a f -> p (w a f)").bitcast(I32).rearrange("p (x q t e) -> p t x q e", t=4, q=16, e=2),
+        )
+
+        load_weight(0, 1, "slot_c")
+
+        def gather_words(jh):
+            pair = keep.tile([P, W], I32, name="pair%d" % jh, tag="slot_p%d" % jh, align_bytes=64)
+            nc.vector.tensor_copy(pair[:].bitcast(U32), tab[:].bitcast(U32).indirect(offsets[:, 32 * jh : 32 * jh + 32]))
+            v = keep.tile([P, PASSES, 2 * W], U8, name="v%d" % jh, align_bytes=64)
+            nc.vector.tensor_copy(v[:].bitcast(U16), pair[:].bitcast(U16).rearrange("p (c d) -> p d c", d=2))
+            return v
+
+        def order_weight(w, g):
+            nc.vector.tensor_copy(
+                w_q[w, g][:].rearrange("p a t (q r) -> p t a q r", r=8),
+                w_raw[w, g][:].rearrange("p a (q t r) -> p t a q r", t=4, r=8),
+            )
+
+        def squares(v, jh, g, split_from):
+            sq = []
+            for w in range(2):
+                sq.append(ring.tile([P, 4, W], F32, name="sq%d" % w, align_bytes=64))
+            later = []
+            for t in range(4):
+                for w in range(2):
+                    bank = psum.tile([P, W], F32, name="bank")
+                    for a in range(PASSES):
+                        c0 = g * W + t * P
+                        nc.tensor.matmul_mx(
+                            out=bank[:],
+                            lhsT=w_q[w, g][:, a, t, :].bitcast(FP8X4),
+                            lhsT_scale=w_sc[:, w, a, c0 : c0 + P],
+                            rhs=v[:, a, :].bitcast(FP4X4),
+                            rhs_scale=v_sc[:, a, jh * W : (jh + 1) * W],
+                            start=(a == 0),
+                            stop=(a == PASSES - 1),
+                        )
+                    u = 4 * g + t
+                    cols = W if t < split_from else W // 2
+                    nc.scalar.activation(sq[w][:, t, 0:cols], bank[:, 0:cols], ACT.Square, scale=root[:, u : u + 1])
+                    if cols < W:
+                        later.append((w, t, u, bank))
+            for w, t, u, bank in later:
+                nc.scalar.activation(sq[w][:, t, W // 2 : W], bank[:, W // 2 : W], ACT.Square, scale=root[:, u : u + 1])
+            return sq
+
+        def power(sq, c0, c1):
+            cols = c1 - c0
+            h = ring.tile([P, cols, 4], BF16, name="h", align_bytes=64)
+            nc.vector.tensor_tensor(
+                h[:].rearrange("p (c i) t -> p c t i", i=2),
+                sq[0][:, :, c0:c1].rearrange("p t (c i) -> p c t i", i=2),
+                sq[1][:, :, c0:c1].rearrange("p t (c i) -> p c t i", i=2),
+                ALU.add,
+            )
+            h_q = ring.tile([P, cols], U32, name="h_q", align_bytes=64, bufs=5)
+            h_sc = ring.tile([P, cols], U8, name="h_sc", align_bytes=64, bufs=5)
+            nc.vector.quantize_mx(out=h_q[:].bitcast(FP8X4), scales=h_sc[:], in_=h[:].rearrange("p c t -> p (c t)"))
+            return h_q, h_sc
+
+        def filters(fb_raw):
+            fb_b = keep.tile([P, GROUPS, N, 4], BF16, name="fb_b", align_bytes=64)
+            for g in range(GROUPS):
+                nc.vector.tensor_tensor(
+                    fb_b[:, g].rearrange("p (c i) t -> p c t i", i=2),
+                    fb_raw[:, g].rearrange("p t (c i) -> p c t i", i=2),
+                    sign[:, 4 * g : 4 * g + 4].unsqueeze(1).unsqueeze(3).broadcast_to([P, N // 2, 4, 2]),
+                    ALU.mult,
+                )
+            fb_q = keep.tile([P, GROUPS, N], U32, name="fb_q", align_bytes=64)
+            fb_sc = keep.tile([P, GROUPS, N], U8, name="fb_sc", align_bytes=64)
+            nc.vector.quantize_mx(
+                out=fb_q[:].rearrange("p g n -> p (g n)").bitcast(FP8X4),
+                scales=fb_sc[:].rearrange("p g n -> p (g n)"),
+                in_=fb_b[:].rearrange("p g n t -> p (g n t)"),
+            )
+            return fb_q, fb_sc
+
+        def gather_level(jh):
+            picked = keep.tile([P, W], F32, name="picked_level%d" % jh)
+            nc.vector.tensor_copy(picked[:], level[:].indirect(offsets[:, 32 * jh : 32 * jh + 32]))
+            return picked
+
+        def finish(jh, c0, c1, hs, fb_q, fb_sc, picked):
+            cols = c1 - c0
+            for nt in range(N // P):
+                bank = psum.tile([P, cols], F32, name="bank")
+                for g in range(GROUPS):
+                    nc.tensor.matmul_mx(
+                        out=bank[:],
+                        lhsT=fb_q[:, g, nt * P : (nt + 1) * P].bitcast(FP8X4),
+                        lhsT_scale=fb_sc[:, g, nt * P : (nt + 1) * P],
+                        rhs=hs[g][0].bitcast(FP8X4),
+                        rhs_scale=hs[g][1],
+                        start=(g == 0),
+                        stop=(g == GROUPS - 1),
+                    )
+                y = ring.tile([P, cols], F32, name="y")
+                nc.vector.tensor_tensor(y[:], bank[:], picked[:, c0:c1], ALU.mult)
+                nc.sync.dma_start(out[nt * P : (nt + 1) * P, jh * W + c0 : jh * W + c1], y[:])
+
+        def cut(h, c0, c1):
+            return h[0][:, c0:c1], h[1][:, c0:c1]
+
+        v0 = gather_words(0)
+        load_weight(1, 1, "slot_p0")
+        order_weight(0, 0)
+        fb_raw = keep.tile([P, GROUPS, 4, N], F32, name="fb_raw", tag="slot_d", align_bytes=64)
+        fb_by_row = fb.rearrange("(g q t r) n -> g r q t n", g=GROUPS, t=4, r=8)
+        for g in range(GROUPS):
+            for r in range(8):
+                nc.sync.dma_start(fb_raw[r:P:8, g, :, :], fb_by_row[g, r])
+        order_weight(1, 0)
+        level = keep.tile([P, T], F32, name="level", tag="slot_e", align_bytes=64)
+        nc.sync.dma_start(level[:], ts)
+        sq00 = squares(v0, 0, 0, 4)
+        v1 = gather_words(1)
+        sq10 = squares(v1, 1, 0, 4)
+        order_weight(0, 1)
+        order_weight(1, 1)
+        sq01 = squares(v0, 0, 1, 4)
+        h00 = power(sq00, 0, W)
+        fb_q, fb_sc = filters(fb_raw)
+        h10 = power(sq10, 0, W)
+        sq11 = squares(v1, 1, 1, 2)
+        level0 = gather_level(0)
+        level1 = gather_level(1)
+        h01 = power(sq01, 0, W)
+        finish(0, 0, W, [cut(h00, 0, W), cut(h01, 0, W)], fb_q, fb_sc, level0)
+        H = W // 2
+        h11a = power(sq11, 0, H)
+        h11b = power(sq11, H, W)
+        finish(1, 0, H, [cut(h10, 0, H), cut(h11a, 0, H)], fb_q, fb_sc, level1)
+        finish(1, H, W, [cut(h10, H, W), cut(h11b, 0, H)], fb_q, fb_sc, level1)

@@ -34,71 +34,74 @@ def tile_list_meltab_gain_kernel(
     with ExitStack() as ctx:
         keep = ctx.enter_context(tc.tile_pool(name="keep", bufs=1))
         ring = ctx.enter_context(tc.tile_pool(name="ring", bufs=4))
+        early = ctx.enter_context(tc.tile_pool(name="early", bufs=1))
         psum = ctx.enter_context(tc.psum_pool(name="psum", bufs=8))
 
         offsets = keep.tile([P, J // 16], U16, name="offsets")
         tab = keep.tile([P, T], I32, name="tab", align_bytes=64)
-        tab_sc = keep.tile([P, T], U8, name="tab_sc", align_bytes=64)
+        tab_sc = early.tile([P, T], U8, name="tab_sc", align_bytes=64, offset=3072)
         picked_sc = keep.tile([P, J], U8, name="picked_sc", tag="slot_c", align_bytes=64)
         v_sc = keep.tile([P, PASSES, J], U8, name="v_sc", align_bytes=64)
-        w_sc_raw = keep.tile([P, 2, PASSES, F], U8, name="w_sc_raw", align_bytes=64)
-        w_sc = keep.tile([P, 2, PASSES, F], U8, name="w_sc", align_bytes=64)
         gn_rows = keep.tile([P, P], F32, name="gn_rows")
         ident = keep.tile([P, P], F32, name="ident")
         w_raw = {}
         w_q = {}
-        for g in range(GROUPS):
-            for w in range(2):
+        w_sc = []
+        for w in range(2):
+            w_sc.append(keep.tile([P, PASSES, F], U8, name="w_sc%d" % w, align_bytes=64))
+            for g in range(GROUPS):
                 w_q[w, g] = keep.tile([P, PASSES, 4, P], I32, name="w_q%d%d" % (w, g), align_bytes=64)
 
-        nc.vector.memset(w_sc_raw[:].rearrange("p w a f -> p (w a f)").bitcast(I32), 0)
-        nc.vector.memset(tab_sc[32:64, :].bitcast(I32), 0)
-        nc.vector.memset(tab_sc[64:128, :].bitcast(I32), 0)
-        nc.vector.memset(v_sc[:].rearrange("p a j -> p (a j)").bitcast(I32), 0)
-        nc.gpsimd.memset(gn_rows[:], 0.0)
+        def load_scales(w, raw, engine, queue):
+            engine.memset(raw[:].rearrange("p a f -> p (a f)").bitcast(I32), 0)
+            rows = w_scales[w].bitcast(I32).rearrange("a (u r) f -> r u a f", r=4)
+            for r in range(4):
+                queue.dma_start(raw[r:P:32, :, :].bitcast(I32), rows[r])
+
+        def load_weight(w, g, raw):
+            w_raw[w, g] = raw
+            words = w_words[w].rearrange("a p f b -> p a (f b)").bitcast(I32)
+            nc.sync.dma_start(raw[:], words[:, :, g * W : (g + 1) * W])
+
+        def order_scales(w, raw):
+            nc.vector.tensor_copy(
+                w_sc[w][:].rearrange("p a f -> p (a f)").bitcast(I32).rearrange("p (x t q e) -> p t x q e", t=4, q=16, e=2),
+                raw[:].rearrange("p a f -> p (a f)").bitcast(I32).rearrange("p (x q t e) -> p t x q e", t=4, q=16, e=2),
+            )
 
         nc.sync.dma_start(offsets[:], offs)
         nc.sync.dma_start(tab_sc[0:32, :].bitcast(I32), tab_scales.rearrange("a q t -> (a q) t").bitcast(I32))
-        nc.sync.dma_start(tab[:], tab_words.rearrange("e p t b -> p (e t b)").bitcast(I32))
-        for w in range(2):
-            rows = w_scales[w].bitcast(I32).rearrange("a (u r) f -> r u a f", r=4)
-            for r in range(4):
-                nc.scalar.dma_start(w_sc_raw[r:P:32, w, :, :].bitcast(I32), rows[r])
+        nc.gpsimd.memset(gn_rows[:], 0.0)
         gn_by_tile = gn.rearrange("(g q t r) -> g t q r", g=GROUPS, t=4, r=8)
         for g in range(GROUPS):
-            nc.gpsimd.dma_start(gn_rows[4 * g : 4 * g + 4, :].rearrange("t (q r) -> t q r", r=8), gn_by_tile[g])
+            nc.sync.dma_start(gn_rows[4 * g : 4 * g + 4, :].rearrange("t (q r) -> t q r", r=8), gn_by_tile[g])
+        nc.sync.dma_start(tab[:], tab_words.rearrange("e p t b -> p (e t b)").bitcast(I32))
+        load_weight(0, 0, keep.tile([P, PASSES, W], I32, name="co_raw0", align_bytes=64))
+        co_sc_raw = keep.tile([P, PASSES, F], U8, name="co_sc_raw", tag="slot_s0", align_bytes=64)
+        load_scales(0, co_sc_raw, nc.vector, nc.scalar)
+        nc.vector.memset(tab_sc[32:64, :].bitcast(I32), 0)
+        nc.vector.memset(tab_sc[64:128, :].bitcast(I32), 0)
+        nc.vector.memset(v_sc[:].rearrange("p a j -> p (a j)").bitcast(I32), 0)
         make_identity(nc, ident[:])
-
-        def load_weight(w, g, tag):
-            w_raw[w, g] = keep.tile([P, PASSES, W], I32, name="w_raw%d%d" % (w, g), tag=tag, align_bytes=64)
-            words = w_words[w].rearrange("a p f b -> p a (f b)").bitcast(I32)
-            nc.sync.dma_start(w_raw[w, g][:], words[:, :, g * W : (g + 1) * W])
-
-        load_weight(0, 0, "slot_d")
-        load_weight(1, 0, "slot_e")
 
         nc.vector.tensor_copy(picked_sc[:], tab_sc[:].indirect(offsets[:]))
         for a in range(PASSES):
             for r in range(4):
-                nc.scalar.dma_start(v_sc[r:P:32, a, :].bitcast(I32), picked_sc[16 * a + r : 16 * a + 16 : 4, :].bitcast(I32))
+                nc.sync.dma_start(v_sc[r:P:32, a, :].bitcast(I32), picked_sc[16 * a + r : 16 * a + 16 : 4, :].bitcast(I32))
+        si_sc_raw = early.tile([P, PASSES, F], U8, name="si_sc_raw", align_bytes=64, offset=4096)
+        load_scales(1, si_sc_raw, nc.gpsimd, nc.sync)
+        load_weight(1, 0, early.tile([P, PASSES, W], I32, name="si_raw0", align_bytes=64, offset=6144))
 
         gn_t = psum.tile([P, P], F32, name="bank")
         nc.tensor.transpose(gn_t[:], gn_rows[:], ident[:])
+        gn_p = keep.tile([P, 8], F32, name="gn_p")
         two_pos = keep.tile([P, 8], F32, name="two_pos")
         sign = keep.tile([P, 8], F32, name="sign")
         gn_abs = keep.tile([P, 8], F32, name="gn_abs")
         root = keep.tile([P, 8], F32, name="root")
         nc.scalar.activation(gn_abs[:], gn_t[:, 0:8], ACT.Abs)
+        nc.scalar.copy(gn_p[:], gn_t[:, 0:8])
         nc.scalar.activation(root[:], gn_abs[:], ACT.Sqrt)
-        nc.vector.tensor_scalar(two_pos[:], gn_t[:, 0:8], 0.0, 2.0, ALU.is_ge, ALU.mult)
-        nc.vector.tensor_scalar_add(sign[:], two_pos[:], -1.0)
-
-        nc.vector.tensor_copy(
-            w_sc[:].rearrange("p w a f -> p (w a f)").bitcast(I32).rearrange("p (x t q e) -> p t x q e", t=4, q=16, e=2),
-            w_sc_raw[:].rearrange("p w a f -> p (w a f)").bitcast(I32).rearrange("p (x q t e) -> p t x q e", t=4, q=16, e=2),
-        )
-
-        load_weight(0, 1, "slot_c")
 
         def gather_words(jh):
             pair = keep.tile([P, W], I32, name="pair%d" % jh, tag="slot_p%d" % jh, align_bytes=64)
@@ -113,20 +116,20 @@ def tile_list_meltab_gain_kernel(
                 w_raw[w, g][:].rearrange("p a (q t r) -> p t a q r", t=4, r=8),
             )
 
-        def squares(v, jh, g, split_from):
+        def squares(v, jh, g, split_from, order):
             sq = []
             for w in range(2):
                 sq.append(ring.tile([P, 4, W], F32, name="sq%d" % w, align_bytes=64))
             later = []
-            for t in range(4):
-                for w in range(2):
+            for t, w in order:
+                if True:
                     bank = psum.tile([P, W], F32, name="bank")
                     for a in range(PASSES):
                         c0 = g * W + t * P
                         nc.tensor.matmul_mx(
                             out=bank[:],
                             lhsT=w_q[w, g][:, a, t, :].bitcast(FP8X4),
-                            lhsT_scale=w_sc[:, w, a, c0 : c0 + P],
+                            lhsT_scale=w_sc[w][:, a, c0 : c0 + P],
                             rhs=v[:, a, :].bitcast(FP4X4),
                             rhs_scale=v_sc[:, a, jh * W : (jh + 1) * W],
                             start=(a == 0),
@@ -156,6 +159,8 @@ def tile_list_meltab_gain_kernel(
             return h_q, h_sc
 
         def filters(fb_raw):
+            nc.vector.tensor_scalar(two_pos[:], gn_p[:], 0.0, 2.0, ALU.is_ge, ALU.mult)
+            nc.vector.tensor_scalar_add(sign[:], two_pos[:], -1.0)
             fb_b = keep.tile([P, GROUPS, N, 4], BF16, name="fb_b", align_bytes=64)
             for g in range(GROUPS):
                 nc.vector.tensor_tensor(
@@ -172,11 +177,6 @@ def tile_list_meltab_gain_kernel(
                 in_=fb_b[:].rearrange("p g n t -> p (g n t)"),
             )
             return fb_q, fb_sc
-
-        def gather_level(jh):
-            picked = keep.tile([P, W], F32, name="picked_level%d" % jh)
-            nc.vector.tensor_copy(picked[:], level[:].indirect(offsets[:, 32 * jh : 32 * jh + 32]))
-            return picked
 
         def finish(jh, c0, c1, hs, fb_q, fb_sc, picked):
             cols = c1 - c0
@@ -199,33 +199,39 @@ def tile_list_meltab_gain_kernel(
         def cut(h, c0, c1):
             return h[0][:, c0:c1], h[1][:, c0:c1]
 
+        co_first = [(t, w) for w in range(2) for t in range(4)]
+        by_tile = [(t, w) for t in range(4) for w in range(2)]
+        order_scales(0, co_sc_raw)
+        load_weight(0, 1, keep.tile([P, PASSES, W], I32, name="co_raw1", tag="slot_s0", align_bytes=64))
         v0 = gather_words(0)
-        load_weight(1, 1, "slot_p0")
         order_weight(0, 0)
-        fb_raw = keep.tile([P, GROUPS, 4, N], F32, name="fb_raw", tag="slot_d", align_bytes=64)
-        fb_by_row = fb.rearrange("(g q t r) n -> g r q t n", g=GROUPS, t=4, r=8)
-        for g in range(GROUPS):
-            for r in range(8):
-                nc.sync.dma_start(fb_raw[r:P:8, g, :, :], fb_by_row[g, r])
+        order_scales(1, si_sc_raw)
         order_weight(1, 0)
-        level = keep.tile([P, T], F32, name="level", tag="slot_e", align_bytes=64)
+        load_weight(1, 1, keep.tile([P, PASSES, W], I32, name="si_raw1", tag="slot_c", align_bytes=64))
+        fb_raw = keep.tile([P, GROUPS, 4, N], F32, name="fb_raw", tag="slot_p0", align_bytes=64)
+        fb_by_slot = fb.rearrange("(g q t r) n -> g t q r n", g=GROUPS, t=4, r=8)
+        for g in range(GROUPS):
+            for t in range(4):
+                nc.sync.dma_start(fb_raw[:, g, t, :], fb_by_slot[g, t])
+        level = early.tile([P, T], F32, name="level", align_bytes=64, offset=0)
         nc.sync.dma_start(level[:], ts)
-        sq00 = squares(v0, 0, 0, 4)
+        sq00 = squares(v0, 0, 0, 4, co_first)
         v1 = gather_words(1)
-        sq10 = squares(v1, 1, 0, 4)
+        sq10 = squares(v1, 1, 0, 4, by_tile)
         order_weight(0, 1)
         order_weight(1, 1)
-        sq01 = squares(v0, 0, 1, 4)
+        sq01 = squares(v0, 0, 1, 4, by_tile)
         h00 = power(sq00, 0, W)
         fb_q, fb_sc = filters(fb_raw)
         h10 = power(sq10, 0, W)
-        sq11 = squares(v1, 1, 1, 2)
-        level0 = gather_level(0)
-        level1 = gather_level(1)
+        sq11 = squares(v1, 1, 1, 2, by_tile)
+        picked_level = keep.tile([P, J], F32, name="picked_level")
+        nc.vector.tensor_copy(picked_level[:], level[:].indirect(offsets[:]))
+        level0, level1 = picked_level[:, 0:W], picked_level[:, W:J]
         h01 = power(sq01, 0, W)
-        finish(0, 0, W, [cut(h00, 0, W), cut(h01, 0, W)], fb_q, fb_sc, level0)
         H = W // 2
         h11a = power(sq11, 0, H)
+        finish(0, 0, W, [cut(h00, 0, W), cut(h01, 0, W)], fb_q, fb_sc, level0)
         h11b = power(sq11, H, W)
         finish(1, 0, H, [cut(h10, 0, H), cut(h11a, 0, H)], fb_q, fb_sc, level1)
         finish(1, H, W, [cut(h10, H, W), cut(h11b, 0, H)], fb_q, fb_sc, level1)

@@ -106,6 +106,9 @@ def tile_list_meltab_gain_kernel(
         def gather_words(jh):
             pair = keep.tile([P, W], I32, name="pair%d" % jh, tag="slot_p%d" % jh, align_bytes=64)
             nc.vector.tensor_copy(pair[:].bitcast(U32), tab[:].bitcast(U32).indirect(offsets[:, 32 * jh : 32 * jh + 32]))
+            return pair
+
+        def part_words(jh, pair):
             v = keep.tile([P, PASSES, 2 * W], U8, name="v%d" % jh, align_bytes=64)
             nc.vector.tensor_copy(v[:].bitcast(U16), pair[:].bitcast(U16).rearrange("p (c d) -> p d c", d=2))
             return v
@@ -144,15 +147,20 @@ def tile_list_meltab_gain_kernel(
                 nc.scalar.activation(sq[w][:, t, W // 2 : W], bank[:, W // 2 : W], ACT.Square, scale=root[:, u : u + 1])
             return sq
 
-        def power(sq, c0, c1):
+        def power(sq, c0, c1, h=None):
             cols = c1 - c0
-            h = ring.tile([P, cols, 4], BF16, name="h", align_bytes=64)
+            if h is None:
+                h = ring.tile([P, cols, 4], BF16, name="h", align_bytes=64)
             nc.vector.tensor_tensor(
                 h[:].rearrange("p (c i) t -> p c t i", i=2),
                 sq[0][:, :, c0:c1].rearrange("p t (c i) -> p c t i", i=2),
                 sq[1][:, :, c0:c1].rearrange("p t (c i) -> p c t i", i=2),
                 ALU.add,
             )
+            return h
+
+        def quantize(h):
+            cols = h.shape[1]
             h_q = ring.tile([P, cols], U32, name="h_q", align_bytes=64, bufs=5)
             h_sc = ring.tile([P, cols], U8, name="h_sc", align_bytes=64, bufs=5)
             nc.vector.quantize_mx(out=h_q[:].bitcast(FP8X4), scales=h_sc[:], in_=h[:].rearrange("p c t -> p (c t)"))
@@ -201,37 +209,45 @@ def tile_list_meltab_gain_kernel(
 
         co_first = [(t, w) for w in range(2) for t in range(4)]
         by_tile = [(t, w) for t in range(4) for w in range(2)]
+        H = W // 2
+        pair0 = gather_words(0)
         order_scales(0, co_sc_raw)
-        load_weight(0, 1, keep.tile([P, PASSES, W], I32, name="co_raw1", tag="slot_s0", align_bytes=64))
-        v0 = gather_words(0)
-        order_weight(0, 0)
-        order_scales(1, si_sc_raw)
-        order_weight(1, 0)
-        load_weight(1, 1, keep.tile([P, PASSES, W], I32, name="si_raw1", tag="slot_c", align_bytes=64))
-        fb_raw = keep.tile([P, GROUPS, 4, N], F32, name="fb_raw", tag="slot_p0", align_bytes=64)
+        fb_raw = keep.tile([P, GROUPS, 4, N], F32, name="fb_raw", tag="slot_s0", align_bytes=64)
         fb_by_slot = fb.rearrange("(g q t r) n -> g t q r n", g=GROUPS, t=4, r=8)
         for g in range(GROUPS):
             for t in range(4):
                 nc.sync.dma_start(fb_raw[:, g, t, :], fb_by_slot[g, t])
+        v0 = part_words(0, pair0)
+        order_weight(0, 0)
+        pair1 = gather_words(1)
+        order_scales(1, si_sc_raw)
+        order_weight(1, 0)
+        v1 = part_words(1, pair1)
+        load_weight(0, 1, keep.tile([P, PASSES, W], I32, name="co_raw1", tag="slot_p0", align_bytes=64))
+        load_weight(1, 1, keep.tile([P, PASSES, W], I32, name="si_raw1", tag="slot_c", align_bytes=64))
         level = early.tile([P, T], F32, name="level", align_bytes=64, offset=0)
         nc.sync.dma_start(level[:], ts)
         sq00 = squares(v0, 0, 0, 4, co_first)
-        v1 = gather_words(1)
         sq10 = squares(v1, 1, 0, 4, by_tile)
+        fb_q, fb_sc = filters(fb_raw)
         order_weight(0, 1)
+        sum00 = power(sq00, 0, W, keep.tile([P, W, 4], BF16, name="h_first", tag="slot_s0", align_bytes=64))
         order_weight(1, 1)
         sq01 = squares(v0, 0, 1, 4, by_tile)
-        h00 = power(sq00, 0, W)
-        fb_q, fb_sc = filters(fb_raw)
-        h10 = power(sq10, 0, W)
-        sq11 = squares(v1, 1, 1, 2, by_tile)
+        h00 = quantize(sum00)
         picked_level = keep.tile([P, J], F32, name="picked_level")
-        nc.vector.tensor_copy(picked_level[:], level[:].indirect(offsets[:]))
         level0, level1 = picked_level[:, 0:W], picked_level[:, W:J]
-        h01 = power(sq01, 0, W)
-        H = W // 2
-        h11a = power(sq11, 0, H)
+        sum10 = power(sq10, 0, W)
+        nc.vector.tensor_copy(level0, level[:].indirect(offsets[:, 0:32]))
+        h10 = quantize(sum10)
+        sq11 = squares(v1, 1, 1, 2, by_tile)
+        sum01 = power(sq01, 0, W)
+        nc.vector.tensor_copy(level1, level[:].indirect(offsets[:, 32:64]))
+        h01 = quantize(sum01)
+        sum11a = power(sq11, 0, H)
         finish(0, 0, W, [cut(h00, 0, W), cut(h01, 0, W)], fb_q, fb_sc, level0)
-        h11b = power(sq11, H, W)
+        h11a = quantize(sum11a)
+        sum11b = power(sq11, H, W)
         finish(1, 0, H, [cut(h10, 0, H), cut(h11a, 0, H)], fb_q, fb_sc, level1)
+        h11b = quantize(sum11b)
         finish(1, H, W, [cut(h10, H, W), cut(h11b, 0, H)], fb_q, fb_sc, level1)

@@ -35,22 +35,19 @@ def tile_list_meltab_gain_kernel(
         keep = ctx.enter_context(tc.tile_pool(name="keep", bufs=1))
         ring = ctx.enter_context(tc.tile_pool(name="ring", bufs=4))
         early = ctx.enter_context(tc.tile_pool(name="early", bufs=1))
+        chain = ctx.enter_context(tc.tile_pool(name="chain", bufs=1))
         psum = ctx.enter_context(tc.psum_pool(name="psum", bufs=8))
 
         offsets = keep.tile([P, J // 16], U16, name="offsets")
         tab = keep.tile([P, T], I32, name="tab", align_bytes=64)
         tab_sc = early.tile([P, T], U8, name="tab_sc", align_bytes=64, offset=3072)
-        picked_sc = keep.tile([P, J], U8, name="picked_sc", tag="slot_c", align_bytes=64)
+        picked_sc = chain.tile([P, J], U8, name="picked_sc", align_bytes=64, offset=19968)
         v_sc = keep.tile([P, PASSES, J], U8, name="v_sc", align_bytes=64)
         gn_rows = keep.tile([P, P], F32, name="gn_rows")
         ident = keep.tile([P, P], F32, name="ident")
         w_raw = {}
         w_q = {}
-        w_sc = []
-        for w in range(2):
-            w_sc.append(keep.tile([P, PASSES, F], U8, name="w_sc%d" % w, align_bytes=64))
-            for g in range(GROUPS):
-                w_q[w, g] = keep.tile([P, PASSES, 4, P], I32, name="w_q%d%d" % (w, g), align_bytes=64)
+        w_sc = {}
 
         def load_scales(w, raw, engine, queue):
             engine.memset(raw[:].rearrange("p a f -> p (a f)").bitcast(I32), 0)
@@ -64,33 +61,33 @@ def tile_list_meltab_gain_kernel(
             nc.sync.dma_start(raw[:], words[:, :, g * W : (g + 1) * W])
 
         def order_scales(w, raw):
+            w_sc[w] = chain.tile([P, PASSES, F], U8, name="w_sc%d" % w, align_bytes=64, offset=8192 * w + 4096)
             nc.vector.tensor_copy(
                 w_sc[w][:].rearrange("p a f -> p (a f)").bitcast(I32).rearrange("p (x t q e) -> p t x q e", t=4, q=16, e=2),
                 raw[:].rearrange("p a f -> p (a f)").bitcast(I32).rearrange("p (x q t e) -> p t x q e", t=4, q=16, e=2),
             )
 
-        nc.sync.dma_start(offsets[:], offs)
-        nc.sync.dma_start(tab_sc[0:32, :].bitcast(I32), tab_scales.rearrange("a q t -> (a q) t").bitcast(I32))
+        nc.vector.memset(tab_sc[0:96, :].bitcast(I32), 0)
+        co_sc_raw = keep.tile([P, PASSES, F], U8, name="co_sc_raw", tag="slot_s0", align_bytes=64)
         nc.gpsimd.memset(gn_rows[:], 0.0)
+        load_scales(0, co_sc_raw, nc.gpsimd, nc.scalar)
+        si_sc_raw = early.tile([P, PASSES, F], U8, name="si_sc_raw", align_bytes=64, offset=12288)
+        load_scales(1, si_sc_raw, nc.gpsimd, nc.scalar)
+        nc.sync.dma_start(offsets[:], offs)
+        nc.sync.dma_start(tab_sc[96:P, :].bitcast(I32), tab_scales.rearrange("a q t -> (a q) t").bitcast(I32))
         gn_by_tile = gn.rearrange("(g q t r) -> g t q r", g=GROUPS, t=4, r=8)
         for g in range(GROUPS):
             nc.sync.dma_start(gn_rows[4 * g : 4 * g + 4, :].rearrange("t (q r) -> t q r", r=8), gn_by_tile[g])
         nc.sync.dma_start(tab[:], tab_words.rearrange("e p t b -> p (e t b)").bitcast(I32))
-        load_weight(0, 0, keep.tile([P, PASSES, W], I32, name="co_raw0", align_bytes=64))
-        co_sc_raw = keep.tile([P, PASSES, F], U8, name="co_sc_raw", tag="slot_s0", align_bytes=64)
-        load_scales(0, co_sc_raw, nc.vector, nc.scalar)
-        nc.vector.memset(tab_sc[32:64, :].bitcast(I32), 0)
-        nc.vector.memset(tab_sc[64:128, :].bitcast(I32), 0)
-        nc.vector.memset(v_sc[:].rearrange("p a j -> p (a j)").bitcast(I32), 0)
+        load_weight(0, 0, chain.tile([P, PASSES, W], I32, name="co_raw0", align_bytes=64, offset=10240))
+        load_weight(1, 0, early.tile([P, PASSES, W], I32, name="si_raw0", align_bytes=64, offset=8192))
         make_identity(nc, ident[:])
+        nc.gpsimd.memset(v_sc[:].rearrange("p a j -> p (a j)").bitcast(I32), 0)
 
         nc.vector.tensor_copy(picked_sc[:], tab_sc[:].indirect(offsets[:]))
         for a in range(PASSES):
             for r in range(4):
-                nc.sync.dma_start(v_sc[r:P:32, a, :].bitcast(I32), picked_sc[16 * a + r : 16 * a + 16 : 4, :].bitcast(I32))
-        si_sc_raw = early.tile([P, PASSES, F], U8, name="si_sc_raw", align_bytes=64, offset=4096)
-        load_scales(1, si_sc_raw, nc.gpsimd, nc.sync)
-        load_weight(1, 0, early.tile([P, PASSES, W], I32, name="si_raw0", align_bytes=64, offset=6144))
+                nc.sync.dma_start(v_sc[r:P:32, a, :].bitcast(I32), picked_sc[96 + 16 * a + r : 96 + 16 * a + 16 : 4, :].bitcast(I32))
 
         gn_t = psum.tile([P, P], F32, name="bank")
         nc.tensor.transpose(gn_t[:], gn_rows[:], ident[:])
@@ -103,8 +100,7 @@ def tile_list_meltab_gain_kernel(
         nc.scalar.copy(gn_p[:], gn_t[:, 0:8])
         nc.scalar.activation(root[:], gn_abs[:], ACT.Sqrt)
 
-        def gather_words(jh):
-            pair = keep.tile([P, W], I32, name="pair%d" % jh, tag="slot_p%d" % jh, align_bytes=64)
+        def gather_words(jh, pair):
             nc.vector.tensor_copy(pair[:].bitcast(U32), tab[:].bitcast(U32).indirect(offsets[:, 32 * jh : 32 * jh + 32]))
             return pair
 
@@ -114,6 +110,10 @@ def tile_list_meltab_gain_kernel(
             return v
 
         def order_weight(w, g):
+            if g == 0:
+                w_q[w, g] = chain.tile([P, PASSES, 4, P], I32, name="w_q%d%d" % (w, g), align_bytes=64, offset=8192 * w)
+            else:
+                w_q[w, g] = keep.tile([P, PASSES, 4, P], I32, name="w_q%d%d" % (w, g), align_bytes=64)
             nc.vector.tensor_copy(
                 w_q[w, g][:].rearrange("p a t (q r) -> p t a q r", r=8),
                 w_raw[w, g][:].rearrange("p a (q t r) -> p t a q r", t=4, r=8),
@@ -210,21 +210,21 @@ def tile_list_meltab_gain_kernel(
         co_first = [(t, w) for w in range(2) for t in range(4)]
         by_tile = [(t, w) for t in range(4) for w in range(2)]
         H = W // 2
-        pair0 = gather_words(0)
+        pair0 = gather_words(0, chain.tile([P, W], I32, name="pair0", align_bytes=64, offset=3072))
+        v0 = part_words(0, pair0)
         order_scales(0, co_sc_raw)
         fb_raw = keep.tile([P, GROUPS, 4, N], F32, name="fb_raw", tag="slot_s0", align_bytes=64)
         fb_by_slot = fb.rearrange("(g q t r) n -> g t q r n", g=GROUPS, t=4, r=8)
         for g in range(GROUPS):
             for t in range(4):
                 nc.sync.dma_start(fb_raw[:, g, t, :], fb_by_slot[g, t])
-        v0 = part_words(0, pair0)
         order_weight(0, 0)
-        pair1 = gather_words(1)
+        pair1 = gather_words(1, keep.tile([P, W], I32, name="pair1", align_bytes=64))
         order_scales(1, si_sc_raw)
         order_weight(1, 0)
         v1 = part_words(1, pair1)
-        load_weight(0, 1, keep.tile([P, PASSES, W], I32, name="co_raw1", tag="slot_p0", align_bytes=64))
-        load_weight(1, 1, keep.tile([P, PASSES, W], I32, name="si_raw1", tag="slot_c", align_bytes=64))
+        load_weight(0, 1, chain.tile([P, PASSES, W], I32, name="co_raw1", align_bytes=64, offset=16384))
+        load_weight(1, 1, chain.tile([P, PASSES, W], I32, name="si_raw1", align_bytes=64, offset=20480))
         level = early.tile([P, T], F32, name="level", align_bytes=64, offset=0)
         nc.sync.dma_start(level[:], ts)
         sq00 = squares(v0, 0, 0, 4, co_first)

@@ -34,110 +34,115 @@ def tile_list_meltab_gain_kernel(
     with ExitStack() as ctx:
         keep = ctx.enter_context(tc.tile_pool(name="keep", bufs=1))
         ring = ctx.enter_context(tc.tile_pool(name="ring", bufs=4))
-        early = ctx.enter_context(tc.tile_pool(name="early", bufs=1))
         chain = ctx.enter_context(tc.tile_pool(name="chain", bufs=1))
         psum = ctx.enter_context(tc.psum_pool(name="psum", bufs=8))
 
         offsets = keep.tile([P, J // 16], U16, name="offsets")
         tab = keep.tile([P, T], I32, name="tab", align_bytes=64)
-        tab_sc = early.tile([P, T], U8, name="tab_sc", align_bytes=64, offset=3072)
-        picked_sc = chain.tile([P, J], U8, name="picked_sc", align_bytes=64, offset=19968)
-        v_sc = keep.tile([P, PASSES, J], U8, name="v_sc", align_bytes=64)
-        gn_rows = keep.tile([P, P], F32, name="gn_rows")
+        tab_sc = keep.tile([P, T], U8, name="tab_sc", align_bytes=64)
+        w_sc_raw = keep.tile([P, 2 * F], U8, name="w_sc_raw", align_bytes=64)
+        joined = chain.tile([P, J + 2 * F], U8, name="joined", align_bytes=64, offset=32768)
+        planes = [keep.tile([P, J + 2 * F], U8, name="plane%d" % a, align_bytes=64) for a in range(PASSES)]
+        picked_sc = chain.tile([P, J], U8, name="picked_sc", align_bytes=64, offset=0)
+        gn_rows = keep.tile([P, GROUPS, P], F32, name="gn_rows")
         ident = keep.tile([P, P], F32, name="ident")
         w_raw = {}
         w_q = {}
-        w_sc = {}
 
-        def load_scales(w, raw, engine, queue):
-            engine.memset(raw[:].rearrange("p a f -> p (a f)").bitcast(I32), 0)
-            rows = w_scales[w].bitcast(I32).rearrange("a (u r) f -> r u a f", r=4)
-            for r in range(4):
-                queue.dma_start(raw[r:P:32, :, :].bitcast(I32), rows[r])
-
-        def load_weight(w, g, raw):
+        def load_weight(w, g, offset):
+            raw = chain.tile([P, PASSES, W], I32, name="w_raw%d%d" % (w, g), align_bytes=64, offset=offset)
             w_raw[w, g] = raw
             words = w_words[w].rearrange("a p f b -> p a (f b)").bitcast(I32)
             nc.sync.dma_start(raw[:], words[:, :, g * W : (g + 1) * W])
 
-        def order_scales(w, raw):
-            w_sc[w] = chain.tile([P, PASSES, F], U8, name="w_sc%d" % w, align_bytes=64, offset=8192 * w + 4096)
-            nc.vector.tensor_copy(
-                w_sc[w][:].rearrange("p a f -> p (a f)").bitcast(I32).rearrange("p (x t q e) -> p t x q e", t=4, q=16, e=2),
-                raw[:].rearrange("p a f -> p (a f)").bitcast(I32).rearrange("p (x q t e) -> p t x q e", t=4, q=16, e=2),
-            )
-
-        nc.vector.memset(tab_sc[0:96, :].bitcast(I32), 0)
-        co_sc_raw = keep.tile([P, PASSES, F], U8, name="co_sc_raw", tag="slot_s0", align_bytes=64)
         nc.gpsimd.memset(gn_rows[:], 0.0)
-        load_scales(0, co_sc_raw, nc.gpsimd, nc.scalar)
-        si_sc_raw = early.tile([P, PASSES, F], U8, name="si_sc_raw", align_bytes=64, offset=12288)
-        load_scales(1, si_sc_raw, nc.gpsimd, nc.scalar)
-        nc.sync.dma_start(offsets[:], offs)
+        nc.vector.memset(tab_sc[0:96, :].bitcast(I32), 0)
+        nc.sync.dma_start(
+            gn_rows[0:4].rearrange("t g (q r) -> t (g q) r", r=8), gn.rearrange("(x t r) -> t x r", t=4, r=8)
+        )
         nc.sync.dma_start(tab_sc[96:P, :].bitcast(I32), tab_scales.rearrange("a q t -> (a q) t").bitcast(I32))
-        gn_by_tile = gn.rearrange("(g q t r) -> g t q r", g=GROUPS, t=4, r=8)
-        for g in range(GROUPS):
-            nc.sync.dma_start(gn_rows[4 * g : 4 * g + 4, :].rearrange("t (q r) -> t q r", r=8), gn_by_tile[g])
+        nc.sync.dma_start(offsets[:], offs)
         nc.sync.dma_start(tab[:], tab_words.rearrange("e p t b -> p (e t b)").bitcast(I32))
-        load_weight(0, 0, chain.tile([P, PASSES, W], I32, name="co_raw0", align_bytes=64, offset=10240))
-        load_weight(1, 0, early.tile([P, PASSES, W], I32, name="si_raw0", align_bytes=64, offset=8192))
+        load_weight(0, 0, 12288)
+        load_weight(1, 0, 16384)
+        for w in range(2):
+            nc.scalar.dma_start(
+                w_sc_raw[96:P, w * F : (w + 1) * F].bitcast(I32), w_scales[w].rearrange("a q f -> (a q) f").bitcast(I32)
+            )
+        warm = keep.tile([P, 1], F32, name="warm")
+        zero = keep.tile([P, 1], F32, name="zero")
+        nc.gpsimd.memset(zero[:], 0.0)
+        nc.scalar.activation(warm[:], zero[:], ACT.Sqrt)
         make_identity(nc, ident[:])
-        nc.gpsimd.memset(v_sc[:].rearrange("p a j -> p (a j)").bitcast(I32), 0)
+        for a in range(PASSES):
+            nc.vector.memset(planes[a][:].bitcast(I32), 0)
+
+        gn_t = psum.tile([P, GROUPS, P], F32, name="bank")
+        for g in range(GROUPS):
+            nc.tensor.transpose(gn_t[:, g, :], gn_rows[:, g, :], ident[:])
+        gn_p = keep.tile([P, GROUPS, 4], F32, name="gn_p")
+        two_pos = keep.tile([P, GROUPS, 4], F32, name="two_pos")
+        sign = keep.tile([P, GROUPS, 4], F32, name="sign")
+        gn_abs = keep.tile([P, GROUPS, 4], F32, name="gn_abs")
+        root = keep.tile([P, 8], F32, name="root")
+        nc.scalar.activation(gn_abs[:], gn_t[:, :, 0:4], ACT.Abs)
+        nc.scalar.copy(gn_p[:], gn_t[:, :, 0:4])
+        nc.scalar.activation(root[:], gn_abs[:].rearrange("p g t -> p (g t)"), ACT.Sqrt)
 
         nc.vector.tensor_copy(picked_sc[:], tab_sc[:].indirect(offsets[:]))
+        nc.vector.tensor_copy(
+            joined[96:P, J:].bitcast(I32).rearrange("p (x t q e) -> p t x q e", t=4, q=16, e=2),
+            w_sc_raw[96:P, :].bitcast(I32).rearrange("p (x q t e) -> p t x q e", t=4, q=16, e=2),
+        )
+        nc.vector.tensor_copy(joined[96:P, 0:J].bitcast(I32), picked_sc[96:P, :].bitcast(I32))
         for a in range(PASSES):
             for r in range(4):
-                nc.sync.dma_start(v_sc[r:P:32, a, :].bitcast(I32), picked_sc[96 + 16 * a + r : 96 + 16 * a + 16 : 4, :].bitcast(I32))
-
-        gn_t = psum.tile([P, P], F32, name="bank")
-        nc.tensor.transpose(gn_t[:], gn_rows[:], ident[:])
-        gn_p = keep.tile([P, 8], F32, name="gn_p")
-        two_pos = keep.tile([P, 8], F32, name="two_pos")
-        sign = keep.tile([P, 8], F32, name="sign")
-        gn_abs = keep.tile([P, 8], F32, name="gn_abs")
-        root = keep.tile([P, 8], F32, name="root")
-        nc.scalar.activation(gn_abs[:], gn_t[:, 0:8], ACT.Abs)
-        nc.scalar.copy(gn_p[:], gn_t[:, 0:8])
-        nc.scalar.activation(root[:], gn_abs[:], ACT.Sqrt)
+                nc.scalar.dma_start(planes[a][r:P:32, :].bitcast(I32), joined[96 + 16 * a + r : 96 + 16 * a + 16 : 4, :].bitcast(I32))
 
         def gather_words(jh, pair):
             nc.vector.tensor_copy(pair[:].bitcast(U32), tab[:].bitcast(U32).indirect(offsets[:, 32 * jh : 32 * jh + 32]))
             return pair
 
-        def part_words(jh, pair):
-            v = keep.tile([P, PASSES, 2 * W], U8, name="v%d" % jh, align_bytes=64)
-            nc.vector.tensor_copy(v[:].bitcast(U16), pair[:].bitcast(U16).rearrange("p (c d) -> p d c", d=2))
-            return v
+        v = {}
 
-        def order_weight(w, g):
-            if g == 0:
-                w_q[w, g] = chain.tile([P, PASSES, 4, P], I32, name="w_q%d%d" % (w, g), align_bytes=64, offset=8192 * w)
-            else:
-                w_q[w, g] = keep.tile([P, PASSES, 4, P], I32, name="w_q%d%d" % (w, g), align_bytes=64)
+        def part_words(jh, pair, passes):
+            tile = keep.tile([P, len(passes), 2 * W], U8, name="v%d%d" % (jh, passes[0]), align_bytes=64)
+            halves = pair[:].bitcast(U16).rearrange("p (c d) -> p d c", d=2)
+            nc.vector.tensor_copy(tile[:].bitcast(U16), halves[:, passes[0] : passes[-1] + 1, :])
+            for i, a in enumerate(passes):
+                v[jh, a] = tile[:, i, :]
+
+        def order_weight(w, g, passes, tile=None):
+            if tile is None:
+                tile = keep.tile([P, len(passes), 4, P], I32, name="w_q%d%d%d" % (w, g, passes[0]), align_bytes=64)
             nc.vector.tensor_copy(
-                w_q[w, g][:].rearrange("p a t (q r) -> p t a q r", r=8),
-                w_raw[w, g][:].rearrange("p a (q t r) -> p t a q r", t=4, r=8),
+                tile[:].rearrange("p a t (q r) -> p t a q r", r=8),
+                w_raw[w, g][:, passes[0] : passes[-1] + 1, :].rearrange("p a (q t r) -> p t a q r", t=4, r=8),
             )
+            for i, a in enumerate(passes):
+                w_q[w, g, a] = tile[:, i]
 
-        def squares(v, jh, g, split_from, order):
+        def squares(jh, g, split_from, order):
             sq = []
             for w in range(2):
                 sq.append(ring.tile([P, 4, W], F32, name="sq%d" % w, align_bytes=64))
             later = []
-            for t, w in order:
-                if True:
-                    bank = psum.tile([P, W], F32, name="bank")
-                    for a in range(PASSES):
-                        c0 = g * W + t * P
-                        nc.tensor.matmul_mx(
-                            out=bank[:],
-                            lhsT=w_q[w, g][:, a, t, :].bitcast(FP8X4),
-                            lhsT_scale=w_sc[w][:, a, c0 : c0 + P],
-                            rhs=v[:, a, :].bitcast(FP4X4),
-                            rhs_scale=v_sc[:, a, jh * W : (jh + 1) * W],
-                            start=(a == 0),
-                            stop=(a == PASSES - 1),
-                        )
+            banks = {}
+            for t, w, a in order:
+                if a == 0:
+                    banks[t, w] = psum.tile([P, W], F32, name="bank")
+                bank = banks[t, w]
+                c0 = J + w * F + g * W + t * P
+                nc.tensor.matmul_mx(
+                    out=bank[:],
+                    lhsT=w_q[w, g, a][:, t, :].bitcast(FP8X4),
+                    lhsT_scale=planes[a][:, c0 : c0 + P],
+                    rhs=v[jh, a].bitcast(FP4X4),
+                    rhs_scale=planes[a][:, jh * W : (jh + 1) * W],
+                    start=(a == 0),
+                    stop=(a == PASSES - 1),
+                )
+                if a == PASSES - 1:
                     u = 4 * g + t
                     cols = W if t < split_from else W // 2
                     nc.scalar.activation(sq[w][:, t, 0:cols], bank[:, 0:cols], ACT.Square, scale=root[:, u : u + 1])
@@ -174,7 +179,7 @@ def tile_list_meltab_gain_kernel(
                 nc.vector.tensor_tensor(
                     fb_b[:, g].rearrange("p (c i) t -> p c t i", i=2),
                     fb_raw[:, g].rearrange("p t (c i) -> p c t i", i=2),
-                    sign[:, 4 * g : 4 * g + 4].unsqueeze(1).unsqueeze(3).broadcast_to([P, N // 2, 4, 2]),
+                    sign[:, g, :].unsqueeze(1).unsqueeze(3).broadcast_to([P, N // 2, 4, 2]),
                     ALU.mult,
                 )
             fb_q = keep.tile([P, GROUPS, N], U32, name="fb_q", align_bytes=64)
@@ -207,42 +212,42 @@ def tile_list_meltab_gain_kernel(
         def cut(h, c0, c1):
             return h[0][:, c0:c1], h[1][:, c0:c1]
 
-        co_first = [(t, w) for w in range(2) for t in range(4)]
-        by_tile = [(t, w) for t in range(4) for w in range(2)]
+        first_unit = [(t, 0, a) for a in range(PASSES) for t in range(4)] + [(t, 1, a) for t in range(4) for a in range(PASSES)]
+        by_tile = [(t, w, a) for t in range(4) for w in range(2) for a in range(PASSES)]
         H = W // 2
-        pair0 = gather_words(0, chain.tile([P, W], I32, name="pair0", align_bytes=64, offset=3072))
-        v0 = part_words(0, pair0)
-        order_scales(0, co_sc_raw)
-        fb_raw = keep.tile([P, GROUPS, 4, N], F32, name="fb_raw", tag="slot_s0", align_bytes=64)
+        pair0 = gather_words(0, chain.tile([P, W], I32, name="pair0", align_bytes=64, offset=8192))
+        order_weight(0, 0, [0])
+        part_words(0, pair0, [0])
+        order_weight(0, 0, [1])
+        part_words(0, pair0, [1])
+        order_weight(1, 0, [0, 1], chain.tile([P, PASSES, 4, P], I32, name="si_q0", align_bytes=64, offset=32768))
+        pair1 = gather_words(1, keep.tile([P, W], I32, name="pair1", align_bytes=64))
+        fb_raw = chain.tile([P, GROUPS, 4, N], F32, name="fb_raw", align_bytes=64, offset=0)
         fb_by_slot = fb.rearrange("(g q t r) n -> g t q r n", g=GROUPS, t=4, r=8)
         for g in range(GROUPS):
             for t in range(4):
                 nc.sync.dma_start(fb_raw[:, g, t, :], fb_by_slot[g, t])
-        order_weight(0, 0)
-        pair1 = gather_words(1, keep.tile([P, W], I32, name="pair1", align_bytes=64))
-        order_scales(1, si_sc_raw)
-        order_weight(1, 0)
-        v1 = part_words(1, pair1)
-        load_weight(0, 1, chain.tile([P, PASSES, W], I32, name="co_raw1", align_bytes=64, offset=16384))
-        load_weight(1, 1, chain.tile([P, PASSES, W], I32, name="si_raw1", align_bytes=64, offset=20480))
-        level = early.tile([P, T], F32, name="level", align_bytes=64, offset=0)
+        load_weight(0, 1, 8192)
+        load_weight(1, 1, 12288)
+        level = chain.tile([P, T], F32, name="level", align_bytes=64, offset=16384)
         nc.sync.dma_start(level[:], ts)
-        sq00 = squares(v0, 0, 0, 4, co_first)
-        sq10 = squares(v1, 1, 0, 4, by_tile)
+        sq00 = squares(0, 0, 4, first_unit)
+        part_words(1, pair1, [0, 1])
+        sq10 = squares(1, 0, 4, by_tile)
         fb_q, fb_sc = filters(fb_raw)
-        order_weight(0, 1)
-        sum00 = power(sq00, 0, W, keep.tile([P, W, 4], BF16, name="h_first", tag="slot_s0", align_bytes=64))
-        order_weight(1, 1)
-        sq01 = squares(v0, 0, 1, 4, by_tile)
-        h00 = quantize(sum00)
+        order_weight(0, 1, [0, 1])
+        order_weight(1, 1, [0, 1])
+        sum00 = power(sq00, 0, W, chain.tile([P, W, 4], BF16, name="h_first", align_bytes=64, offset=10240))
+        sq01 = squares(0, 1, 4, by_tile)
         picked_level = keep.tile([P, J], F32, name="picked_level")
         level0, level1 = picked_level[:, 0:W], picked_level[:, W:J]
-        sum10 = power(sq10, 0, W)
         nc.vector.tensor_copy(level0, level[:].indirect(offsets[:, 0:32]))
-        h10 = quantize(sum10)
-        sq11 = squares(v1, 1, 1, 2, by_tile)
-        sum01 = power(sq01, 0, W)
+        h00 = quantize(sum00)
+        sum10 = power(sq10, 0, W)
         nc.vector.tensor_copy(level1, level[:].indirect(offsets[:, 32:64]))
+        h10 = quantize(sum10)
+        sq11 = squares(1, 1, 2, by_tile)
+        sum01 = power(sq01, 0, W)
         h01 = quantize(sum01)
         sum11a = power(sq11, 0, H)
         finish(0, 0, W, [cut(h00, 0, W), cut(h01, 0, W)], fb_q, fb_sc, level0)

@@ -41,9 +41,9 @@ def tile_list_meltab_gain_kernel(
         tab = keep.tile([P, T], I32, name="tab", align_bytes=64)
         tab_sc = keep.tile([P, T], U8, name="tab_sc", align_bytes=64)
         w_sc_raw = keep.tile([P, 2 * F], U8, name="w_sc_raw", align_bytes=64)
-        joined = chain.tile([P, J + 2 * F], U8, name="joined", align_bytes=64, offset=32768)
+        joined = chain.tile([P, J + 2 * F], U8, name="joined", align_bytes=64, offset=36864)
         planes = [keep.tile([P, J + 2 * F], U8, name="plane%d" % a, align_bytes=64) for a in range(PASSES)]
-        picked_sc = chain.tile([P, J], U8, name="picked_sc", align_bytes=64, offset=0)
+        picked_sc = chain.tile([P, J], U8, name="picked_sc", align_bytes=64, offset=15872)
         gn_rows = keep.tile([P, GROUPS, P], F32, name="gn_rows")
         ident = keep.tile([P, P], F32, name="ident")
         w_raw = {}
@@ -63,8 +63,9 @@ def tile_list_meltab_gain_kernel(
         nc.sync.dma_start(tab_sc[96:P, :].bitcast(I32), tab_scales.rearrange("a q t -> (a q) t").bitcast(I32))
         nc.sync.dma_start(offsets[:], offs)
         nc.sync.dma_start(tab[:], tab_words.rearrange("e p t b -> p (e t b)").bitcast(I32))
-        load_weight(0, 0, 12288)
-        load_weight(1, 0, 16384)
+        load_weight(0, 0, 28672)
+        load_weight(1, 0, 45056)
+
         for w in range(2):
             nc.scalar.dma_start(
                 w_sc_raw[96:P, w * F : (w + 1) * F].bitcast(I32), w_scales[w].rearrange("a q f -> (a q) f").bitcast(I32)
@@ -129,7 +130,8 @@ def tile_list_meltab_gain_kernel(
             later = []
             banks = {}
             for t, w, a in order:
-                if a == 0:
+                first = (t, w) not in banks
+                if first:
                     banks[t, w] = psum.tile([P, W], F32, name="bank")
                 bank = banks[t, w]
                 c0 = J + w * F + g * W + t * P
@@ -139,10 +141,10 @@ def tile_list_meltab_gain_kernel(
                     lhsT_scale=planes[a][:, c0 : c0 + P],
                     rhs=v[jh, a].bitcast(FP4X4),
                     rhs_scale=planes[a][:, jh * W : (jh + 1) * W],
-                    start=(a == 0),
-                    stop=(a == PASSES - 1),
+                    start=first,
+                    stop=not first,
                 )
-                if a == PASSES - 1:
+                if not first:
                     u = 4 * g + t
                     cols = W if t < split_from else W // 2
                     nc.scalar.activation(sq[w][:, t, 0:cols], bank[:, 0:cols], ACT.Square, scale=root[:, u : u + 1])
@@ -172,8 +174,8 @@ def tile_list_meltab_gain_kernel(
             return h_q, h_sc
 
         def filters(fb_raw):
-            nc.vector.tensor_scalar(two_pos[:], gn_p[:], 0.0, 2.0, ALU.is_ge, ALU.mult)
-            nc.vector.tensor_scalar_add(sign[:], two_pos[:], -1.0)
+            nc.gpsimd.tensor_scalar(two_pos[:], gn_p[:], 0.0, 2.0, ALU.is_ge, ALU.mult)
+            nc.gpsimd.tensor_scalar(sign[:], two_pos[:], 1.0, -1.0, ALU.mult, ALU.add)
             fb_b = keep.tile([P, GROUPS, N, 4], BF16, name="fb_b", align_bytes=64)
             for g in range(GROUPS):
                 nc.vector.tensor_tensor(
@@ -191,45 +193,54 @@ def tile_list_meltab_gain_kernel(
             )
             return fb_q, fb_sc
 
-        def finish(jh, c0, c1, hs, fb_q, fb_sc, picked):
-            cols = c1 - c0
+        def filter_bank(bank, nt, hs, fb_q, fb_sc):
+            for g in range(GROUPS):
+                nc.tensor.matmul_mx(
+                    out=bank,
+                    lhsT=fb_q[:, g, nt * P : (nt + 1) * P].bitcast(FP8X4),
+                    lhsT_scale=fb_sc[:, g, nt * P : (nt + 1) * P],
+                    rhs=hs[g][0].bitcast(FP8X4),
+                    rhs_scale=hs[g][1],
+                    start=(g == 0),
+                    stop=(g == GROUPS - 1),
+                )
+
+        def finish_wide(j0, hs, fb_q, fb_sc, picked, tiles):
+            for nt, y in tiles:
+                bank = psum.tile([P, W], F32, name="bank")
+                filter_bank(bank[:], nt, hs, fb_q, fb_sc)
+                nc.vector.tensor_tensor(y[:], bank[:], picked[:, j0 : j0 + W], ALU.mult)
+                nc.sync.dma_start(out[nt * P : (nt + 1) * P, j0 : j0 + W], y[:])
+
+        def finish_narrow(j0, cols, hs, fb_q, fb_sc, picked):
+            bank = psum.tile([P, N // P, cols], F32, name="bank")
             for nt in range(N // P):
-                bank = psum.tile([P, cols], F32, name="bank")
-                for g in range(GROUPS):
-                    nc.tensor.matmul_mx(
-                        out=bank[:],
-                        lhsT=fb_q[:, g, nt * P : (nt + 1) * P].bitcast(FP8X4),
-                        lhsT_scale=fb_sc[:, g, nt * P : (nt + 1) * P],
-                        rhs=hs[g][0].bitcast(FP8X4),
-                        rhs_scale=hs[g][1],
-                        start=(g == 0),
-                        stop=(g == GROUPS - 1),
-                    )
-                y = ring.tile([P, cols], F32, name="y")
-                nc.vector.tensor_tensor(y[:], bank[:], picked[:, c0:c1], ALU.mult)
-                nc.sync.dma_start(out[nt * P : (nt + 1) * P, jh * W + c0 : jh * W + c1], y[:])
+                filter_bank(bank[:, nt, :], nt, hs, fb_q, fb_sc)
+            y = ring.tile([P, N // P, cols], F32, name="y")
+            nc.vector.tensor_tensor(y[:], bank[:], picked[:, j0 : j0 + cols].unsqueeze(1).broadcast_to([P, N // P, cols]), ALU.mult)
+            nc.sync.dma_start(out.rearrange("(nt p) j -> p nt j", p=P)[:, :, j0 : j0 + cols], y[:])
 
         def cut(h, c0, c1):
             return h[0][:, c0:c1], h[1][:, c0:c1]
 
-        first_unit = [(t, 0, a) for a in range(PASSES) for t in range(4)] + [(t, 1, a) for t in range(4) for a in range(PASSES)]
+        first_unit = [(t, 0, a) for a in range(PASSES) for t in range(4)] + [(t, 1, a) for t in range(4) for a in reversed(range(PASSES))]
         by_tile = [(t, w, a) for t in range(4) for w in range(2) for a in range(PASSES)]
         H = W // 2
-        pair0 = gather_words(0, chain.tile([P, W], I32, name="pair0", align_bytes=64, offset=8192))
-        order_weight(0, 0, [0])
-        part_words(0, pair0, [0])
-        order_weight(0, 0, [1])
-        part_words(0, pair0, [1])
-        order_weight(1, 0, [0, 1], chain.tile([P, PASSES, 4, P], I32, name="si_q0", align_bytes=64, offset=32768))
-        pair1 = gather_words(1, keep.tile([P, W], I32, name="pair1", align_bytes=64))
-        fb_raw = chain.tile([P, GROUPS, 4, N], F32, name="fb_raw", align_bytes=64, offset=0)
+        fb_raw = chain.tile([P, GROUPS, 4, N], F32, name="fb_raw", align_bytes=64, offset=16384)
         fb_by_slot = fb.rearrange("(g q t r) n -> g t q r n", g=GROUPS, t=4, r=8)
         for g in range(GROUPS):
             for t in range(4):
                 nc.sync.dma_start(fb_raw[:, g, t, :], fb_by_slot[g, t])
-        load_weight(0, 1, 8192)
-        load_weight(1, 1, 12288)
-        level = chain.tile([P, T], F32, name="level", align_bytes=64, offset=16384)
+        pair0 = gather_words(0, chain.tile([P, W], I32, name="pair0", align_bytes=64, offset=40960))
+        order_weight(0, 0, [0])
+        part_words(0, pair0, [0])
+        order_weight(0, 0, [1])
+        part_words(0, pair0, [1])
+        order_weight(1, 0, [0, 1])
+        pair1 = gather_words(1, chain.tile([P, W], I32, name="pair1", align_bytes=64, offset=30720))
+        load_weight(0, 1, 40960)
+        load_weight(1, 1, 25600)
+        level = chain.tile([P, T], F32, name="level", align_bytes=64, offset=45056)
         nc.sync.dma_start(level[:], ts)
         sq00 = squares(0, 0, 4, first_unit)
         part_words(1, pair1, [0, 1])
@@ -237,22 +248,22 @@ def tile_list_meltab_gain_kernel(
         fb_q, fb_sc = filters(fb_raw)
         order_weight(0, 1, [0, 1])
         order_weight(1, 1, [0, 1])
-        sum00 = power(sq00, 0, W, chain.tile([P, W, 4], BF16, name="h_first", align_bytes=64, offset=10240))
+        sum00 = power(sq00, 0, W, chain.tile([P, W, 4], BF16, name="h_first", align_bytes=64, offset=24576))
         sq01 = squares(0, 1, 4, by_tile)
-        picked_level = keep.tile([P, J], F32, name="picked_level")
-        level0, level1 = picked_level[:, 0:W], picked_level[:, W:J]
-        nc.vector.tensor_copy(level0, level[:].indirect(offsets[:, 0:32]))
         h00 = quantize(sum00)
+        picked_level = keep.tile([P, J], F32, name="picked_level")
+        nc.vector.tensor_copy(picked_level[:], level[:].indirect(offsets[:]))
         sum10 = power(sq10, 0, W)
-        nc.vector.tensor_copy(level1, level[:].indirect(offsets[:, 32:64]))
         h10 = quantize(sum10)
         sq11 = squares(1, 1, 2, by_tile)
         sum01 = power(sq01, 0, W)
         h01 = quantize(sum01)
         sum11a = power(sq11, 0, H)
-        finish(0, 0, W, [cut(h00, 0, W), cut(h01, 0, W)], fb_q, fb_sc, level0)
+        left = [cut(h00, 0, W), cut(h01, 0, W)]
+        finish_wide(0, left, fb_q, fb_sc, picked_level, [(0, keep.tile([P, W], F32, name="y_first"))])
         h11a = quantize(sum11a)
-        sum11b = power(sq11, H, W)
-        finish(1, 0, H, [cut(h10, 0, H), cut(h11a, 0, H)], fb_q, fb_sc, level1)
+        sum11b = power(sq11, H, W, chain.tile([P, H, 4], BF16, name="h_last", align_bytes=64, offset=0))
+        finish_narrow(W, H, [cut(h10, 0, H), cut(h11a, 0, H)], fb_q, fb_sc, picked_level)
         h11b = quantize(sum11b)
-        finish(1, H, W, [cut(h10, H, W), cut(h11b, 0, H)], fb_q, fb_sc, level1)
+        finish_wide(0, left, fb_q, fb_sc, picked_level, [(1, chain.tile([P, W], F32, name="y_second", align_bytes=64, offset=0))])
+        finish_narrow(W + H, H, [cut(h10, H, W), cut(h11b, 0, H)], fb_q, fb_sc, picked_level)

@@ -123,35 +123,44 @@ def tile_list_meltab_gain_kernel(
             for i, a in enumerate(passes):
                 w_q[w, g, a] = tile[:, i]
 
-        def squares(jh, g, split_from, order):
-            sq = []
-            for w in range(2):
-                sq.append(ring.tile([P, 4, W], F32, name="sq%d" % w, align_bytes=64))
-            later = []
+        def product(bank, jh, g, t, w, a, c0, cols, first):
+            f0 = J + w * F + g * W + t * P
+            j0 = jh * W + c0
+            nc.tensor.matmul_mx(
+                out=bank,
+                lhsT=w_q[w, g, a][:, t, :].bitcast(FP8X4),
+                lhsT_scale=planes[a][:, f0 : f0 + P],
+                rhs=v[jh, a][:, 2 * c0 : 2 * (c0 + cols)].bitcast(FP4X4),
+                rhs_scale=planes[a][:, j0 : j0 + cols],
+                start=first,
+                stop=not first,
+            )
+
+        def squares(jh, g, order):
+            sq = [ring.tile([P, 4, W], F32, name="sq%d" % w, align_bytes=64, bufs=3) for w in range(2)]
             banks = {}
             for t, w, a in order:
                 first = (t, w) not in banks
                 if first:
                     banks[t, w] = psum.tile([P, W], F32, name="bank")
-                bank = banks[t, w]
-                c0 = J + w * F + g * W + t * P
-                nc.tensor.matmul_mx(
-                    out=bank[:],
-                    lhsT=w_q[w, g, a][:, t, :].bitcast(FP8X4),
-                    lhsT_scale=planes[a][:, c0 : c0 + P],
-                    rhs=v[jh, a].bitcast(FP4X4),
-                    rhs_scale=planes[a][:, jh * W : (jh + 1) * W],
-                    start=first,
-                    stop=not first,
-                )
+                product(banks[t, w][:], jh, g, t, w, a, 0, W, first)
                 if not first:
                     u = 4 * g + t
-                    cols = W if t < split_from else W // 2
-                    nc.scalar.activation(sq[w][:, t, 0:cols], bank[:, 0:cols], ACT.Square, scale=root[:, u : u + 1])
-                    if cols < W:
-                        later.append((w, t, u, bank))
-            for w, t, u, bank in later:
-                nc.scalar.activation(sq[w][:, t, W // 2 : W], bank[:, W // 2 : W], ACT.Square, scale=root[:, u : u + 1])
+                    nc.scalar.activation(sq[w][:, t, :], banks[t, w][:], ACT.Square, scale=root[:, u : u + 1])
+            return sq
+
+        def narrow_squares(jh, g, c0, cols):
+            sq = [keep.tile([P, 4, cols], F32, name="sq%d_%d" % (w, c0), align_bytes=64) for w in range(2)]
+            for t0 in range(0, 4, 2):
+                for w in range(2):
+                    bank = psum.tile([P, 2, cols], F32, name="bank")
+                    for t in range(t0, t0 + 2):
+                        for c in range(0, cols, P):
+                            for a in range(PASSES):
+                                product(bank[:, t - t0, c : c + P], jh, g, t, w, a, c0 + c, P, a == 0)
+                    for t in range(t0, t0 + 2):
+                        u = 4 * g + t
+                        nc.scalar.activation(sq[w][:, t, :], bank[:, t - t0, :], ACT.Square, scale=root[:, u : u + 1])
             return sq
 
         def power(sq, c0, c1, h=None):
@@ -168,10 +177,10 @@ def tile_list_meltab_gain_kernel(
 
         def quantize(h):
             cols = h.shape[1]
-            h_q = ring.tile([P, cols], U32, name="h_q", align_bytes=64, bufs=5)
-            h_sc = ring.tile([P, cols], U8, name="h_sc", align_bytes=64, bufs=5)
+            h_q = ring.tile([P, cols], U32, name="h_q", align_bytes=64, bufs=6)
+            h_sc = ring.tile([P, cols], U8, name="h_sc", align_bytes=64, bufs=6)
             nc.vector.quantize_mx(out=h_q[:].bitcast(FP8X4), scales=h_sc[:], in_=h[:].rearrange("p c t -> p (c t)"))
-            return h_q, h_sc
+            return h_q[:], h_sc[:]
 
         def filters(fb_raw):
             nc.gpsimd.tensor_scalar(two_pos[:], gn_p[:], 0.0, 2.0, ALU.is_ge, ALU.mult)
@@ -205,8 +214,9 @@ def tile_list_meltab_gain_kernel(
                     stop=(g == GROUPS - 1),
                 )
 
-        def finish_wide(j0, hs, fb_q, fb_sc, picked, tiles):
-            for nt, y in tiles:
+        def finish_wide(j0, hs, fb_q, fb_sc, picked):
+            for nt in range(N // P):
+                y = ring.tile([P, W], F32, name="y")
                 bank = psum.tile([P, W], F32, name="bank")
                 filter_bank(bank[:], nt, hs, fb_q, fb_sc)
                 nc.vector.tensor_tensor(y[:], bank[:], picked[:, j0 : j0 + W], ALU.mult)
@@ -242,28 +252,29 @@ def tile_list_meltab_gain_kernel(
         load_weight(1, 1, 25600)
         level = chain.tile([P, T], F32, name="level", align_bytes=64, offset=45056)
         nc.sync.dma_start(level[:], ts)
-        sq00 = squares(0, 0, 4, first_unit)
+        sq00 = squares(0, 0, first_unit)
         part_words(1, pair1, [0, 1])
-        sq10 = squares(1, 0, 4, by_tile)
+        sq10 = squares(1, 0, by_tile)
         fb_q, fb_sc = filters(fb_raw)
         order_weight(0, 1, [0, 1])
         order_weight(1, 1, [0, 1])
         sum00 = power(sq00, 0, W, chain.tile([P, W, 4], BF16, name="h_first", align_bytes=64, offset=24576))
-        sq01 = squares(0, 1, 4, by_tile)
+        sq01 = squares(0, 1, by_tile)
         h00 = quantize(sum00)
         picked_level = keep.tile([P, J], F32, name="picked_level")
         nc.vector.tensor_copy(picked_level[:], level[:].indirect(offsets[:]))
         sum10 = power(sq10, 0, W)
         h10 = quantize(sum10)
-        sq11 = squares(1, 1, 2, by_tile)
+        Q = W // 4
+        sq11a = narrow_squares(1, 1, 0, H)
+        sq11b = narrow_squares(1, 1, H, Q)
+        sq11c = narrow_squares(1, 1, H + Q, Q)
         sum01 = power(sq01, 0, W)
         h01 = quantize(sum01)
-        sum11a = power(sq11, 0, H)
-        left = [cut(h00, 0, W), cut(h01, 0, W)]
-        finish_wide(0, left, fb_q, fb_sc, picked_level, [(0, keep.tile([P, W], F32, name="y_first"))])
-        h11a = quantize(sum11a)
-        sum11b = power(sq11, H, W, chain.tile([P, H, 4], BF16, name="h_last", align_bytes=64, offset=0))
-        finish_narrow(W, H, [cut(h10, 0, H), cut(h11a, 0, H)], fb_q, fb_sc, picked_level)
-        h11b = quantize(sum11b)
-        finish_wide(0, left, fb_q, fb_sc, picked_level, [(1, chain.tile([P, W], F32, name="y_second", align_bytes=64, offset=0))])
-        finish_narrow(W + H, H, [cut(h10, H, W), cut(h11b, 0, H)], fb_q, fb_sc, picked_level)
+        finish_wide(0, [h00, h01], fb_q, fb_sc, picked_level)
+        h11a = quantize(power(sq11a, 0, H))
+        finish_narrow(W, H, [cut(h10, 0, H), h11a], fb_q, fb_sc, picked_level)
+        h11b = quantize(power(sq11b, 0, Q))
+        finish_narrow(W + H, Q, [cut(h10, H, H + Q), h11b], fb_q, fb_sc, picked_level)
+        h11c = quantize(power(sq11c, 0, Q))
+        finish_narrow(W + H + Q, Q, [cut(h10, H + Q, W), h11c], fb_q, fb_sc, picked_level)

@@ -22,6 +22,7 @@ W = 512
 HALVES = J // W
 GROUPS = F // 512
 PASSES = K // 512
+ROW = 8
 
 
 def tile_list_meltab_gain_kernel(
@@ -35,12 +36,13 @@ def tile_list_meltab_gain_kernel(
         keep = ctx.enter_context(tc.tile_pool(name="keep", bufs=1))
         ring = ctx.enter_context(tc.tile_pool(name="ring", bufs=4))
         chain = ctx.enter_context(tc.tile_pool(name="chain", bufs=1))
+        tail = ctx.enter_context(tc.tile_pool(name="tail", bufs=1))
         psum = ctx.enter_context(tc.psum_pool(name="psum", bufs=8))
 
         offsets = keep.tile([P, J // 16], U16, name="offsets")
         tab = keep.tile([P, T], I32, name="tab", align_bytes=64)
         tab_sc = keep.tile([P, T], U8, name="tab_sc", align_bytes=64)
-        w_sc_raw = keep.tile([P, 2 * F], U8, name="w_sc_raw", align_bytes=64)
+        w_sc_raw = chain.tile([P, 2 * F], U8, name="w_sc_raw", align_bytes=64, offset=45056)
         joined = chain.tile([P, J + 2 * F], U8, name="joined", align_bytes=64, offset=36864)
         planes = [keep.tile([P, J + 2 * F], U8, name="plane%d" % a, align_bytes=64) for a in range(PASSES)]
         picked_sc = chain.tile([P, J], U8, name="picked_sc", align_bytes=64, offset=15872)
@@ -64,31 +66,14 @@ def tile_list_meltab_gain_kernel(
         nc.sync.dma_start(offsets[:], offs)
         nc.sync.dma_start(tab[:], tab_words.rearrange("e p t b -> p (e t b)").bitcast(I32))
         load_weight(0, 0, 28672)
-        load_weight(1, 0, 45056)
 
         for w in range(2):
             nc.scalar.dma_start(
                 w_sc_raw[96:P, w * F : (w + 1) * F].bitcast(I32), w_scales[w].rearrange("a q f -> (a q) f").bitcast(I32)
             )
-        warm = keep.tile([P, 1], F32, name="warm")
-        zero = keep.tile([P, 1], F32, name="zero")
-        nc.gpsimd.memset(zero[:], 0.0)
-        nc.scalar.activation(warm[:], zero[:], ACT.Sqrt)
         make_identity(nc, ident[:])
         for a in range(PASSES):
             nc.vector.memset(planes[a][:].bitcast(I32), 0)
-
-        gn_t = psum.tile([P, GROUPS, P], F32, name="bank")
-        for g in range(GROUPS):
-            nc.tensor.transpose(gn_t[:, g, :], gn_rows[:, g, :], ident[:])
-        gn_p = keep.tile([P, GROUPS, 4], F32, name="gn_p")
-        two_pos = keep.tile([P, GROUPS, 4], F32, name="two_pos")
-        sign = keep.tile([P, GROUPS, 4], F32, name="sign")
-        gn_abs = keep.tile([P, GROUPS, 4], F32, name="gn_abs")
-        root = keep.tile([P, 8], F32, name="root")
-        nc.scalar.activation(gn_abs[:], gn_t[:, :, 0:4], ACT.Abs)
-        nc.scalar.copy(gn_p[:], gn_t[:, :, 0:4])
-        nc.scalar.activation(root[:], gn_abs[:].rearrange("p g t -> p (g t)"), ACT.Sqrt)
 
         nc.vector.tensor_copy(picked_sc[:], tab_sc[:].indirect(offsets[:]))
         nc.vector.tensor_copy(
@@ -96,9 +81,35 @@ def tile_list_meltab_gain_kernel(
             w_sc_raw[96:P, :].bitcast(I32).rearrange("p (x q t e) -> p t x q e", t=4, q=16, e=2),
         )
         nc.vector.tensor_copy(joined[96:P, 0:J].bitcast(I32), picked_sc[96:P, :].bitcast(I32))
-        for a in range(PASSES):
+        for a, queue in enumerate((nc.scalar, nc.sync)):
             for r in range(4):
-                nc.scalar.dma_start(planes[a][r:P:32, :].bitcast(I32), joined[96 + 16 * a + r : 96 + 16 * a + 16 : 4, :].bitcast(I32))
+                queue.dma_start(planes[a][r:P:32, :].bitcast(I32), joined[96 + 16 * a + r : 96 + 16 * a + 16 : 4, :].bitcast(I32))
+
+        load_weight(1, 0, 12288)
+
+        gn_t = psum.tile([P, GROUPS, P], F32, name="bank")
+        for g in range(GROUPS):
+            nc.tensor.transpose(gn_t[:, g, :], gn_rows[:, g, :], ident[:])
+        two_pos = keep.tile([P, GROUPS, 4], F32, name="two_pos")
+        sign = keep.tile([P, GROUPS, 4], F32, name="sign")
+        gn_abs = keep.tile([P, GROUPS, 4], F32, name="gn_abs")
+        root = keep.tile([P, 8], F32, name="root")
+        nc.vector.tensor_scalar(two_pos[:], gn_t[:, :, 0:4], 0.0, 2.0, ALU.is_ge, ALU.mult)
+        nc.vector.tensor_scalar_add(sign[:], two_pos[:], -1.0)
+        nc.vector.tensor_tensor(gn_abs[:], gn_t[:, :, 0:4], sign[:], ALU.mult)
+        nc.scalar.activation(root[:], gn_abs[:].rearrange("p g t -> p (g t)"), ACT.Sqrt)
+
+        level = chain.tile([P, T], F32, name="level", align_bytes=64, offset=45056)
+        for c0 in range(0, T, W):
+            nc.gpsimd.memset(level[:, c0 : c0 + W], 0.0)
+        nc.scalar.dma_start(level[ROW : ROW + 1, :], ts[0:1, :])
+        picked_level = keep.tile([P, J], F32, name="picked_level")
+
+        def spread_level(jh, picked_row):
+            cols = slice(jh * W, (jh + 1) * W)
+            nc.vector.tensor_copy(picked_row[:], level[:].indirect(offsets[:, 32 * jh : 32 * jh + 32]))
+            nc.sync.dma_start(out[0:1, cols], picked_row[ROW : ROW + 1, :])
+            nc.sync.dma_start(picked_level[:, cols], out[0, cols].partition_broadcast(P))
 
         def gather_words(jh, pair):
             nc.vector.tensor_copy(pair[:].bitcast(U32), tab[:].bitcast(U32).indirect(offsets[:, 32 * jh : 32 * jh + 32]))
@@ -150,7 +161,10 @@ def tile_list_meltab_gain_kernel(
             return sq
 
         def narrow_squares(jh, g, c0, cols):
-            sq = [keep.tile([P, 4, cols], F32, name="sq%d_%d" % (w, c0), align_bytes=64) for w in range(2)]
+            sq = [
+                tail.tile([P, 4, cols], F32, name="sq%d_%d" % (w, c0), align_bytes=64, offset=16 * (2 * c0 + w * cols))
+                for w in range(2)
+            ]
             for t0 in range(0, 4, 2):
                 for w in range(2):
                     bank = psum.tile([P, 2, cols], F32, name="bank")
@@ -175,16 +189,15 @@ def tile_list_meltab_gain_kernel(
             )
             return h
 
-        def quantize(h):
+        def quantize(h, h_q=None):
             cols = h.shape[1]
-            h_q = ring.tile([P, cols], U32, name="h_q", align_bytes=64, bufs=6)
+            if h_q is None:
+                h_q = ring.tile([P, cols], U32, name="h_q", align_bytes=64, bufs=6)
             h_sc = ring.tile([P, cols], U8, name="h_sc", align_bytes=64, bufs=6)
             nc.vector.quantize_mx(out=h_q[:].bitcast(FP8X4), scales=h_sc[:], in_=h[:].rearrange("p c t -> p (c t)"))
             return h_q[:], h_sc[:]
 
         def filters(fb_raw):
-            nc.gpsimd.tensor_scalar(two_pos[:], gn_p[:], 0.0, 2.0, ALU.is_ge, ALU.mult)
-            nc.gpsimd.tensor_scalar(sign[:], two_pos[:], 1.0, -1.0, ALU.mult, ALU.add)
             fb_b = keep.tile([P, GROUPS, N, 4], BF16, name="fb_b", align_bytes=64)
             for g in range(GROUPS):
                 nc.vector.tensor_tensor(
@@ -214,26 +227,24 @@ def tile_list_meltab_gain_kernel(
                     stop=(g == GROUPS - 1),
                 )
 
-        def finish_wide(j0, hs, fb_q, fb_sc, picked):
-            for nt in range(N // P):
-                y = ring.tile([P, W], F32, name="y")
-                bank = psum.tile([P, W], F32, name="bank")
-                filter_bank(bank[:], nt, hs, fb_q, fb_sc)
-                nc.vector.tensor_tensor(y[:], bank[:], picked[:, j0 : j0 + W], ALU.mult)
-                nc.sync.dma_start(out[nt * P : (nt + 1) * P, j0 : j0 + W], y[:])
+        def finish_wide(nt, hs, fb_q, fb_sc, picked, y):
+            bank = psum.tile([P, W], F32, name="bank")
+            filter_bank(bank[:], nt, hs, fb_q, fb_sc)
+            nc.vector.tensor_tensor(y[:], bank[:], picked[:, 0:W], ALU.mult)
+            nc.sync.dma_start(out[nt * P : (nt + 1) * P, 0:W], y[:])
 
-        def finish_narrow(j0, cols, hs, fb_q, fb_sc, picked):
+        def finish_narrow(j0, cols, hs, fb_q, fb_sc, picked, y):
             bank = psum.tile([P, N // P, cols], F32, name="bank")
             for nt in range(N // P):
                 filter_bank(bank[:, nt, :], nt, hs, fb_q, fb_sc)
-            y = ring.tile([P, N // P, cols], F32, name="y")
             nc.vector.tensor_tensor(y[:], bank[:], picked[:, j0 : j0 + cols].unsqueeze(1).broadcast_to([P, N // P, cols]), ALU.mult)
             nc.sync.dma_start(out.rearrange("(nt p) j -> p nt j", p=P)[:, :, j0 : j0 + cols], y[:])
 
         def cut(h, c0, c1):
             return h[0][:, c0:c1], h[1][:, c0:c1]
 
-        first_unit = [(t, 0, a) for a in range(PASSES) for t in range(4)] + [(t, 1, a) for t in range(4) for a in reversed(range(PASSES))]
+        first_unit = [(t, 0, a) for a in range(PASSES) for t in range(2)]
+        first_unit += [(t, w, a) for w in range(2) for t in range(4) if w or t >= 2 for a in reversed(range(PASSES))]
         by_tile = [(t, w, a) for t in range(4) for w in range(2) for a in range(PASSES)]
         H = W // 2
         fb_raw = chain.tile([P, GROUPS, 4, N], F32, name="fb_raw", align_bytes=64, offset=16384)
@@ -250,19 +261,17 @@ def tile_list_meltab_gain_kernel(
         pair1 = gather_words(1, chain.tile([P, W], I32, name="pair1", align_bytes=64, offset=30720))
         load_weight(0, 1, 40960)
         load_weight(1, 1, 25600)
-        level = chain.tile([P, T], F32, name="level", align_bytes=64, offset=45056)
-        nc.sync.dma_start(level[:], ts)
         sq00 = squares(0, 0, first_unit)
         part_words(1, pair1, [0, 1])
+        spread_level(0, chain.tile([P, W], F32, name="picked_row0", align_bytes=64, offset=30720))
         sq10 = squares(1, 0, by_tile)
         fb_q, fb_sc = filters(fb_raw)
         order_weight(0, 1, [0, 1])
         order_weight(1, 1, [0, 1])
         sum00 = power(sq00, 0, W, chain.tile([P, W, 4], BF16, name="h_first", align_bytes=64, offset=24576))
         sq01 = squares(0, 1, by_tile)
+        spread_level(1, chain.tile([P, W], F32, name="picked_row1", align_bytes=64, offset=28672))
         h00 = quantize(sum00)
-        picked_level = keep.tile([P, J], F32, name="picked_level")
-        nc.vector.tensor_copy(picked_level[:], level[:].indirect(offsets[:]))
         sum10 = power(sq10, 0, W)
         h10 = quantize(sum10)
         Q = W // 4
@@ -270,11 +279,18 @@ def tile_list_meltab_gain_kernel(
         sq11b = narrow_squares(1, 1, H, Q)
         sq11c = narrow_squares(1, 1, H + Q, Q)
         sum01 = power(sq01, 0, W)
-        h01 = quantize(sum01)
-        finish_wide(0, [h00, h01], fb_q, fb_sc, picked_level)
-        h11a = quantize(power(sq11a, 0, H))
-        finish_narrow(W, H, [cut(h10, 0, H), h11a], fb_q, fb_sc, picked_level)
-        h11b = quantize(power(sq11b, 0, Q))
-        finish_narrow(W + H, Q, [cut(h10, H, H + Q), h11b], fb_q, fb_sc, picked_level)
-        h11c = quantize(power(sq11c, 0, Q))
-        finish_narrow(W + H + Q, Q, [cut(h10, H + Q, W), h11c], fb_q, fb_sc, picked_level)
+        sum11a = power(sq11a, 0, H)
+        h01 = quantize(sum01, tail.tile([P, W], U32, name="h_q01", align_bytes=64, offset=0))
+        h11a = quantize(sum11a)
+        sum11b = power(sq11b, 0, Q)
+        finish_wide(0, [h00, h01], fb_q, fb_sc, picked_level, tail.tile([P, W], F32, name="y0", align_bytes=64, offset=8192))
+        h11b = quantize(sum11b)
+        sum11c = power(sq11c, 0, Q, tail.tile([P, Q, 4], BF16, name="h_last", align_bytes=64, offset=18432))
+        finish_wide(1, [h00, h01], fb_q, fb_sc, picked_level, tail.tile([P, W], F32, name="y1", align_bytes=64, offset=12288))
+        h11c = quantize(sum11c)
+        y_a = tail.tile([P, 2, H], F32, name="y_a", align_bytes=64, offset=18432 + 512 - 2048)
+        finish_narrow(W, H, [cut(h10, 0, H), h11a], fb_q, fb_sc, picked_level, y_a)
+        y_b = tail.tile([P, 2, Q], F32, name="y_b", align_bytes=64, offset=18432 + 512)
+        finish_narrow(W + H, Q, [cut(h10, H, H + Q), h11b], fb_q, fb_sc, picked_level, y_b)
+        y_c = keep.tile([P, 2, Q], F32, name="y_c", align_bytes=64)
+        finish_narrow(W + H + Q, Q, [cut(h10, H + Q, W), h11c], fb_q, fb_sc, picked_level, y_c)

@@ -22,7 +22,7 @@ W = 512
 HALVES = J // W
 GROUPS = F // 512
 PASSES = K // 512
-ROW = 8
+ROW = 127
 
 
 def tile_list_meltab_gain_kernel(
@@ -37,17 +37,24 @@ def tile_list_meltab_gain_kernel(
         ring = ctx.enter_context(tc.tile_pool(name="ring", bufs=4))
         chain = ctx.enter_context(tc.tile_pool(name="chain", bufs=1))
         tail = ctx.enter_context(tc.tile_pool(name="tail", bufs=1))
-        psum = ctx.enter_context(tc.psum_pool(name="psum", bufs=8))
+        psum = ctx.enter_context(tc.psum_pool(name="psum", bufs=1))
 
         offsets = keep.tile([P, J // 16], U16, name="offsets")
         tab = keep.tile([P, T], I32, name="tab", align_bytes=64)
         tab_sc = keep.tile([P, T], U8, name="tab_sc", align_bytes=64)
-        w_sc_raw = chain.tile([P, 2 * F], U8, name="w_sc_raw", align_bytes=64, offset=45056)
-        joined = chain.tile([P, J + 2 * F], U8, name="joined", align_bytes=64, offset=36864)
-        planes = [keep.tile([P, J + 2 * F], U8, name="plane%d" % a, align_bytes=64) for a in range(PASSES)]
-        picked_sc = chain.tile([P, J], U8, name="picked_sc", align_bytes=64, offset=15872)
+        w_sc_raw = keep.tile([P, 4 * W], U8, name="w_sc_raw", align_bytes=64)
+        widths = (2 * W, 4 * W)
+        joined = [keep.tile([P, widths[jh]], U8, name="joined%d" % jh, align_bytes=64) for jh in range(HALVES)]
+        planes = [keep.tile([P, PASSES, widths[jh]], U8, name="planes%d" % jh, align_bytes=64) for jh in range(HALVES)]
         gn_rows = keep.tile([P, GROUPS, P], F32, name="gn_rows")
         ident = keep.tile([P, P], F32, name="ident")
+        level = chain.tile([P, T], F32, name="level", align_bytes=64, offset=28672)
+        turns = []
+
+        def next_bank(shape):
+            turns.append(shape)
+            return psum.tile(shape, F32, name="bank%d" % (len(turns) % 8))
+
         w_raw = {}
         w_q = {}
 
@@ -57,59 +64,67 @@ def tile_list_meltab_gain_kernel(
             words = w_words[w].rearrange("a p f b -> p a (f b)").bitcast(I32)
             nc.sync.dma_start(raw[:], words[:, :, g * W : (g + 1) * W])
 
-        nc.gpsimd.memset(gn_rows[:], 0.0)
-        nc.vector.memset(tab_sc[0:96, :].bitcast(I32), 0)
-        nc.sync.dma_start(
-            gn_rows[0:4].rearrange("t g (q r) -> t (g q) r", r=8), gn.rearrange("(x t r) -> t x r", t=4, r=8)
-        )
-        nc.sync.dma_start(tab_sc[96:P, :].bitcast(I32), tab_scales.rearrange("a q t -> (a q) t").bitcast(I32))
+        nc.sync.dma_start(tab_sc[96:P, :].bitcast(I32), tab_scales.bitcast(I32).rearrange("a q t -> q a t"))
         nc.sync.dma_start(offsets[:], offs)
+        nc.sync.dma_start(
+            gn_rows[P - 4 : P].rearrange("t g (q r) -> t (g q) r", r=8), gn.rearrange("(x t r) -> t x r", t=4, r=8)
+        )
         nc.sync.dma_start(tab[:], tab_words.rearrange("e p t b -> p (e t b)").bitcast(I32))
-        load_weight(0, 0, 28672)
+        load_weight(0, 0, 24576)
 
         for w in range(2):
             nc.scalar.dma_start(
-                w_sc_raw[96:P, w * F : (w + 1) * F].bitcast(I32), w_scales[w].rearrange("a q f -> (a q) f").bitcast(I32)
+                w_sc_raw[96:P, w * F : (w + 1) * F].bitcast(I32), w_scales[w].bitcast(I32).rearrange("a q f -> q a f")
             )
+        nc.scalar.dma_start(level[ROW : ROW + 1, :], ts[0:1, :])
+
+        nc.vector.memset(tab_sc[0:96, :].bitcast(I32), 0)
+        for jh in range(HALVES):
+            nc.vector.memset(planes[jh][:].bitcast(I32), 0)
+        nc.gpsimd.memset(gn_rows[0 : P - 4], 0.0)
         make_identity(nc, ident[:])
-        for a in range(PASSES):
-            nc.vector.memset(planes[a][:].bitcast(I32), 0)
+        for c0 in range(0, T, W):
+            nc.gpsimd.memset(level[0:ROW, c0 : c0 + W], 0.0)
 
-        nc.vector.tensor_copy(picked_sc[:], tab_sc[:].indirect(offsets[:]))
-        nc.vector.tensor_copy(
-            joined[96:P, J:].bitcast(I32).rearrange("p (x t q e) -> p t x q e", t=4, q=16, e=2),
-            w_sc_raw[96:P, :].bitcast(I32).rearrange("p (x q t e) -> p t x q e", t=4, q=16, e=2),
-        )
-        nc.vector.tensor_copy(joined[96:P, 0:J].bitcast(I32), picked_sc[96:P, :].bitcast(I32))
-        for a, queue in enumerate((nc.scalar, nc.sync)):
-            for r in range(4):
-                queue.dma_start(planes[a][r:P:32, :].bitcast(I32), joined[96 + 16 * a + r : 96 + 16 * a + 16 : 4, :].bitcast(I32))
+        def fill_planes(jh, x0, x1, queue):
+            picked_sc = keep.tile([P, W], U8, name="picked_sc%d" % jh, align_bytes=64)
+            nc.vector.tensor_copy(picked_sc[:], tab_sc[:].indirect(offsets[:, 32 * jh : 32 * jh + 32]))
+            nc.vector.tensor_copy(
+                joined[jh][96:P, W:].bitcast(I32).rearrange("p (x t q e) -> p t x q e", t=4, q=16, e=2),
+                w_sc_raw[96:P, x0 * W : x1 * W].bitcast(I32).rearrange("p (x q t e) -> p t x q e", t=4, q=16, e=2),
+            )
+            nc.vector.tensor_copy(joined[jh][96:P, 0:W].bitcast(I32), picked_sc[96:P, :].bitcast(I32))
+            for quad in range(4):
+                queue.dma_start(
+                    planes[jh][32 * quad : 32 * quad + 4].bitcast(I32),
+                    joined[jh][96 + 8 * quad : 96 + 8 * quad + 8, :].bitcast(I32),
+                )
 
-        load_weight(1, 0, 12288)
+        fill_planes(0, 0, 1, nc.scalar)
+        fill_planes(1, 1, 4, nc.sync)
+        load_weight(1, 0, 0)
+        load_weight(0, 1, 4096)
+        load_weight(1, 1, 8192)
+        fb_raw = chain.tile([P, GROUPS, 4, N], F32, name="fb_raw", align_bytes=64, offset=12288)
+        fb_by_slot = fb.rearrange("(g q t r) n -> g t q r n", g=GROUPS, t=4, r=8)
+        for g in range(GROUPS):
+            for t in range(4):
+                nc.sync.dma_start(fb_raw[:, g, t, :], fb_by_slot[g, t])
 
-        gn_t = psum.tile([P, GROUPS, P], F32, name="bank")
+        gn_t = next_bank([P, GROUPS, P])
         for g in range(GROUPS):
             nc.tensor.transpose(gn_t[:, g, :], gn_rows[:, g, :], ident[:])
         two_pos = keep.tile([P, GROUPS, 4], F32, name="two_pos")
         sign = keep.tile([P, GROUPS, 4], F32, name="sign")
         gn_abs = keep.tile([P, GROUPS, 4], F32, name="gn_abs")
         root = keep.tile([P, 8], F32, name="root")
-        nc.vector.tensor_scalar(two_pos[:], gn_t[:, :, 0:4], 0.0, 2.0, ALU.is_ge, ALU.mult)
+        nc.vector.tensor_scalar(two_pos[:], gn_t[:, :, P - 4 : P], 0.0, 2.0, ALU.is_ge, ALU.mult)
         nc.vector.tensor_scalar_add(sign[:], two_pos[:], -1.0)
-        nc.vector.tensor_tensor(gn_abs[:], gn_t[:, :, 0:4], sign[:], ALU.mult)
+        nc.vector.tensor_tensor(gn_abs[:], gn_t[:, :, P - 4 : P], sign[:], ALU.mult)
         nc.scalar.activation(root[:], gn_abs[:].rearrange("p g t -> p (g t)"), ACT.Sqrt)
 
-        level = chain.tile([P, T], F32, name="level", align_bytes=64, offset=45056)
-        for c0 in range(0, T, W):
-            nc.gpsimd.memset(level[:, c0 : c0 + W], 0.0)
-        nc.scalar.dma_start(level[ROW : ROW + 1, :], ts[0:1, :])
         picked_level = keep.tile([P, J], F32, name="picked_level")
 
-        def spread_level(jh, picked_row):
-            cols = slice(jh * W, (jh + 1) * W)
-            nc.vector.tensor_copy(picked_row[:], level[:].indirect(offsets[:, 32 * jh : 32 * jh + 32]))
-            nc.sync.dma_start(out[0:1, cols], picked_row[ROW : ROW + 1, :])
-            nc.sync.dma_start(picked_level[:, cols], out[0, cols].partition_broadcast(P))
 
         def gather_words(jh, pair):
             nc.vector.tensor_copy(pair[:].bitcast(U32), tab[:].bitcast(U32).indirect(offsets[:, 32 * jh : 32 * jh + 32]))
@@ -135,14 +150,14 @@ def tile_list_meltab_gain_kernel(
                 w_q[w, g, a] = tile[:, i]
 
         def product(bank, jh, g, t, w, a, c0, cols, first):
-            f0 = J + w * F + g * W + t * P
-            j0 = jh * W + c0
+            x = 2 * w + g
+            f0 = max(x, 1) * W + t * P
             nc.tensor.matmul_mx(
                 out=bank,
                 lhsT=w_q[w, g, a][:, t, :].bitcast(FP8X4),
-                lhsT_scale=planes[a][:, f0 : f0 + P],
+                lhsT_scale=planes[min(x, 1)][:, a, f0 : f0 + P],
                 rhs=v[jh, a][:, 2 * c0 : 2 * (c0 + cols)].bitcast(FP4X4),
-                rhs_scale=planes[a][:, j0 : j0 + cols],
+                rhs_scale=planes[jh][:, a, c0 : c0 + cols],
                 start=first,
                 stop=not first,
             )
@@ -153,7 +168,7 @@ def tile_list_meltab_gain_kernel(
             for t, w, a in order:
                 first = (t, w) not in banks
                 if first:
-                    banks[t, w] = psum.tile([P, W], F32, name="bank")
+                    banks[t, w] = next_bank([P, W])
                 product(banks[t, w][:], jh, g, t, w, a, 0, W, first)
                 if not first:
                     u = 4 * g + t
@@ -167,7 +182,7 @@ def tile_list_meltab_gain_kernel(
             ]
             for t0 in range(0, 4, 2):
                 for w in range(2):
-                    bank = psum.tile([P, 2, cols], F32, name="bank")
+                    bank = next_bank([P, 2, cols])
                     for t in range(t0, t0 + 2):
                         for c in range(0, cols, P):
                             for a in range(PASSES):
@@ -197,23 +212,24 @@ def tile_list_meltab_gain_kernel(
             nc.vector.quantize_mx(out=h_q[:].bitcast(FP8X4), scales=h_sc[:], in_=h[:].rearrange("p c t -> p (c t)"))
             return h_q[:], h_sc[:]
 
-        def filters(fb_raw):
-            fb_b = keep.tile([P, GROUPS, N, 4], BF16, name="fb_b", align_bytes=64)
-            for g in range(GROUPS):
-                nc.vector.tensor_tensor(
-                    fb_b[:, g].rearrange("p (c i) t -> p c t i", i=2),
-                    fb_raw[:, g].rearrange("p t (c i) -> p c t i", i=2),
-                    sign[:, g, :].unsqueeze(1).unsqueeze(3).broadcast_to([P, N // 2, 4, 2]),
-                    ALU.mult,
-                )
-            fb_q = keep.tile([P, GROUPS, N], U32, name="fb_q", align_bytes=64)
-            fb_sc = keep.tile([P, GROUPS, N], U8, name="fb_sc", align_bytes=64)
+        fb_b = keep.tile([P, GROUPS, N, 4], BF16, name="fb_b", align_bytes=64)
+        fb_q = keep.tile([P, GROUPS, N], U32, name="fb_q", align_bytes=64)
+        fb_sc = keep.tile([P, GROUPS, N], U8, name="fb_sc", align_bytes=64)
+
+        def round_filters(g):
+            nc.vector.tensor_tensor(
+                fb_b[:, g].rearrange("p (c i) t -> p c t i", i=2),
+                fb_raw[:, g].rearrange("p t (c i) -> p c t i", i=2),
+                sign[:, g, :].unsqueeze(1).unsqueeze(3).broadcast_to([P, N // 2, 4, 2]),
+                ALU.mult,
+            )
+
+        def quantize_filters():
             nc.vector.quantize_mx(
                 out=fb_q[:].rearrange("p g n -> p (g n)").bitcast(FP8X4),
                 scales=fb_sc[:].rearrange("p g n -> p (g n)"),
                 in_=fb_b[:].rearrange("p g n t -> p (g n t)"),
             )
-            return fb_q, fb_sc
 
         def filter_bank(bank, nt, hs, fb_q, fb_sc):
             for g in range(GROUPS):
@@ -228,13 +244,13 @@ def tile_list_meltab_gain_kernel(
                 )
 
         def finish_wide(nt, hs, fb_q, fb_sc, picked, y):
-            bank = psum.tile([P, W], F32, name="bank")
+            bank = next_bank([P, W])
             filter_bank(bank[:], nt, hs, fb_q, fb_sc)
             nc.vector.tensor_tensor(y[:], bank[:], picked[:, 0:W], ALU.mult)
             nc.sync.dma_start(out[nt * P : (nt + 1) * P, 0:W], y[:])
 
         def finish_narrow(j0, cols, hs, fb_q, fb_sc, picked, y):
-            bank = psum.tile([P, N // P, cols], F32, name="bank")
+            bank = next_bank([P, N // P, cols])
             for nt in range(N // P):
                 filter_bank(bank[:, nt, :], nt, hs, fb_q, fb_sc)
             nc.vector.tensor_tensor(y[:], bank[:], picked[:, j0 : j0 + cols].unsqueeze(1).broadcast_to([P, N // P, cols]), ALU.mult)
@@ -243,54 +259,50 @@ def tile_list_meltab_gain_kernel(
         def cut(h, c0, c1):
             return h[0][:, c0:c1], h[1][:, c0:c1]
 
-        first_unit = [(t, 0, a) for a in range(PASSES) for t in range(2)]
-        first_unit += [(t, w, a) for w in range(2) for t in range(4) if w or t >= 2 for a in reversed(range(PASSES))]
+        first_unit = [(t, w, a) for w in range(2) for t in range(4) for a in range(PASSES)]
         by_tile = [(t, w, a) for t in range(4) for w in range(2) for a in range(PASSES)]
         H = W // 2
-        fb_raw = chain.tile([P, GROUPS, 4, N], F32, name="fb_raw", align_bytes=64, offset=16384)
-        fb_by_slot = fb.rearrange("(g q t r) n -> g t q r n", g=GROUPS, t=4, r=8)
-        for g in range(GROUPS):
-            for t in range(4):
-                nc.sync.dma_start(fb_raw[:, g, t, :], fb_by_slot[g, t])
-        pair0 = gather_words(0, chain.tile([P, W], I32, name="pair0", align_bytes=64, offset=40960))
+        Q = W // 4
+        pair0 = gather_words(0, chain.tile([P, W], I32, name="pair0", align_bytes=64, offset=22528))
         order_weight(0, 0, [0])
         part_words(0, pair0, [0])
         order_weight(0, 0, [1])
         part_words(0, pair0, [1])
         order_weight(1, 0, [0, 1])
-        pair1 = gather_words(1, chain.tile([P, W], I32, name="pair1", align_bytes=64, offset=30720))
-        load_weight(0, 1, 40960)
-        load_weight(1, 1, 25600)
-        sq00 = squares(0, 0, first_unit)
+        pair1 = gather_words(1, chain.tile([P, W], I32, name="pair1", align_bytes=64, offset=24576))
         part_words(1, pair1, [0, 1])
-        spread_level(0, chain.tile([P, W], F32, name="picked_row0", align_bytes=64, offset=30720))
-        sq10 = squares(1, 0, by_tile)
-        fb_q, fb_sc = filters(fb_raw)
+        sq00 = squares(0, 0, first_unit)
         order_weight(0, 1, [0, 1])
         order_weight(1, 1, [0, 1])
-        sum00 = power(sq00, 0, W, chain.tile([P, W, 4], BF16, name="h_first", align_bytes=64, offset=24576))
+        picked_row = chain.tile([P, J], F32, name="picked_row", align_bytes=64, offset=8192)
+        nc.vector.tensor_copy(picked_row[:], level[:].indirect(offsets[:]))
+        nc.sync.dma_start(out[0:1, :], picked_row[ROW : ROW + 1, :])
+        nc.sync.dma_start(picked_level[:], out[0, :].partition_broadcast(P))
         sq01 = squares(0, 1, by_tile)
-        spread_level(1, chain.tile([P, W], F32, name="picked_row1", align_bytes=64, offset=28672))
+        sum00 = power(sq00, 0, W, chain.tile([P, W, 4], BF16, name="h_first", align_bytes=64, offset=28672))
+        round_filters(0)
         h00 = quantize(sum00)
-        sum10 = power(sq10, 0, W)
-        h10 = quantize(sum10)
-        Q = W // 4
+        round_filters(1)
+        sq10 = squares(1, 0, by_tile)
+        sum01 = power(sq01, 0, W)
+        quantize_filters()
+        h01 = quantize(sum01)
         sq11a = narrow_squares(1, 1, 0, H)
         sq11b = narrow_squares(1, 1, H, Q)
+        finish_wide(0, [h00, h01], fb_q, fb_sc, picked_level, keep.tile([P, W], F32, name="y0", align_bytes=64))
+        finish_wide(1, [h00, h01], fb_q, fb_sc, picked_level, keep.tile([P, W], F32, name="y1", align_bytes=64))
+        sum10 = power(sq10, 0, W)
         sq11c = narrow_squares(1, 1, H + Q, Q)
-        sum01 = power(sq01, 0, W)
         sum11a = power(sq11a, 0, H)
-        h01 = quantize(sum01, tail.tile([P, W], U32, name="h_q01", align_bytes=64, offset=0))
+        h10 = quantize(sum10)
         h11a = quantize(sum11a)
         sum11b = power(sq11b, 0, Q)
-        finish_wide(0, [h00, h01], fb_q, fb_sc, picked_level, tail.tile([P, W], F32, name="y0", align_bytes=64, offset=8192))
-        h11b = quantize(sum11b)
-        sum11c = power(sq11c, 0, Q, tail.tile([P, Q, 4], BF16, name="h_last", align_bytes=64, offset=18432))
-        finish_wide(1, [h00, h01], fb_q, fb_sc, picked_level, tail.tile([P, W], F32, name="y1", align_bytes=64, offset=12288))
-        h11c = quantize(sum11c)
-        y_a = tail.tile([P, 2, H], F32, name="y_a", align_bytes=64, offset=18432 + 512 - 2048)
+        y_a = keep.tile([P, 2, H], F32, name="y_a", align_bytes=64)
         finish_narrow(W, H, [cut(h10, 0, H), h11a], fb_q, fb_sc, picked_level, y_a)
-        y_b = tail.tile([P, 2, Q], F32, name="y_b", align_bytes=64, offset=18432 + 512)
+        h11b = quantize(sum11b)
+        sum11c = power(sq11c, 0, Q)
+        y_b = keep.tile([P, 2, Q], F32, name="y_b", align_bytes=64)
         finish_narrow(W + H, Q, [cut(h10, H, H + Q), h11b], fb_q, fb_sc, picked_level, y_b)
+        h11c = quantize(sum11c)
         y_c = keep.tile([P, 2, Q], F32, name="y_c", align_bytes=64)
         finish_narrow(W + H + Q, Q, [cut(h10, H + Q, W), h11c], fb_q, fb_sc, picked_level, y_c)

@@ -22,7 +22,6 @@ W = 512
 HALVES = J // W
 GROUPS = F // 512
 PASSES = K // 512
-ROW = 127
 
 
 def tile_list_meltab_gain_kernel(
@@ -76,15 +75,12 @@ def tile_list_meltab_gain_kernel(
             nc.scalar.dma_start(
                 w_sc_raw[96:P, w * F : (w + 1) * F].bitcast(I32), w_scales[w].bitcast(I32).rearrange("a q f -> q a f")
             )
-        nc.scalar.dma_start(level[ROW : ROW + 1, :], ts[0:1, :])
 
         nc.vector.memset(tab_sc[0:96, :].bitcast(I32), 0)
         for jh in range(HALVES):
             nc.vector.memset(planes[jh][:].bitcast(I32), 0)
-        nc.gpsimd.memset(gn_rows[0 : P - 4], 0.0)
+        nc.vector.memset(gn_rows[0 : P - 4], 0.0)
         make_identity(nc, ident[:])
-        for c0 in range(0, T, W):
-            nc.gpsimd.memset(level[0:ROW, c0 : c0 + W], 0.0)
 
         def fill_planes(jh, x0, x1, queue):
             picked_sc = keep.tile([P, W], U8, name="picked_sc%d" % jh, align_bytes=64)
@@ -103,13 +99,14 @@ def tile_list_meltab_gain_kernel(
         fill_planes(0, 0, 1, nc.scalar)
         fill_planes(1, 1, 4, nc.sync)
         load_weight(1, 0, 0)
-        load_weight(0, 1, 4096)
-        load_weight(1, 1, 8192)
-        fb_raw = chain.tile([P, GROUPS, 4, N], F32, name="fb_raw", align_bytes=64, offset=12288)
+        fb_raw = [chain.tile([P, 4, N], F32, name="fb_raw%d" % g, align_bytes=64, offset=12288 + 4096 * g) for g in range(GROUPS)]
         fb_by_slot = fb.rearrange("(g q t r) n -> g t q r n", g=GROUPS, t=4, r=8)
         for g in range(GROUPS):
             for t in range(4):
-                nc.sync.dma_start(fb_raw[:, g, t, :], fb_by_slot[g, t])
+                nc.sync.dma_start(fb_raw[g][:, t, :], fb_by_slot[g, t])
+        load_weight(0, 1, 4096)
+        load_weight(1, 1, 8192)
+        nc.sync.dma_start(level[:], ts)
 
         gn_t = next_bank([P, GROUPS, P])
         for g in range(GROUPS):
@@ -219,7 +216,7 @@ def tile_list_meltab_gain_kernel(
         def round_filters(g):
             nc.vector.tensor_tensor(
                 fb_b[:, g].rearrange("p (c i) t -> p c t i", i=2),
-                fb_raw[:, g].rearrange("p t (c i) -> p c t i", i=2),
+                fb_raw[g][:].rearrange("p t (c i) -> p c t i", i=2),
                 sign[:, g, :].unsqueeze(1).unsqueeze(3).broadcast_to([P, N // 2, 4, 2]),
                 ALU.mult,
             )
@@ -272,37 +269,34 @@ def tile_list_meltab_gain_kernel(
         pair1 = gather_words(1, chain.tile([P, W], I32, name="pair1", align_bytes=64, offset=24576))
         part_words(1, pair1, [0, 1])
         sq00 = squares(0, 0, first_unit)
+        sq10 = squares(1, 0, by_tile)
+        round_filters(0)
+        round_filters(1)
+        quantize_filters()
         order_weight(0, 1, [0, 1])
         order_weight(1, 1, [0, 1])
-        picked_row = chain.tile([P, J], F32, name="picked_row", align_bytes=64, offset=8192)
-        nc.vector.tensor_copy(picked_row[:], level[:].indirect(offsets[:]))
-        nc.sync.dma_start(out[0:1, :], picked_row[ROW : ROW + 1, :])
-        nc.sync.dma_start(picked_level[:], out[0, :].partition_broadcast(P))
+        sum00 = power(sq00, 0, W, chain.tile([P, W, 4], BF16, name="h_first", align_bytes=64, offset=6144))
         sq01 = squares(0, 1, by_tile)
-        sum00 = power(sq00, 0, W, chain.tile([P, W, 4], BF16, name="h_first", align_bytes=64, offset=28672))
-        round_filters(0)
         h00 = quantize(sum00)
-        round_filters(1)
-        sq10 = squares(1, 0, by_tile)
-        sum01 = power(sq01, 0, W)
-        quantize_filters()
-        h01 = quantize(sum01)
+        sum10 = power(sq10, 0, W, chain.tile([P, W, 4], BF16, name="h_second", align_bytes=64, offset=10240))
+        h10 = quantize(sum10)
+        nc.vector.tensor_copy(picked_level[:], level[:].indirect(offsets[:]))
         sq11a = narrow_squares(1, 1, 0, H)
         sq11b = narrow_squares(1, 1, H, Q)
-        finish_wide(0, [h00, h01], fb_q, fb_sc, picked_level, keep.tile([P, W], F32, name="y0", align_bytes=64))
-        finish_wide(1, [h00, h01], fb_q, fb_sc, picked_level, keep.tile([P, W], F32, name="y1", align_bytes=64))
-        sum10 = power(sq10, 0, W)
         sq11c = narrow_squares(1, 1, H + Q, Q)
-        sum11a = power(sq11a, 0, H)
-        h10 = quantize(sum10)
+        sum01 = power(sq01, 0, W, chain.tile([P, W, 4], BF16, name="h_third", align_bytes=64, offset=28672))
+        sum11a = power(sq11a, 0, H, chain.tile([P, H, 4], BF16, name="h_a", align_bytes=64, offset=32768))
+        h01 = quantize(sum01)
         h11a = quantize(sum11a)
-        sum11b = power(sq11b, 0, Q)
+        sum11b = power(sq11b, 0, Q, chain.tile([P, Q, 4], BF16, name="h_b", align_bytes=64, offset=34816))
+        finish_wide(0, [h00, h01], fb_q, fb_sc, picked_level, keep.tile([P, W], F32, name="y0", align_bytes=64))
+        h11b = quantize(sum11b)
+        sum11c = power(sq11c, 0, Q, chain.tile([P, Q, 4], BF16, name="h_c", align_bytes=64, offset=35840))
+        finish_wide(1, [h00, h01], fb_q, fb_sc, picked_level, keep.tile([P, W], F32, name="y1", align_bytes=64))
+        h11c = quantize(sum11c)
         y_a = keep.tile([P, 2, H], F32, name="y_a", align_bytes=64)
         finish_narrow(W, H, [cut(h10, 0, H), h11a], fb_q, fb_sc, picked_level, y_a)
-        h11b = quantize(sum11b)
-        sum11c = power(sq11c, 0, Q)
         y_b = keep.tile([P, 2, Q], F32, name="y_b", align_bytes=64)
         finish_narrow(W + H, Q, [cut(h10, H, H + Q), h11b], fb_q, fb_sc, picked_level, y_b)
-        h11c = quantize(sum11c)
         y_c = keep.tile([P, 2, Q], F32, name="y_c", align_bytes=64)
         finish_narrow(W + H + Q, Q, [cut(h10, H + Q, W), h11c], fb_q, fb_sc, picked_level, y_c)

@@ -122,6 +122,9 @@ def tile_list_meltab_gain_kernel(
 
         picked_level = keep.tile([P, J], F32, name="picked_level")
 
+        def gather_level(jh):
+            nc.vector.tensor_copy(picked_level[:, jh * W : (jh + 1) * W], level[:].indirect(offsets[:, 32 * jh : 32 * jh + 32]))
+
 
         def gather_words(jh, pair):
             nc.vector.tensor_copy(pair[:].bitcast(U32), tab[:].bitcast(U32).indirect(offsets[:, 32 * jh : 32 * jh + 32]))
@@ -256,6 +259,21 @@ def tile_list_meltab_gain_kernel(
         def cut(h, c0, c1):
             return h[0][:, c0:c1], h[1][:, c0:c1]
 
+        zeros = keep.tile([P, P, 4], BF16, name="zeros", align_bytes=64)
+        nc.vector.memset(zeros[:].rearrange("p c t -> p (c t)").bitcast(I32), 0)
+        zero_q, zero_sc = quantize(zeros)
+        warm = next_bank([P, W])
+        for i in range(3):
+            nc.tensor.matmul_mx(
+                out=warm[:],
+                lhsT=zero_q.bitcast(FP8X4),
+                lhsT_scale=zero_sc,
+                rhs=tab[:, 0 : W // 2].bitcast(U8).bitcast(FP4X4),
+                rhs_scale=tab_sc[:, 0:W],
+                start=True,
+                stop=True,
+            )
+
         first_unit = [(t, w, a) for w in range(2) for t in range(4) for a in range(PASSES)]
         by_tile = [(t, w, a) for t in range(4) for w in range(2) for a in range(PASSES)]
         H = W // 2
@@ -280,7 +298,8 @@ def tile_list_meltab_gain_kernel(
         h00 = quantize(sum00)
         sum10 = power(sq10, 0, W, chain.tile([P, W, 4], BF16, name="h_second", align_bytes=64, offset=10240))
         h10 = quantize(sum10)
-        nc.vector.tensor_copy(picked_level[:], level[:].indirect(offsets[:]))
+        gather_level(0)
+        gather_level(1)
         sq11a = narrow_squares(1, 1, 0, H)
         sq11b = narrow_squares(1, 1, H, Q)
         sq11c = narrow_squares(1, 1, H + Q, Q)

@@ -42,7 +42,7 @@ def tile_list_meltab_gain_kernel(
         tab = keep.tile([P, T], I32, name="tab", align_bytes=64)
         tab_sc = keep.tile([P, T], U8, name="tab_sc", align_bytes=64)
         w_sc_raw = keep.tile([P, 4 * W], U8, name="w_sc_raw", align_bytes=64)
-        widths = (2 * W, 4 * W)
+        widths = (3 * W, 3 * W)
         joined = [keep.tile([P, widths[jh]], U8, name="joined%d" % jh, align_bytes=64) for jh in range(HALVES)]
         planes = [keep.tile([P, PASSES, widths[jh]], U8, name="planes%d" % jh, align_bytes=64) for jh in range(HALVES)]
         gn_rows = keep.tile([P, GROUPS, P], F32, name="gn_rows")
@@ -82,28 +82,36 @@ def tile_list_meltab_gain_kernel(
         nc.vector.memset(gn_rows[0 : P - 4], 0.0)
         make_identity(nc, ident[:])
 
-        def fill_planes(jh, x0, x1, queue):
-            picked_sc = keep.tile([P, W], U8, name="picked_sc%d" % jh, align_bytes=64)
+        def join_scales(jh):
+            picked_sc = chain.tile([P, W], U8, name="picked_sc%d" % jh, align_bytes=64, offset=20480)
             nc.vector.tensor_copy(picked_sc[:], tab_sc[:].indirect(offsets[:, 32 * jh : 32 * jh + 32]))
             nc.vector.tensor_copy(
-                joined[jh][96:P, W:].bitcast(I32).rearrange("p (x t q e) -> p t x q e", t=4, q=16, e=2),
-                w_sc_raw[96:P, x0 * W : x1 * W].bitcast(I32).rearrange("p (x q t e) -> p t x q e", t=4, q=16, e=2),
+                joined[jh][96:P, W:].bitcast(I32).rearrange("p (w t q e) -> p t w q e", t=4, q=16, e=2),
+                w_sc_raw[96:P, :].bitcast(I32).rearrange("p (w g q t e) -> p g t w q e", g=GROUPS, t=4, q=16, e=2)[:, jh],
             )
             nc.vector.tensor_copy(joined[jh][96:P, 0:W].bitcast(I32), picked_sc[96:P, :].bitcast(I32))
+
+        def fill_planes(jh, queue):
             for quad in range(4):
                 queue.dma_start(
                     planes[jh][32 * quad : 32 * quad + 4].bitcast(I32),
                     joined[jh][96 + 8 * quad : 96 + 8 * quad + 8, :].bitcast(I32),
                 )
 
-        fill_planes(0, 0, 1, nc.scalar)
-        fill_planes(1, 1, 4, nc.sync)
-        load_weight(1, 0, 0)
         fb_raw = [chain.tile([P, 4, N], F32, name="fb_raw%d" % g, align_bytes=64, offset=12288 + 4096 * g) for g in range(GROUPS)]
         fb_by_slot = fb.rearrange("(g q t r) n -> g t q r n", g=GROUPS, t=4, r=8)
-        for g in range(GROUPS):
+
+        def load_filters(g):
             for t in range(4):
                 nc.sync.dma_start(fb_raw[g][:, t, :], fb_by_slot[g, t])
+
+        join_scales(0)
+        fill_planes(0, nc.scalar)
+        join_scales(1)
+        load_weight(1, 0, 0)
+        load_filters(0)
+        fill_planes(1, nc.sync)
+        load_filters(1)
         load_weight(0, 1, 4096)
         load_weight(1, 1, 8192)
         nc.sync.dma_start(level[:], ts)
@@ -121,9 +129,6 @@ def tile_list_meltab_gain_kernel(
         nc.scalar.activation(root[:], gn_abs[:].rearrange("p g t -> p (g t)"), ACT.Sqrt)
 
         picked_level = keep.tile([P, J], F32, name="picked_level")
-
-        def gather_level(jh):
-            nc.vector.tensor_copy(picked_level[:, jh * W : (jh + 1) * W], level[:].indirect(offsets[:, 32 * jh : 32 * jh + 32]))
 
 
         def gather_words(jh, pair):
@@ -150,12 +155,11 @@ def tile_list_meltab_gain_kernel(
                 w_q[w, g, a] = tile[:, i]
 
         def product(bank, jh, g, t, w, a, c0, cols, first):
-            x = 2 * w + g
-            f0 = max(x, 1) * W + t * P
+            f0 = (1 + w) * W + t * P
             nc.tensor.matmul_mx(
                 out=bank,
                 lhsT=w_q[w, g, a][:, t, :].bitcast(FP8X4),
-                lhsT_scale=planes[min(x, 1)][:, a, f0 : f0 + P],
+                lhsT_scale=planes[g][:, a, f0 : f0 + P],
                 rhs=v[jh, a][:, 2 * c0 : 2 * (c0 + cols)].bitcast(FP4X4),
                 rhs_scale=planes[jh][:, a, c0 : c0 + cols],
                 start=first,
@@ -263,7 +267,7 @@ def tile_list_meltab_gain_kernel(
         nc.vector.memset(zeros[:].rearrange("p c t -> p (c t)").bitcast(I32), 0)
         zero_q, zero_sc = quantize(zeros)
         warm = next_bank([P, W])
-        for i in range(3):
+        for i in range(4):
             nc.tensor.matmul_mx(
                 out=warm[:],
                 lhsT=zero_q.bitcast(FP8X4),
@@ -277,29 +281,28 @@ def tile_list_meltab_gain_kernel(
         first_unit = [(t, w, a) for w in range(2) for t in range(4) for a in range(PASSES)]
         by_tile = [(t, w, a) for t in range(4) for w in range(2) for a in range(PASSES)]
         H = W // 2
-        Q = W // 4
         pair0 = gather_words(0, chain.tile([P, W], I32, name="pair0", align_bytes=64, offset=22528))
         order_weight(0, 0, [0])
         part_words(0, pair0, [0])
         order_weight(0, 0, [1])
         part_words(0, pair0, [1])
         order_weight(1, 0, [0, 1])
-        pair1 = gather_words(1, chain.tile([P, W], I32, name="pair1", align_bytes=64, offset=24576))
+        pair1 = gather_words(1, chain.tile([P, W], I32, name="pair1", align_bytes=64, offset=0))
         part_words(1, pair1, [0, 1])
+        Q = W // 4
         sq00 = squares(0, 0, first_unit)
         sq10 = squares(1, 0, by_tile)
         round_filters(0)
         round_filters(1)
-        quantize_filters()
         order_weight(0, 1, [0, 1])
+        sum00 = power(sq00, 0, W, chain.tile([P, W, 4], BF16, name="h_first", align_bytes=64, offset=4096))
+        quantize_filters()
         order_weight(1, 1, [0, 1])
-        sum00 = power(sq00, 0, W, chain.tile([P, W, 4], BF16, name="h_first", align_bytes=64, offset=6144))
-        sq01 = squares(0, 1, by_tile)
-        h00 = quantize(sum00)
+        sq01 = squares(0, 1, first_unit)
+        h00 = quantize(sum00, chain.tile([P, W], U32, name="h_q_first", align_bytes=64, offset=8192))
         sum10 = power(sq10, 0, W, chain.tile([P, W, 4], BF16, name="h_second", align_bytes=64, offset=10240))
-        h10 = quantize(sum10)
-        gather_level(0)
-        gather_level(1)
+        nc.vector.tensor_copy(picked_level[:], level[:].indirect(offsets[:]))
+        h10 = quantize(sum10, chain.tile([P, W], U32, name="h_q_second", align_bytes=64, offset=36864))
         sq11a = narrow_squares(1, 1, 0, H)
         sq11b = narrow_squares(1, 1, H, Q)
         sq11c = narrow_squares(1, 1, H + Q, Q)

@@ -69,7 +69,6 @@ def tile_list_meltab_gain_kernel(
             gn_rows[P - 4 : P].rearrange("t g (q r) -> t (g q) r", r=8), gn.rearrange("(x t r) -> t x r", t=4, r=8)
         )
         nc.sync.dma_start(tab[:], tab_words.rearrange("e p t b -> p (e t b)").bitcast(I32))
-        load_weight(0, 0, 24576)
 
         for w in range(2):
             nc.scalar.dma_start(
@@ -106,7 +105,8 @@ def tile_list_meltab_gain_kernel(
                 nc.sync.dma_start(fb_raw[g][:, t, :], fb_by_slot[g, t])
 
         join_scales(0)
-        fill_planes(0, nc.scalar)
+        fill_planes(0, nc.sync)
+        load_weight(0, 0, 24576)
         join_scales(1)
         load_weight(1, 0, 0)
         load_filters(0)

@@ -76,13 +76,20 @@ def tile_list_meltab_gain_kernel(
             )
 
         nc.vector.memset(tab_sc[0:96, :].bitcast(I32), 0)
-        for jh in range(HALVES):
-            nc.vector.memset(planes[jh][:].bitcast(I32), 0)
         nc.vector.memset(gn_rows[0 : P - 4], 0.0)
+        zeros = keep.tile([P, P, 4], BF16, name="zeros", align_bytes=64)
+        nc.vector.memset(zeros[:].rearrange("p c t -> p (c t)").bitcast(I32), 0)
         make_identity(nc, ident[:])
+        for jh in range(HALVES):
+            nc.gpsimd.memset(planes[jh][:].bitcast(I32), 0)
+        zero_q = keep.tile([P, P], U32, name="zero_q", align_bytes=64)
+        zero_sc = keep.tile([P, P], U8, name="zero_sc", align_bytes=64)
+        nc.vector.quantize_mx(out=zero_q[:].bitcast(FP8X4), scales=zero_sc[:], in_=zeros[:].rearrange("p c t -> p (c t)"))
+        picked_scales = {}
 
         def join_scales(jh):
             picked_sc = chain.tile([P, W], U8, name="picked_sc%d" % jh, align_bytes=64, offset=20480)
+            picked_scales[jh] = picked_sc
             nc.vector.tensor_copy(picked_sc[:], tab_sc[:].indirect(offsets[:, 32 * jh : 32 * jh + 32]))
             nc.vector.tensor_copy(
                 joined[jh][96:P, W:].bitcast(I32).rearrange("p (w t q e) -> p t w q e", t=4, q=16, e=2),
@@ -119,13 +126,11 @@ def tile_list_meltab_gain_kernel(
         gn_t = next_bank([P, GROUPS, P])
         for g in range(GROUPS):
             nc.tensor.transpose(gn_t[:, g, :], gn_rows[:, g, :], ident[:])
-        two_pos = keep.tile([P, GROUPS, 4], F32, name="two_pos")
         sign = keep.tile([P, GROUPS, 4], F32, name="sign")
         gn_abs = keep.tile([P, GROUPS, 4], F32, name="gn_abs")
         root = keep.tile([P, 8], F32, name="root")
-        nc.vector.tensor_scalar(two_pos[:], gn_t[:, :, P - 4 : P], 0.0, 2.0, ALU.is_ge, ALU.mult)
-        nc.vector.tensor_scalar_add(sign[:], two_pos[:], -1.0)
-        nc.vector.tensor_tensor(gn_abs[:], gn_t[:, :, P - 4 : P], sign[:], ALU.mult)
+        nc.scalar.activation(gn_abs[:], gn_t[:, :, P - 4 : P], ACT.Abs)
+        nc.scalar.activation(sign[:], gn_t[:, :, P - 4 : P], ACT.Sign)
         nc.scalar.activation(root[:], gn_abs[:].rearrange("p g t -> p (g t)"), ACT.Sqrt)
 
         picked_level = keep.tile([P, J], F32, name="picked_level")
@@ -263,17 +268,14 @@ def tile_list_meltab_gain_kernel(
         def cut(h, c0, c1):
             return h[0][:, c0:c1], h[1][:, c0:c1]
 
-        zeros = keep.tile([P, P, 4], BF16, name="zeros", align_bytes=64)
-        nc.vector.memset(zeros[:].rearrange("p c t -> p (c t)").bitcast(I32), 0)
-        zero_q, zero_sc = quantize(zeros)
-        warm = next_bank([P, W])
+        warm = psum.tile([P, W], F32, name="bank1")
         for i in range(4):
             nc.tensor.matmul_mx(
                 out=warm[:],
-                lhsT=zero_q.bitcast(FP8X4),
-                lhsT_scale=zero_sc,
-                rhs=tab[:, 0 : W // 2].bitcast(U8).bitcast(FP4X4),
-                rhs_scale=tab_sc[:, 0:W],
+                lhsT=zero_q[:].bitcast(FP8X4),
+                lhsT_scale=zero_sc[:],
+                rhs=tab_sc[:, 0 : 2 * W].bitcast(FP4X4),
+                rhs_scale=picked_scales[1][:],
                 start=True,
                 stop=True,
             )

@@ -172,7 +172,7 @@ def tile_list_meltab_gain_kernel(
             )
 
         def squares(jh, g, order):
-            sq = [ring.tile([P, 4, W], F32, name="sq%d" % w, align_bytes=64, bufs=3) for w in range(2)]
+            sq = [ring.tile([P, 4, W], F32, name="sq%d" % w, align_bytes=64, bufs=2) for w in range(2)]
             banks = {}
             for t, w, a in order:
                 first = (t, w) not in banks
@@ -186,7 +186,7 @@ def tile_list_meltab_gain_kernel(
 
         def narrow_squares(jh, g, c0, cols):
             sq = [
-                tail.tile([P, 4, cols], F32, name="sq%d_%d" % (w, c0), align_bytes=64, offset=16 * (2 * c0 + w * cols))
+                tail.tile([P, 4, cols], F32, name="sq%d_%d_%d" % (w, jh, c0), align_bytes=64, offset=16 * (2 * (jh * W + c0) + w * cols))
                 for w in range(2)
             ]
             for t0 in range(0, 4, 2):
@@ -213,11 +213,12 @@ def tile_list_meltab_gain_kernel(
             )
             return h
 
-        def quantize(h, h_q=None):
+        def quantize(h, h_q=None, h_sc=None):
             cols = h.shape[1]
             if h_q is None:
                 h_q = ring.tile([P, cols], U32, name="h_q", align_bytes=64, bufs=6)
-            h_sc = ring.tile([P, cols], U8, name="h_sc", align_bytes=64, bufs=6)
+            if h_sc is None:
+                h_sc = ring.tile([P, cols], U8, name="h_sc", align_bytes=64, bufs=6)
             nc.vector.quantize_mx(out=h_q[:].bitcast(FP8X4), scales=h_sc[:], in_=h[:].rearrange("p c t -> p (c t)"))
             return h_q[:], h_sc[:]
 
@@ -300,17 +301,21 @@ def tile_list_meltab_gain_kernel(
         sum00 = power(sq00, 0, W, chain.tile([P, W, 4], BF16, name="h_first", align_bytes=64, offset=4096))
         quantize_filters()
         order_weight(1, 1, [0, 1])
-        sq01 = squares(0, 1, first_unit)
+        sq01a = narrow_squares(0, 1, 0, H)
+        sq01b = narrow_squares(0, 1, H, H)
         h00 = quantize(sum00, chain.tile([P, W], U32, name="h_q_first", align_bytes=64, offset=8192))
         sum10 = power(sq10, 0, W, chain.tile([P, W, 4], BF16, name="h_second", align_bytes=64, offset=10240))
         nc.vector.tensor_copy(picked_level[:], level[:].indirect(offsets[:]))
+        sum01a = power(sq01a, 0, H, chain.tile([P, H, 4], BF16, name="h_third_a", align_bytes=64, offset=28672))
         h10 = quantize(sum10, chain.tile([P, W], U32, name="h_q_second", align_bytes=64, offset=36864))
+        h01 = (keep.tile([P, W], U32, name="h01_q", align_bytes=64)[:], keep.tile([P, W], U8, name="h01_sc", align_bytes=64)[:])
+        quantize(sum01a, *cut(h01, 0, H))
         sq11a = narrow_squares(1, 1, 0, H)
         sq11b = narrow_squares(1, 1, H, Q)
         sq11c = narrow_squares(1, 1, H + Q, Q)
-        sum01 = power(sq01, 0, W, chain.tile([P, W, 4], BF16, name="h_third", align_bytes=64, offset=28672))
+        sum01b = power(sq01b, 0, H, chain.tile([P, H, 4], BF16, name="h_third_b", align_bytes=64, offset=30720))
         sum11a = power(sq11a, 0, H, chain.tile([P, H, 4], BF16, name="h_a", align_bytes=64, offset=32768))
-        h01 = quantize(sum01)
+        quantize(sum01b, *cut(h01, H, W))
         h11a = quantize(sum11a)
         sum11b = power(sq11b, 0, Q, chain.tile([P, Q, 4], BF16, name="h_b", align_bytes=64, offset=34816))
         finish_wide(0, [h00, h01], fb_q, fb_sc, picked_level, keep.tile([P, W], F32, name="y0", align_bytes=64))

@@ -292,7 +292,6 @@ def tile_list_meltab_gain_kernel(
         order_weight(1, 0, [0, 1])
         pair1 = gather_words(1, chain.tile([P, W], I32, name="pair1", align_bytes=64, offset=0))
         part_words(1, pair1, [0, 1])
-        Q = W // 4
         sq00 = squares(0, 0, first_unit)
         sq10 = squares(1, 0, by_tile)
         round_filters(0)
@@ -311,21 +310,16 @@ def tile_list_meltab_gain_kernel(
         h01 = (keep.tile([P, W], U32, name="h01_q", align_bytes=64)[:], keep.tile([P, W], U8, name="h01_sc", align_bytes=64)[:])
         quantize(sum01a, *cut(h01, 0, H))
         sq11a = narrow_squares(1, 1, 0, H)
-        sq11b = narrow_squares(1, 1, H, Q)
-        sq11c = narrow_squares(1, 1, H + Q, Q)
+        sq11b = narrow_squares(1, 1, H, H)
         sum01b = power(sq01b, 0, H, chain.tile([P, H, 4], BF16, name="h_third_b", align_bytes=64, offset=30720))
         sum11a = power(sq11a, 0, H, chain.tile([P, H, 4], BF16, name="h_a", align_bytes=64, offset=32768))
         quantize(sum01b, *cut(h01, H, W))
         h11a = quantize(sum11a)
-        sum11b = power(sq11b, 0, Q, chain.tile([P, Q, 4], BF16, name="h_b", align_bytes=64, offset=34816))
+        sum11b = power(sq11b, 0, H, chain.tile([P, H, 4], BF16, name="h_b", align_bytes=64, offset=34816))
         finish_wide(0, [h00, h01], fb_q, fb_sc, picked_level, keep.tile([P, W], F32, name="y0", align_bytes=64))
         h11b = quantize(sum11b)
-        sum11c = power(sq11c, 0, Q, chain.tile([P, Q, 4], BF16, name="h_c", align_bytes=64, offset=35840))
         finish_wide(1, [h00, h01], fb_q, fb_sc, picked_level, keep.tile([P, W], F32, name="y1", align_bytes=64))
-        h11c = quantize(sum11c)
         y_a = keep.tile([P, 2, H], F32, name="y_a", align_bytes=64)
         finish_narrow(W, H, [cut(h10, 0, H), h11a], fb_q, fb_sc, picked_level, y_a)
-        y_b = keep.tile([P, 2, Q], F32, name="y_b", align_bytes=64)
-        finish_narrow(W + H, Q, [cut(h10, H, H + Q), h11b], fb_q, fb_sc, picked_level, y_b)
-        y_c = keep.tile([P, 2, Q], F32, name="y_c", align_bytes=64)
-        finish_narrow(W + H + Q, Q, [cut(h10, H + Q, W), h11c], fb_q, fb_sc, picked_level, y_c)
+        y_b = keep.tile([P, 2, H], F32, name="y_b", align_bytes=64)
+        finish_narrow(W + H, H, [cut(h10, H, W), h11b], fb_q, fb_sc, picked_level, y_b)

@@ -19,9 +19,11 @@ ACT = mybir.ActivationFunctionType
 
 P = 128
 W = 512
+Q = 256
 HALVES = J // W
 GROUPS = F // 512
 PASSES = K // 512
+SLOTS = 4
 
 
 def tile_list_meltab_gain_kernel(
@@ -33,204 +35,217 @@ def tile_list_meltab_gain_kernel(
 
     with ExitStack() as ctx:
         keep = ctx.enter_context(tc.tile_pool(name="keep", bufs=1))
-        ring = ctx.enter_context(tc.tile_pool(name="ring", bufs=4))
-        chain = ctx.enter_context(tc.tile_pool(name="chain", bufs=1))
-        tail = ctx.enter_context(tc.tile_pool(name="tail", bufs=1))
+        ring = ctx.enter_context(tc.tile_pool(name="ring", bufs=3))
+        shared = ctx.enter_context(tc.tile_pool(name="shared", bufs=1))
         psum = ctx.enter_context(tc.psum_pool(name="psum", bufs=1))
 
         offsets = keep.tile([P, J // 16], U16, name="offsets")
-        tab = keep.tile([P, T], I32, name="tab", align_bytes=64)
+        tab = shared.tile([P, T], I32, name="tab", align_bytes=64, offset=23 * 4096)
         tab_sc = keep.tile([P, T], U8, name="tab_sc", align_bytes=64)
-        w_sc_raw = keep.tile([P, 4 * W], U8, name="w_sc_raw", align_bytes=64)
-        widths = (3 * W, 3 * W)
-        joined = [keep.tile([P, widths[jh]], U8, name="joined%d" % jh, align_bytes=64) for jh in range(HALVES)]
-        planes = [keep.tile([P, PASSES, widths[jh]], U8, name="planes%d" % jh, align_bytes=64) for jh in range(HALVES)]
-        gn_rows = keep.tile([P, GROUPS, P], F32, name="gn_rows")
+        w_sc_raw = keep.tile([P, 2 * F], U8, name="w_sc_raw", align_bytes=64)
+        joined = [shared.tile([P, 3 * W], U8, name="joined%d" % s, align_bytes=64, offset=5 * 4096 - W + 4096 * 4 * s) for s in range(2)]
+        planes = [keep.tile([P, PASSES, 3 * W], U8, name="planes%d" % s, align_bytes=64) for s in range(2)]
+        gain = shared.tile([P, GROUPS, SLOTS], F32, name="gain", align_bytes=64, offset=2048 + 128)
+        level = shared.tile([P, T], F32, name="level", align_bytes=64, offset=27 * 4096)
+        level_blocks = keep.tile([P, P], F32, name="level_blocks", align_bytes=64)
+        level_cols = [
+            shared.tile([P, 24], F32, name="level_cols0", align_bytes=64, offset=18 * 4096 - 64),
+            keep.tile([P, 8], F32, name="level_cols1", align_bytes=64),
+        ]
         ident = keep.tile([P, P], F32, name="ident")
-        level = chain.tile([P, T], F32, name="level", align_bytes=64, offset=28672)
+        fb_raw = shared.tile([P, GROUPS, SLOTS, N], F32, name="fb_raw", align_bytes=64, offset=23 * 4096)
+
         turns = []
 
-        def next_bank(shape):
-            turns.append(shape)
+        def next_bank(shape, skip=0):
+            turns.extend([shape] * (1 + skip))
             return psum.tile(shape, F32, name="bank%d" % (len(turns) % 8))
 
         w_raw = {}
-        w_q = {}
 
-        def load_weight(w, g, offset):
-            raw = chain.tile([P, PASSES, W], I32, name="w_raw%d%d" % (w, g), align_bytes=64, offset=offset)
-            w_raw[w, g] = raw
+        def load_weight(w, g, passes, offset):
+            raw = shared.tile([P, len(passes), W], I32, name="w_raw%d%d%d" % (w, g, passes[0]), align_bytes=64, offset=offset)
             words = w_words[w].rearrange("a p f b -> p a (f b)").bitcast(I32)
-            nc.sync.dma_start(raw[:], words[:, :, g * W : (g + 1) * W])
+            nc.sync.dma_start(raw[:], words[:, passes[0] : passes[-1] + 1, g * W : (g + 1) * W])
+            w_raw[w, g, passes[0]] = raw
 
+        nc.sync.dma_start(gain[:], gn.rearrange("(g p t) -> p g t", g=GROUPS, t=SLOTS))
         nc.sync.dma_start(tab_sc[96:P, :].bitcast(I32), tab_scales.bitcast(I32).rearrange("a q t -> q a t"))
         nc.sync.dma_start(offsets[:], offs)
-        nc.sync.dma_start(
-            gn_rows[P - 4 : P].rearrange("t g (q r) -> t (g q) r", r=8), gn.rearrange("(x t r) -> t x r", t=4, r=8)
-        )
+        nc.sync.dma_start(level_blocks[96:P, :], ts[0].rearrange("(m k) -> m k", k=P))
         nc.sync.dma_start(tab[:], tab_words.rearrange("e p t b -> p (e t b)").bitcast(I32))
-
         for w in range(2):
             nc.scalar.dma_start(
                 w_sc_raw[96:P, w * F : (w + 1) * F].bitcast(I32), w_scales[w].bitcast(I32).rearrange("a q f -> q a f")
             )
+        load_weight(0, 0, [0, 1], 11 * 4096)
 
         nc.vector.memset(tab_sc[0:96, :].bitcast(I32), 0)
-        nc.vector.memset(gn_rows[0 : P - 4], 0.0)
-        zeros = keep.tile([P, P, 4], BF16, name="zeros", align_bytes=64)
-        nc.vector.memset(zeros[:].rearrange("p c t -> p (c t)").bitcast(I32), 0)
-        make_identity(nc, ident[:])
-        for jh in range(HALVES):
-            nc.gpsimd.memset(planes[jh][:].bitcast(I32), 0)
+        nc.vector.memset(w_sc_raw[0:96, :].bitcast(I32), 0)
+        zeros = keep.tile([P, W], BF16, name="zeros", align_bytes=64)
         zero_q = keep.tile([P, P], U32, name="zero_q", align_bytes=64)
         zero_sc = keep.tile([P, P], U8, name="zero_sc", align_bytes=64)
-        nc.vector.quantize_mx(out=zero_q[:].bitcast(FP8X4), scales=zero_sc[:], in_=zeros[:].rearrange("p c t -> p (c t)"))
-        picked_scales = {}
+        nc.vector.memset(zeros[:].bitcast(I32), 0)
+        nc.vector.quantize_mx(out=zero_q[:].bitcast(FP8X4), scales=zero_sc[:], in_=zeros[:])
+        nc.gpsimd.memset(level_blocks[0:96, :], 0.0)
+        make_identity(nc, ident[:])
+        for s in range(2):
+            nc.gpsimd.memset(planes[s][:].bitcast(I32), 0)
 
-        def join_scales(jh):
-            picked_sc = chain.tile([P, W], U8, name="picked_sc%d" % jh, align_bytes=64, offset=20480)
-            picked_scales[jh] = picked_sc
-            nc.vector.tensor_copy(picked_sc[:], tab_sc[:].indirect(offsets[:, 32 * jh : 32 * jh + 32]))
+        def join_scales(s):
+            picked_sc = shared.tile([P, (2 - s) * W], U8, name="picked_sc%d" % s, align_bytes=64, offset=2048 - 64 + 64 * s)
+            nc.vector.tensor_copy(picked_sc[:, 0:W], tab_sc[:].indirect(offsets[:, 32 * s : 32 * s + 32]))
             nc.vector.tensor_copy(
-                joined[jh][96:P, W:].bitcast(I32).rearrange("p (w t q e) -> p t w q e", t=4, q=16, e=2),
-                w_sc_raw[96:P, :].bitcast(I32).rearrange("p (w g q t e) -> p g t w q e", g=GROUPS, t=4, q=16, e=2)[:, jh],
+                joined[s][:, W:].rearrange("p (w t m) -> p w t m", w=2, t=SLOTS),
+                w_sc_raw[:].rearrange("p (w g m t) -> p g w t m", w=2, g=GROUPS, t=SLOTS)[:, s],
             )
-            nc.vector.tensor_copy(joined[jh][96:P, 0:W].bitcast(I32), picked_sc[96:P, :].bitcast(I32))
+            nc.vector.tensor_copy(joined[s][96:P, 0:W].bitcast(I32), picked_sc[96:P, 0:W].bitcast(I32))
 
-        def fill_planes(jh, queue):
+        def fill_planes(s, queue):
             for quad in range(4):
                 queue.dma_start(
-                    planes[jh][32 * quad : 32 * quad + 4].bitcast(I32),
-                    joined[jh][96 + 8 * quad : 96 + 8 * quad + 8, :].bitcast(I32),
+                    planes[s][32 * quad : 32 * quad + 4].bitcast(I32),
+                    joined[s][96 + 8 * quad : 96 + 8 * quad + 8, :].bitcast(I32),
                 )
 
-        fb_raw = [chain.tile([P, 4, N], F32, name="fb_raw%d" % g, align_bytes=64, offset=12288 + 4096 * g) for g in range(GROUPS)]
-        fb_by_slot = fb.rearrange("(g q t r) n -> g t q r n", g=GROUPS, t=4, r=8)
-
-        def load_filters(g):
-            for t in range(4):
-                nc.sync.dma_start(fb_raw[g][:, t, :], fb_by_slot[g, t])
-
+        gn_abs = shared.tile([P, GROUPS, SLOTS], F32, name="gn_abs", align_bytes=64, offset=18 * 4096 - 64)
+        root = keep.tile([P, GROUPS, SLOTS], F32, name="root")
+        nc.vector.scalar_tensor_tensor(gn_abs[:], gain[:], -1.0, gain[:], ALU.mult, ALU.max)
+        is_pos = keep.tile([P, GROUPS, SLOTS], F32, name="is_pos")
+        nc.vector.tensor_scalar(is_pos[:], gain[:], 0.0, 2.0, ALU.is_ge, ALU.mult)
+        nc.scalar.activation(root[:], gn_abs[:], ACT.Sqrt)
         join_scales(0)
         fill_planes(0, nc.sync)
-        load_weight(0, 0, 24576)
+        load_weight(1, 0, [0, 1], 2048 + 2 * W - 128)
+
+        sign = keep.tile([P, GROUPS, SLOTS], F32, name="sign")
+        nc.gpsimd.tensor_scalar(sign[:], is_pos[:], 1.0, -1.0, ALU.mult, ALU.add)
         join_scales(1)
-        load_weight(1, 0, 0)
-        load_filters(0)
+
+        turned = next_bank([P, P])
+        nc.tensor.transpose(turned[:], level_blocks[:], ident[:])
+        nc.scalar.copy(level_cols[0][:], turned[:, 96:120])
+        nc.scalar.copy(level_cols[1][:], turned[:, 120:P])
+
+        def spread_level(m0):
+            spread = next_bank([P, 4, P])
+            for m in range(4):
+                part, col = divmod(m0 + m, 24)
+                nc.tensor.transpose(spread[:, m, :], level_cols[part][:, col : col + 1].to_broadcast([P, P]), ident[:])
+            nc.scalar.copy(level[:, m0 * P : (m0 + 4) * P], spread[:].rearrange("p m k -> p (m k)"))
+
+        for m0 in range(0, 24, 4):
+            spread_level(m0)
+        warm = next_bank([P, W], skip=2)
+        for i in range(3):
+            nc.tensor.matmul_mx(
+                out=warm[:],
+                lhsT=zero_q[:].bitcast(FP8X4),
+                lhsT_scale=zero_sc[:],
+                rhs=tab_sc[:, 0 : 2 * W].bitcast(FP4X4),
+                rhs_scale=tab_sc[:, 2 * W : 3 * W],
+                start=True,
+                stop=True,
+            )
+        for m0 in range(24, T // P, 4):
+            spread_level(m0)
+
         fill_planes(1, nc.sync)
-        load_filters(1)
-        load_weight(0, 1, 4096)
-        load_weight(1, 1, 8192)
-        nc.sync.dma_start(level[:], ts)
+        load_weight(0, 1, [0, 1], 4 * 4096)
+        load_weight(1, 1, [0, 1], 5 * 4096)
+        nc.sync.dma_start(
+            fb_raw[:].rearrange("p g t n -> p g (t n)"), fb.rearrange("(g p t) n -> p g (t n)", g=GROUPS, t=SLOTS)
+        )
 
-        gn_t = next_bank([P, GROUPS, P])
-        for g in range(GROUPS):
-            nc.tensor.transpose(gn_t[:, g, :], gn_rows[:, g, :], ident[:])
-        sign = keep.tile([P, GROUPS, 4], F32, name="sign")
-        gn_abs = keep.tile([P, GROUPS, 4], F32, name="gn_abs")
-        root = keep.tile([P, 8], F32, name="root")
-        nc.scalar.activation(gn_abs[:], gn_t[:, :, P - 4 : P], ACT.Abs)
-        nc.scalar.activation(sign[:], gn_t[:, :, P - 4 : P], ACT.Sign)
-        nc.scalar.activation(root[:], gn_abs[:].rearrange("p g t -> p (g t)"), ACT.Sqrt)
+        v = [keep.tile([P, PASSES, 2 * W], U8, name="v%d" % jh, align_bytes=64) for jh in range(HALVES)]
+        w_q = {}
 
-        picked_level = keep.tile([P, J], F32, name="picked_level")
-
-
-        def gather_words(jh, pair):
-            nc.vector.tensor_copy(pair[:].bitcast(U32), tab[:].bitcast(U32).indirect(offsets[:, 32 * jh : 32 * jh + 32]))
+        def gather_words(j0, cols, offset):
+            pair = shared.tile([P, cols], U32, name="pair%d" % j0, align_bytes=64, offset=12 * 4096 + offset)
+            nc.vector.tensor_copy(pair[:], tab[:].bitcast(U32).indirect(offsets[:, j0 // 16 : (j0 + cols) // 16]))
             return pair
 
-        v = {}
-
-        def part_words(jh, pair, passes):
-            tile = keep.tile([P, len(passes), 2 * W], U8, name="v%d%d" % (jh, passes[0]), align_bytes=64)
+        def part_words(j0, pair):
+            jh, c0 = divmod(j0, W)
             halves = pair[:].bitcast(U16).rearrange("p (c d) -> p d c", d=2)
-            nc.vector.tensor_copy(tile[:].bitcast(U16), halves[:, passes[0] : passes[-1] + 1, :])
-            for i, a in enumerate(passes):
-                v[jh, a] = tile[:, i, :]
+            nc.vector.tensor_copy(v[jh][:].bitcast(U16)[:, :, c0 : c0 + pair.shape[1]], halves)
 
-        def order_weight(w, g, passes, tile=None):
-            if tile is None:
-                tile = keep.tile([P, len(passes), 4, P], I32, name="w_q%d%d%d" % (w, g, passes[0]), align_bytes=64)
-            nc.vector.tensor_copy(
-                tile[:].rearrange("p a t (q r) -> p t a q r", r=8),
-                w_raw[w, g][:, passes[0] : passes[-1] + 1, :].rearrange("p a (q t r) -> p t a q r", t=4, r=8),
+        def order_weight(w, g, passes, copy, offset):
+            tile = shared.tile([P, len(passes), SLOTS, P], U32, name="w_q%d%d%d" % (w, g, passes[0]), align_bytes=64, offset=offset)
+            copy(
+                tile[:].rearrange("p a t m -> p a m t"),
+                w_raw[w, g, 0][:, passes[0] : passes[-1] + 1].bitcast(U32).rearrange("p a (m t) -> p a m t", t=SLOTS),
             )
             for i, a in enumerate(passes):
                 w_q[w, g, a] = tile[:, i]
 
-        def product(bank, jh, g, t, w, a, c0, cols, first):
+        def product(sums, g, t, w, a, j0, cols):
+            jh, c0 = divmod(j0, W)
             f0 = (1 + w) * W + t * P
             nc.tensor.matmul_mx(
-                out=bank,
+                out=sums,
                 lhsT=w_q[w, g, a][:, t, :].bitcast(FP8X4),
                 lhsT_scale=planes[g][:, a, f0 : f0 + P],
-                rhs=v[jh, a][:, 2 * c0 : 2 * (c0 + cols)].bitcast(FP4X4),
+                rhs=v[jh][:, a, 2 * c0 : 2 * (c0 + cols)].bitcast(FP4X4),
                 rhs_scale=planes[jh][:, a, c0 : c0 + cols],
-                start=first,
-                stop=not first,
+                start=(a == 0),
+                stop=(a == PASSES - 1),
             )
 
-        def squares(jh, g, order):
-            sq = [ring.tile([P, 4, W], F32, name="sq%d" % w, align_bytes=64, bufs=2) for w in range(2)]
-            banks = {}
-            for t, w, a in order:
-                first = (t, w) not in banks
-                if first:
-                    banks[t, w] = next_bank([P, W])
-                product(banks[t, w][:], jh, g, t, w, a, 0, W, first)
-                if not first:
-                    u = 4 * g + t
-                    nc.scalar.activation(sq[w][:, t, :], banks[t, w][:], ACT.Square, scale=root[:, u : u + 1])
+        def square(dst, src, g, t):
+            nc.scalar.activation(dst, src, ACT.Square, scale=root[:, g, t : t + 1])
+
+        def first_squares():
+            sq = keep.tile([P, SLOTS, 2, W], F32, name="sq_first", align_bytes=64)
+            for w in range(2):
+                banks = [next_bank([P, W]) for t in range(SLOTS)]
+                for a in range(PASSES):
+                    for t in range(SLOTS):
+                        product(banks[t][:], 0, t, w, a, 0, W)
+                for t in range(SLOTS):
+                    square(sq[:, t, w, :], banks[t][:], 0, t)
             return sq
 
-        def narrow_squares(jh, g, c0, cols):
-            sq = [
-                tail.tile([P, 4, cols], F32, name="sq%d_%d_%d" % (w, jh, c0), align_bytes=64, offset=16 * (2 * (jh * W + c0) + w * cols))
-                for w in range(2)
-            ]
-            for t0 in range(0, 4, 2):
+        def paired_squares(g, j0):
+            sq = ring.tile([P, SLOTS, 2, Q], F32, name="sq", align_bytes=64, bufs=4)
+            for t in range(SLOTS):
+                sums = next_bank([P, 2, Q])
                 for w in range(2):
-                    bank = next_bank([P, 2, cols])
-                    for t in range(t0, t0 + 2):
-                        for c in range(0, cols, P):
-                            for a in range(PASSES):
-                                product(bank[:, t - t0, c : c + P], jh, g, t, w, a, c0 + c, P, a == 0)
-                    for t in range(t0, t0 + 2):
-                        u = 4 * g + t
-                        nc.scalar.activation(sq[w][:, t, :], bank[:, t - t0, :], ACT.Square, scale=root[:, u : u + 1])
+                    for a in range(PASSES):
+                        product(sums[:, w, :], g, t, w, a, j0, Q)
+                square(sq[:, t], sums[:], g, t)
             return sq
 
-        def power(sq, c0, c1, h=None):
-            cols = c1 - c0
-            if h is None:
-                h = ring.tile([P, cols, 4], BF16, name="h", align_bytes=64)
+        def power(sq):
+            cols = sq.shape[3]
+            h = ring.tile([P, cols, SLOTS], BF16, name="h%d" % cols, align_bytes=64)
             nc.vector.tensor_tensor(
                 h[:].rearrange("p (c i) t -> p c t i", i=2),
-                sq[0][:, :, c0:c1].rearrange("p t (c i) -> p c t i", i=2),
-                sq[1][:, :, c0:c1].rearrange("p t (c i) -> p c t i", i=2),
+                sq[:, :, 0, :].rearrange("p t (c i) -> p c t i", i=2),
+                sq[:, :, 1, :].rearrange("p t (c i) -> p c t i", i=2),
                 ALU.add,
             )
             return h
 
-        def quantize(h, h_q=None, h_sc=None):
-            cols = h.shape[1]
-            if h_q is None:
-                h_q = ring.tile([P, cols], U32, name="h_q", align_bytes=64, bufs=6)
-            if h_sc is None:
-                h_sc = ring.tile([P, cols], U8, name="h_sc", align_bytes=64, bufs=6)
-            nc.vector.quantize_mx(out=h_q[:].bitcast(FP8X4), scales=h_sc[:], in_=h[:].rearrange("p c t -> p (c t)"))
-            return h_q[:], h_sc[:]
+        h_mx = {}
 
-        fb_b = keep.tile([P, GROUPS, N, 4], BF16, name="fb_b", align_bytes=64)
+        def quantize(h, g, j0):
+            cols = h.shape[1]
+            h_q = keep.tile([P, cols], U32, name="h_q%d_%d" % (g, j0), align_bytes=64)
+            h_sc = keep.tile([P, cols], U8, name="h_sc%d_%d" % (g, j0), align_bytes=64)
+            nc.vector.quantize_mx(out=h_q[:].bitcast(FP8X4), scales=h_sc[:], in_=h[:].rearrange("p c t -> p (c t)"))
+            for c in range(0, cols, Q):
+                h_mx[g, j0 + c] = (h_q[:, c : c + Q], h_sc[:, c : c + Q])
+
+        fb_b = keep.tile([P, GROUPS, N, SLOTS], BF16, name="fb_b", align_bytes=64)
         fb_q = keep.tile([P, GROUPS, N], U32, name="fb_q", align_bytes=64)
         fb_sc = keep.tile([P, GROUPS, N], U8, name="fb_sc", align_bytes=64)
 
         def round_filters(g):
             nc.vector.tensor_tensor(
                 fb_b[:, g].rearrange("p (c i) t -> p c t i", i=2),
-                fb_raw[g][:].rearrange("p t (c i) -> p c t i", i=2),
-                sign[:, g, :].unsqueeze(1).unsqueeze(3).broadcast_to([P, N // 2, 4, 2]),
+                fb_raw[:, g].rearrange("p t (c i) -> p c t i", i=2),
+                sign[:, g, :].unsqueeze(1).unsqueeze(3).broadcast_to([P, N // 2, SLOTS, 2]),
                 ALU.mult,
             )
 
@@ -241,85 +256,72 @@ def tile_list_meltab_gain_kernel(
                 in_=fb_b[:].rearrange("p g n t -> p (g n t)"),
             )
 
-        def filter_bank(bank, nt, hs, fb_q, fb_sc):
-            for g in range(GROUPS):
-                nc.tensor.matmul_mx(
-                    out=bank,
-                    lhsT=fb_q[:, g, nt * P : (nt + 1) * P].bitcast(FP8X4),
-                    lhsT_scale=fb_sc[:, g, nt * P : (nt + 1) * P],
-                    rhs=hs[g][0].bitcast(FP8X4),
-                    rhs_scale=hs[g][1],
-                    start=(g == 0),
-                    stop=(g == GROUPS - 1),
-                )
+        picked_level = shared.tile([P, J], F32, name="picked_level", align_bytes=64, offset=4096)
+        filtered = {}
 
-        def finish_wide(nt, hs, fb_q, fb_sc, picked, y):
-            bank = next_bank([P, W])
-            filter_bank(bank[:], nt, hs, fb_q, fb_sc)
-            nc.vector.tensor_tensor(y[:], bank[:], picked[:, 0:W], ALU.mult)
-            nc.sync.dma_start(out[nt * P : (nt + 1) * P, 0:W], y[:])
-
-        def finish_narrow(j0, cols, hs, fb_q, fb_sc, picked, y):
-            bank = next_bank([P, N // P, cols])
+        def filter_products(j0):
+            sums = next_bank([P, N // P, Q])
+            filtered[j0] = sums
             for nt in range(N // P):
-                filter_bank(bank[:, nt, :], nt, hs, fb_q, fb_sc)
-            nc.vector.tensor_tensor(y[:], bank[:], picked[:, j0 : j0 + cols].unsqueeze(1).broadcast_to([P, N // P, cols]), ALU.mult)
-            nc.sync.dma_start(out.rearrange("(nt p) j -> p nt j", p=P)[:, :, j0 : j0 + cols], y[:])
+                for g in range(GROUPS):
+                    nc.tensor.matmul_mx(
+                        out=sums[:, nt, :],
+                        lhsT=fb_q[:, g, nt * P : (nt + 1) * P].bitcast(FP8X4),
+                        lhsT_scale=fb_sc[:, g, nt * P : (nt + 1) * P],
+                        rhs=h_mx[g, j0][0].bitcast(FP8X4),
+                        rhs_scale=h_mx[g, j0][1],
+                        start=(g == 0),
+                        stop=(g == GROUPS - 1),
+                    )
 
-        def cut(h, c0, c1):
-            return h[0][:, c0:c1], h[1][:, c0:c1]
-
-        warm = psum.tile([P, W], F32, name="bank1")
-        for i in range(4):
-            nc.tensor.matmul_mx(
-                out=warm[:],
-                lhsT=zero_q[:].bitcast(FP8X4),
-                lhsT_scale=zero_sc[:],
-                rhs=tab_sc[:, 0 : 2 * W].bitcast(FP4X4),
-                rhs_scale=picked_scales[1][:],
-                start=True,
-                stop=True,
+        def finish(j0):
+            y = keep.tile([P, N // P, Q], F32, name="y%d" % j0, align_bytes=64)
+            nc.vector.tensor_tensor(
+                y[:], filtered[j0][:], picked_level[:, j0 : j0 + Q].unsqueeze(1).broadcast_to([P, N // P, Q]), ALU.mult
             )
+            nc.sync.dma_start(out.rearrange("(nt p) j -> p nt j", p=P)[:, :, j0 : j0 + Q], y[:])
 
-        first_unit = [(t, w, a) for w in range(2) for t in range(4) for a in range(PASSES)]
-        by_tile = [(t, w, a) for t in range(4) for w in range(2) for a in range(PASSES)]
-        H = W // 2
-        pair0 = gather_words(0, chain.tile([P, W], I32, name="pair0", align_bytes=64, offset=22528))
-        order_weight(0, 0, [0])
-        part_words(0, pair0, [0])
-        order_weight(0, 0, [1])
-        part_words(0, pair0, [1])
-        order_weight(1, 0, [0, 1])
-        pair1 = gather_words(1, chain.tile([P, W], I32, name="pair1", align_bytes=64, offset=0))
-        part_words(1, pair1, [0, 1])
-        sq00 = squares(0, 0, first_unit)
-        sq10 = squares(1, 0, by_tile)
-        round_filters(0)
-        round_filters(1)
-        order_weight(0, 1, [0, 1])
-        sum00 = power(sq00, 0, W, chain.tile([P, W, 4], BF16, name="h_first", align_bytes=64, offset=4096))
-        quantize_filters()
-        order_weight(1, 1, [0, 1])
-        sq01a = narrow_squares(0, 1, 0, H)
-        sq01b = narrow_squares(0, 1, H, H)
-        h00 = quantize(sum00, chain.tile([P, W], U32, name="h_q_first", align_bytes=64, offset=8192))
-        sum10 = power(sq10, 0, W, chain.tile([P, W, 4], BF16, name="h_second", align_bytes=64, offset=10240))
+        pair0 = gather_words(0, Q, 1024)
+        pair1 = gather_words(Q, Q, 2048)
+        part_words(0, pair0)
+        part_words(Q, pair1)
+        order_weight(0, 0, [0], nc.scalar.copy, 18 * 4096 - 2048)
+        order_weight(0, 0, [1], nc.scalar.copy, 18 * 4096)
+        pair2 = gather_words(W, W, 0)
+        order_weight(1, 0, [0, 1], nc.vector.tensor_copy, 25 * 4096)
+        part_words(W, pair2)
+        sq_a = first_squares()
         nc.vector.tensor_copy(picked_level[:], level[:].indirect(offsets[:]))
-        sum01a = power(sq01a, 0, H, chain.tile([P, H, 4], BF16, name="h_third_a", align_bytes=64, offset=28672))
-        h10 = quantize(sum10, chain.tile([P, W], U32, name="h_q_second", align_bytes=64, offset=36864))
-        h01 = (keep.tile([P, W], U32, name="h01_q", align_bytes=64)[:], keep.tile([P, W], U8, name="h01_sc", align_bytes=64)[:])
-        quantize(sum01a, *cut(h01, 0, H))
-        sq11a = narrow_squares(1, 1, 0, H)
-        sq11b = narrow_squares(1, 1, H, H)
-        sum01b = power(sq01b, 0, H, chain.tile([P, H, 4], BF16, name="h_third_b", align_bytes=64, offset=30720))
-        sum11a = power(sq11a, 0, H, chain.tile([P, H, 4], BF16, name="h_a", align_bytes=64, offset=32768))
-        quantize(sum01b, *cut(h01, H, W))
-        h11a = quantize(sum11a)
-        sum11b = power(sq11b, 0, H, chain.tile([P, H, 4], BF16, name="h_b", align_bytes=64, offset=34816))
-        finish_wide(0, [h00, h01], fb_q, fb_sc, picked_level, keep.tile([P, W], F32, name="y0", align_bytes=64))
-        h11b = quantize(sum11b)
-        finish_wide(1, [h00, h01], fb_q, fb_sc, picked_level, keep.tile([P, W], F32, name="y1", align_bytes=64))
-        y_a = keep.tile([P, 2, H], F32, name="y_a", align_bytes=64)
-        finish_narrow(W, H, [cut(h10, 0, H), h11a], fb_q, fb_sc, picked_level, y_a)
-        y_b = keep.tile([P, 2, H], F32, name="y_b", align_bytes=64)
-        finish_narrow(W + H, H, [cut(h10, H, W), h11b], fb_q, fb_sc, picked_level, y_b)
+        sq_b = paired_squares(0, 2 * Q)
+        order_weight(0, 1, [0, 1], nc.vector.tensor_copy, 27 * 4096)
+        order_weight(1, 1, [0, 1], nc.vector.tensor_copy, 28 * 4096)
+        h_a = power(sq_a)
+        sq_c = paired_squares(0, 3 * Q)
+        round_filters(0)
+        quantize(h_a, 0, 0)
+        h_b = power(sq_b)
+        round_filters(1)
+        quantize(h_b, 0, 2 * Q)
+        h_c = power(sq_c)
+        quantize_filters()
+        sq_0 = paired_squares(1, 0)
+        h_0 = power(sq_0)
+        quantize(h_c, 0, 3 * Q)
+        sq_1 = paired_squares(1, Q)
+        h_1 = power(sq_1)
+        quantize(h_0, 1, 0)
+        sq_2 = paired_squares(1, 2 * Q)
+        h_2 = power(sq_2)
+        quantize(h_1, 1, Q)
+        sq_3 = paired_squares(1, 3 * Q)
+        filter_products(0)
+        filter_products(Q)
+        finish(0)
+        quantize(h_2, 1, 2 * Q)
+        filter_products(2 * Q)
+        h_3 = power(sq_3)
+        finish(Q)
+        quantize(h_3, 1, 3 * Q)
+        finish(2 * Q)
+        filter_products(3 * Q)
+        finish(3 * Q)

@@ -1,7 +1,6 @@
 from contextlib import ExitStack
 
 import concourse.mybir as mybir
-from concourse.masks import make_identity
 
 K, F, N, T, J = 1024, 1024, 256, 4096, 1024
 FLOPS = 2 * (2 * K * F * J + F * N * J)
@@ -40,25 +39,19 @@ def tile_list_meltab_gain_kernel(
         psum = ctx.enter_context(tc.psum_pool(name="psum", bufs=1))
 
         offsets = keep.tile([P, J // 16], U16, name="offsets")
-        tab = shared.tile([P, T], I32, name="tab", align_bytes=64, offset=23 * 4096)
+        tab = shared.tile([P, T], I32, name="tab", align_bytes=64, offset=90112)
         tab_sc = keep.tile([P, T], U8, name="tab_sc", align_bytes=64)
         w_sc_raw = keep.tile([P, 2 * F], U8, name="w_sc_raw", align_bytes=64)
-        joined = [shared.tile([P, 3 * W], U8, name="joined%d" % s, align_bytes=64, offset=5 * 4096 - W + 4096 * 4 * s) for s in range(2)]
+        joined = [shared.tile([P, 3 * W], U8, name="joined%d" % s, align_bytes=64, offset=(32256, 40448)[s]) for s in range(2)]
         planes = [keep.tile([P, PASSES, 3 * W], U8, name="planes%d" % s, align_bytes=64) for s in range(2)]
-        gain = shared.tile([P, GROUPS, SLOTS], F32, name="gain", align_bytes=64, offset=2048 + 128)
-        level = shared.tile([P, T], F32, name="level", align_bytes=64, offset=27 * 4096)
-        level_blocks = keep.tile([P, P], F32, name="level_blocks", align_bytes=64)
-        level_cols = [
-            shared.tile([P, 24], F32, name="level_cols0", align_bytes=64, offset=18 * 4096 - 64),
-            keep.tile([P, 8], F32, name="level_cols1", align_bytes=64),
-        ]
-        ident = keep.tile([P, P], F32, name="ident")
-        fb_raw = shared.tile([P, GROUPS, SLOTS, N], F32, name="fb_raw", align_bytes=64, offset=23 * 4096)
+        gain = shared.tile([P, GROUPS, SLOTS], F32, name="gain", align_bytes=64, offset=20224)
+        level = shared.tile([P, T], F32, name="level", align_bytes=64, offset=0)
+        fb_raw = [shared.tile([P, SLOTS, N], F32, name="fb_raw%d" % g, align_bytes=64, offset=(16320, 28672)[g]) for g in range(GROUPS)]
 
         turns = []
 
-        def next_bank(shape, skip=0):
-            turns.extend([shape] * (1 + skip))
+        def next_bank(shape):
+            turns.append(shape)
             return psum.tile(shape, F32, name="bank%d" % (len(turns) % 8))
 
         w_raw = {}
@@ -72,13 +65,12 @@ def tile_list_meltab_gain_kernel(
         nc.sync.dma_start(gain[:], gn.rearrange("(g p t) -> p g t", g=GROUPS, t=SLOTS))
         nc.sync.dma_start(tab_sc[96:P, :].bitcast(I32), tab_scales.bitcast(I32).rearrange("a q t -> q a t"))
         nc.sync.dma_start(offsets[:], offs)
-        nc.sync.dma_start(level_blocks[96:P, :], ts[0].rearrange("(m k) -> m k", k=P))
         nc.sync.dma_start(tab[:], tab_words.rearrange("e p t b -> p (e t b)").bitcast(I32))
         for w in range(2):
             nc.scalar.dma_start(
                 w_sc_raw[96:P, w * F : (w + 1) * F].bitcast(I32), w_scales[w].bitcast(I32).rearrange("a q f -> q a f")
             )
-        load_weight(0, 0, [0, 1], 11 * 4096)
+        load_weight(0, 0, [0, 1], 86016)
 
         nc.vector.memset(tab_sc[0:96, :].bitcast(I32), 0)
         nc.vector.memset(w_sc_raw[0:96, :].bitcast(I32), 0)
@@ -87,13 +79,11 @@ def tile_list_meltab_gain_kernel(
         zero_sc = keep.tile([P, P], U8, name="zero_sc", align_bytes=64)
         nc.vector.memset(zeros[:].bitcast(I32), 0)
         nc.vector.quantize_mx(out=zero_q[:].bitcast(FP8X4), scales=zero_sc[:], in_=zeros[:])
-        nc.gpsimd.memset(level_blocks[0:96, :], 0.0)
-        make_identity(nc, ident[:])
         for s in range(2):
             nc.gpsimd.memset(planes[s][:].bitcast(I32), 0)
 
         def join_scales(s):
-            picked_sc = shared.tile([P, (2 - s) * W], U8, name="picked_sc%d" % s, align_bytes=64, offset=2048 - 64 + 64 * s)
+            picked_sc = shared.tile([P, (2 - s) * W], U8, name="picked_sc%d" % s, align_bytes=64, offset=(20160, 20352)[s])
             nc.vector.tensor_copy(picked_sc[:, 0:W], tab_sc[:].indirect(offsets[:, 32 * s : 32 * s + 32]))
             nc.vector.tensor_copy(
                 joined[s][:, W:].rearrange("p (w t m) -> p w t m", w=2, t=SLOTS),
@@ -108,60 +98,45 @@ def tile_list_meltab_gain_kernel(
                     joined[s][96 + 8 * quad : 96 + 8 * quad + 8, :].bitcast(I32),
                 )
 
-        gn_abs = shared.tile([P, GROUPS, SLOTS], F32, name="gn_abs", align_bytes=64, offset=18 * 4096 - 64)
+        gn_abs = shared.tile([P, GROUPS, 16], F32, name="gn_abs", align_bytes=64, offset=63488 - 64)
         root = keep.tile([P, GROUPS, SLOTS], F32, name="root")
-        nc.vector.scalar_tensor_tensor(gn_abs[:], gain[:], -1.0, gain[:], ALU.mult, ALU.max)
+        nc.vector.scalar_tensor_tensor(gn_abs[:, :, 0:SLOTS], gain[:], -1.0, gain[:], ALU.mult, ALU.max)
         is_pos = keep.tile([P, GROUPS, SLOTS], F32, name="is_pos")
         nc.vector.tensor_scalar(is_pos[:], gain[:], 0.0, 2.0, ALU.is_ge, ALU.mult)
-        nc.scalar.activation(root[:], gn_abs[:], ACT.Sqrt)
+        nc.scalar.activation(root[:], gn_abs[:, :, 0:SLOTS], ACT.Sqrt)
         join_scales(0)
         fill_planes(0, nc.sync)
-        load_weight(1, 0, [0, 1], 2048 + 2 * W - 128)
+        load_weight(1, 0, [0, 1], 21120)
 
         sign = keep.tile([P, GROUPS, SLOTS], F32, name="sign")
         nc.gpsimd.tensor_scalar(sign[:], is_pos[:], 1.0, -1.0, ALU.mult, ALU.add)
         join_scales(1)
 
-        turned = next_bank([P, P])
-        nc.tensor.transpose(turned[:], level_blocks[:], ident[:])
-        nc.scalar.copy(level_cols[0][:], turned[:, 96:120])
-        nc.scalar.copy(level_cols[1][:], turned[:, 120:P])
-
-        def spread_level(m0):
-            spread = next_bank([P, 4, P])
-            for m in range(4):
-                part, col = divmod(m0 + m, 24)
-                nc.tensor.transpose(spread[:, m, :], level_cols[part][:, col : col + 1].to_broadcast([P, P]), ident[:])
-            nc.scalar.copy(level[:, m0 * P : (m0 + 4) * P], spread[:].rearrange("p m k -> p (m k)"))
-
-        for m0 in range(0, 24, 4):
-            spread_level(m0)
-        warm = next_bank([P, W], skip=2)
-        for i in range(3):
+        warm = next_bank([P, W])
+        for i in range(4):
             nc.tensor.matmul_mx(
                 out=warm[:],
                 lhsT=zero_q[:].bitcast(FP8X4),
                 lhsT_scale=zero_sc[:],
-                rhs=tab_sc[:, 0 : 2 * W].bitcast(FP4X4),
-                rhs_scale=tab_sc[:, 2 * W : 3 * W],
+                rhs=tab[:, 0 : W // 2].bitcast(FP4X4),
+                rhs_scale=tab_sc[:, 0:W],
                 start=True,
                 stop=True,
             )
-        for m0 in range(24, T // P, 4):
-            spread_level(m0)
 
+        fb_rows = fb.rearrange("(g p t) n -> g p (t n)", g=GROUPS, t=SLOTS)
+        nc.sync.dma_start(fb_raw[0][:].rearrange("p t n -> p (t n)"), fb_rows[0])
         fill_planes(1, nc.sync)
-        load_weight(0, 1, [0, 1], 4 * 4096)
-        load_weight(1, 1, [0, 1], 5 * 4096)
-        nc.sync.dma_start(
-            fb_raw[:].rearrange("p g t n -> p g (t n)"), fb.rearrange("(g p t) n -> p g (t n)", g=GROUPS, t=SLOTS)
-        )
+        nc.sync.dma_start(fb_raw[1][:].rearrange("p t n -> p (t n)"), fb_rows[1])
+        load_weight(0, 1, [0, 1], 32768)
+        load_weight(1, 1, [0, 1], 90112 + 4096)
+        nc.sync.dma_start(level[:], ts)
 
         v = [keep.tile([P, PASSES, 2 * W], U8, name="v%d" % jh, align_bytes=64) for jh in range(HALVES)]
         w_q = {}
 
         def gather_words(j0, cols, offset):
-            pair = shared.tile([P, cols], U32, name="pair%d" % j0, align_bytes=64, offset=12 * 4096 + offset)
+            pair = shared.tile([P, cols], U32, name="pair%d" % j0, align_bytes=64, offset=57344 + offset)
             nc.vector.tensor_copy(pair[:], tab[:].bitcast(U32).indirect(offsets[:, j0 // 16 : (j0 + cols) // 16]))
             return pair
 
@@ -192,37 +167,49 @@ def tile_list_meltab_gain_kernel(
                 stop=(a == PASSES - 1),
             )
 
-        def square(dst, src, g, t):
-            nc.scalar.activation(dst, src, ACT.Square, scale=root[:, g, t : t + 1])
+        def square(dst, src, roots, t):
+            nc.scalar.activation(dst, src, ACT.Square, scale=roots[:, t : t + 1])
 
         def first_squares():
-            sq = keep.tile([P, SLOTS, 2, W], F32, name="sq_first", align_bytes=64)
-            for w in range(2):
-                banks = [next_bank([P, W]) for t in range(SLOTS)]
-                for a in range(PASSES):
-                    for t in range(SLOTS):
-                        product(banks[t][:], 0, t, w, a, 0, W)
-                for t in range(SLOTS):
-                    square(sq[:, t, w, :], banks[t][:], 0, t)
-            return sq
-
-        def paired_squares(g, j0):
-            sq = ring.tile([P, SLOTS, 2, Q], F32, name="sq", align_bytes=64, bufs=4)
+            sq_re = shared.tile([P, SLOTS, W], F32, name="sq_first_re", align_bytes=64, offset=69632)
+            sq_im = [keep.tile([P, SLOTS, Q], F32, name="sq_first_im%d" % i, align_bytes=64) for i in range(2)]
+            banks = [next_bank([P, W]) for t in range(SLOTS)]
             for t in range(SLOTS):
-                sums = next_bank([P, 2, Q])
-                for w in range(2):
-                    for a in range(PASSES):
-                        product(sums[:, w, :], g, t, w, a, j0, Q)
-                square(sq[:, t], sums[:], g, t)
-            return sq
+                for a in range(PASSES):
+                    product(banks[t][:], 0, t, 0, a, 0, W)
+            for t in range(SLOTS):
+                square(sq_re[:, t, :], banks[t][:], root[:, 0, :], t)
+            for j0 in range(0, W, Q):
+                for t0 in range(0, SLOTS, 2):
+                    sums = next_bank([P, 2, Q])
+                    for t in range(t0, t0 + 2):
+                        for a in range(PASSES):
+                            product(sums[:, t - t0, :], 0, t, 1, a, j0, Q)
+                    for t in range(t0, t0 + 2):
+                        square(sq_im[j0 // Q][:, t, :], sums[:, t - t0, :], root[:, 0, :], t)
+            return [(sq_re[:, :, i * Q : (i + 1) * Q], sq_im[i][:]) for i in range(2)]
 
-        def power(sq):
-            cols = sq.shape[3]
-            h = ring.tile([P, cols, SLOTS], BF16, name="h%d" % cols, align_bytes=64)
+        def paired_squares(g, j0, cols=Q):
+            sq = ring.tile([P, SLOTS, 2, cols], F32, name="sq", align_bytes=64, bufs=7)
+            per_bank = W // (2 * cols)
+            for t0 in range(0, SLOTS, per_bank):
+                sums = next_bank([P, per_bank, 2, cols])
+                for t in range(t0, t0 + per_bank):
+                    for w in range(2):
+                        for a in range(PASSES):
+                            product(sums[:, t - t0, w, :], g, t, w, a, j0, cols)
+                for t in range(t0, t0 + per_bank):
+                    square(sq[:, t], sums[:, t - t0], root[:, g, :], t)
+            return sq[:, :, 0, :], sq[:, :, 1, :]
+
+        def power(sq, h=None):
+            cols = sq[0].shape[2]
+            if h is None:
+                h = ring.tile([P, cols, SLOTS], BF16, name="h%d" % cols, align_bytes=64)
             nc.vector.tensor_tensor(
                 h[:].rearrange("p (c i) t -> p c t i", i=2),
-                sq[:, :, 0, :].rearrange("p t (c i) -> p c t i", i=2),
-                sq[:, :, 1, :].rearrange("p t (c i) -> p c t i", i=2),
+                sq[0].rearrange("p t (c i) -> p c t i", i=2),
+                sq[1].rearrange("p t (c i) -> p c t i", i=2),
                 ALU.add,
             )
             return h
@@ -234,17 +221,17 @@ def tile_list_meltab_gain_kernel(
             h_q = keep.tile([P, cols], U32, name="h_q%d_%d" % (g, j0), align_bytes=64)
             h_sc = keep.tile([P, cols], U8, name="h_sc%d_%d" % (g, j0), align_bytes=64)
             nc.vector.quantize_mx(out=h_q[:].bitcast(FP8X4), scales=h_sc[:], in_=h[:].rearrange("p c t -> p (c t)"))
-            for c in range(0, cols, Q):
-                h_mx[g, j0 + c] = (h_q[:, c : c + Q], h_sc[:, c : c + Q])
+            for c in range(0, cols, P):
+                h_mx[g, j0 + c] = (h_q[:, c:], h_sc[:, c:])
 
-        fb_b = keep.tile([P, GROUPS, N, SLOTS], BF16, name="fb_b", align_bytes=64)
-        fb_q = keep.tile([P, GROUPS, N], U32, name="fb_q", align_bytes=64)
+        fb_b = shared.tile([P, GROUPS, N, SLOTS], BF16, name="fb_b", align_bytes=64, offset=57344)
+        fb_q = shared.tile([P, GROUPS, N], U32, name="fb_q", align_bytes=64, offset=90112 + 4096 + 2048)
         fb_sc = keep.tile([P, GROUPS, N], U8, name="fb_sc", align_bytes=64)
 
         def round_filters(g):
             nc.vector.tensor_tensor(
                 fb_b[:, g].rearrange("p (c i) t -> p c t i", i=2),
-                fb_raw[:, g].rearrange("p t (c i) -> p c t i", i=2),
+                fb_raw[g][:].rearrange("p t (c i) -> p c t i", i=2),
                 sign[:, g, :].unsqueeze(1).unsqueeze(3).broadcast_to([P, N // 2, SLOTS, 2]),
                 ALU.mult,
             )
@@ -256,11 +243,11 @@ def tile_list_meltab_gain_kernel(
                 in_=fb_b[:].rearrange("p g n t -> p (g n t)"),
             )
 
-        picked_level = shared.tile([P, J], F32, name="picked_level", align_bytes=64, offset=4096)
+        picked_level = shared.tile([P, J], F32, name="picked_level", align_bytes=64, offset=69632)
         filtered = {}
 
-        def filter_products(j0):
-            sums = next_bank([P, N // P, Q])
+        def filter_products(j0, cols=Q):
+            sums = next_bank([P, N // P, cols])
             filtered[j0] = sums
             for nt in range(N // P):
                 for g in range(GROUPS):
@@ -268,60 +255,68 @@ def tile_list_meltab_gain_kernel(
                         out=sums[:, nt, :],
                         lhsT=fb_q[:, g, nt * P : (nt + 1) * P].bitcast(FP8X4),
                         lhsT_scale=fb_sc[:, g, nt * P : (nt + 1) * P],
-                        rhs=h_mx[g, j0][0].bitcast(FP8X4),
-                        rhs_scale=h_mx[g, j0][1],
+                        rhs=h_mx[g, j0][0][:, 0:cols].bitcast(FP8X4),
+                        rhs_scale=h_mx[g, j0][1][:, 0:cols],
                         start=(g == 0),
                         stop=(g == GROUPS - 1),
                     )
 
         def finish(j0):
-            y = keep.tile([P, N // P, Q], F32, name="y%d" % j0, align_bytes=64)
+            cols = filtered[j0].shape[2]
+            y = keep.tile([P, N // P, cols], F32, name="y%d" % j0, align_bytes=64)
             nc.vector.tensor_tensor(
-                y[:], filtered[j0][:], picked_level[:, j0 : j0 + Q].unsqueeze(1).broadcast_to([P, N // P, Q]), ALU.mult
+                y[:], filtered[j0][:], picked_level[:, j0 : j0 + cols].unsqueeze(1).broadcast_to([P, N // P, cols]), ALU.mult
             )
-            nc.sync.dma_start(out.rearrange("(nt p) j -> p nt j", p=P)[:, :, j0 : j0 + Q], y[:])
+            nc.sync.dma_start(out.rearrange("(nt p) j -> p nt j", p=P)[:, :, j0 : j0 + cols], y[:])
 
         pair0 = gather_words(0, Q, 1024)
         pair1 = gather_words(Q, Q, 2048)
         part_words(0, pair0)
         part_words(Q, pair1)
-        order_weight(0, 0, [0], nc.scalar.copy, 18 * 4096 - 2048)
-        order_weight(0, 0, [1], nc.scalar.copy, 18 * 4096)
+        order_weight(0, 0, [0], nc.scalar.copy, 61440)
+        order_weight(0, 0, [1], nc.scalar.copy, 63488)
         pair2 = gather_words(W, W, 0)
-        order_weight(1, 0, [0, 1], nc.vector.tensor_copy, 25 * 4096)
+        order_weight(1, 0, [0, 1], nc.vector.tensor_copy, 90112)
         part_words(W, pair2)
         sq_a = first_squares()
-        nc.vector.tensor_copy(picked_level[:], level[:].indirect(offsets[:]))
-        sq_b = paired_squares(0, 2 * Q)
-        order_weight(0, 1, [0, 1], nc.vector.tensor_copy, 27 * 4096)
-        order_weight(1, 1, [0, 1], nc.vector.tensor_copy, 28 * 4096)
-        h_a = power(sq_a)
-        sq_c = paired_squares(0, 3 * Q)
         round_filters(0)
-        quantize(h_a, 0, 0)
-        h_b = power(sq_b)
         round_filters(1)
-        quantize(h_b, 0, 2 * Q)
-        h_c = power(sq_c)
+        sq_b = paired_squares(0, 2 * Q)
+        h_a0 = power(sq_a[0], shared.tile([P, Q, SLOTS], BF16, name="h_a0", align_bytes=64, offset=28672))
+        order_weight(0, 1, [0, 1], nc.vector.tensor_copy, 65536)
+        h_a1 = power(sq_a[1], shared.tile([P, Q, SLOTS], BF16, name="h_a1", align_bytes=64, offset=28672 + 2048))
+        order_weight(1, 1, [0, 1], nc.vector.tensor_copy, 16384)
+        quantize(h_a0, 0, 0)
         quantize_filters()
+        sq_c = paired_squares(0, 3 * Q)
+        quantize(h_a1, 0, Q)
+        h_b = power(sq_b, shared.tile([P, Q, SLOTS], BF16, name="h_b", align_bytes=64, offset=90112 + 4096))
+        h_c = power(sq_c, shared.tile([P, Q, SLOTS], BF16, name="h_c", align_bytes=64, offset=69632 + 4096 + 2048))
+        quantize(h_b, 0, 2 * Q)
+        nc.vector.tensor_copy(picked_level[:], level[:].indirect(offsets[:]))
         sq_0 = paired_squares(1, 0)
-        h_0 = power(sq_0)
+        h_0 = power(sq_0, shared.tile([P, Q, SLOTS], BF16, name="h_0", align_bytes=64, offset=0))
         quantize(h_c, 0, 3 * Q)
         sq_1 = paired_squares(1, Q)
-        h_1 = power(sq_1)
         quantize(h_0, 1, 0)
+        h_1 = power(sq_1, shared.tile([P, Q, SLOTS], BF16, name="h_1", align_bytes=64, offset=2048))
         sq_2 = paired_squares(1, 2 * Q)
-        h_2 = power(sq_2)
-        quantize(h_1, 1, Q)
-        sq_3 = paired_squares(1, 3 * Q)
+        sq_3 = paired_squares(1, 3 * Q, P)
+        sq_4 = paired_squares(1, 3 * Q + P, P)
         filter_products(0)
+        quantize(h_1, 1, Q)
         filter_products(Q)
+        h_2 = power(sq_2)
         finish(0)
         quantize(h_2, 1, 2 * Q)
         filter_products(2 * Q)
         h_3 = power(sq_3)
-        finish(Q)
+        h_4 = power(sq_4)
         quantize(h_3, 1, 3 * Q)
+        filter_products(3 * Q, P)
+        quantize(h_4, 1, 3 * Q + P)
+        filter_products(3 * Q + P, P)
+        finish(Q)
         finish(2 * Q)
-        filter_products(3 * Q)
         finish(3 * Q)
+        finish(3 * Q + P)

@@ -74,11 +74,6 @@ def tile_list_meltab_gain_kernel(
 
         nc.vector.memset(tab_sc[0:96, :].bitcast(I32), 0)
         nc.vector.memset(w_sc_raw[0:96, :].bitcast(I32), 0)
-        zeros = keep.tile([P, W], BF16, name="zeros", align_bytes=64)
-        zero_q = keep.tile([P, P], U32, name="zero_q", align_bytes=64)
-        zero_sc = keep.tile([P, P], U8, name="zero_sc", align_bytes=64)
-        nc.vector.memset(zeros[:].bitcast(I32), 0)
-        nc.vector.quantize_mx(out=zero_q[:].bitcast(FP8X4), scales=zero_sc[:], in_=zeros[:])
         for s in range(2):
             nc.gpsimd.memset(planes[s][:].bitcast(I32), 0)
 
@@ -111,18 +106,6 @@ def tile_list_meltab_gain_kernel(
         sign = keep.tile([P, GROUPS, SLOTS], F32, name="sign")
         nc.gpsimd.tensor_scalar(sign[:], is_pos[:], 1.0, -1.0, ALU.mult, ALU.add)
         join_scales(1)
-
-        warm = next_bank([P, W])
-        for i in range(4):
-            nc.tensor.matmul_mx(
-                out=warm[:],
-                lhsT=zero_q[:].bitcast(FP8X4),
-                lhsT_scale=zero_sc[:],
-                rhs=tab[:, 0 : W // 2].bitcast(FP4X4),
-                rhs_scale=tab_sc[:, 0:W],
-                start=True,
-                stop=True,
-            )
 
         fb_rows = fb.rearrange("(g p t) n -> g p (t n)", g=GROUPS, t=SLOTS)
         nc.sync.dma_start(fb_raw[0][:].rearrange("p t n -> p (t n)"), fb_rows[0])

from contextlib import ExitStack

import concourse.mybir as mybir

K, F, N, T, J = 1024, 1024, 256, 4096, 1024
FLOPS = 2 * (2 * K * F * J + F * N * J)

F32 = mybir.dt.float32
BF16 = mybir.dt.bfloat16
I32 = mybir.dt.int32
U32 = mybir.dt.uint32
U16 = mybir.dt.uint16
U8 = mybir.dt.uint8
FP8X4 = mybir.dt.float8_e4m3fn_x4
FP4X4 = mybir.dt.float4_e2m1fn_x4
ALU = mybir.AluOpType
ACT = mybir.ActivationFunctionType

P = 128
W = 512
Q = 256
HALVES = J // W
GROUPS = F // 512
PASSES = K // 512
SLOTS = 4


def tile_list_meltab_gain_kernel(
    tc, tab_words, tab_scales, co_words, co_scales, si_words, si_scales, gn, fb, ts, offs, out
):
    nc = tc.nc
    w_words = (co_words, si_words)
    w_scales = (co_scales, si_scales)

    with ExitStack() as ctx:
        keep = ctx.enter_context(tc.tile_pool(name="keep", bufs=1))
        ring = ctx.enter_context(tc.tile_pool(name="ring", bufs=3))
        shared = ctx.enter_context(tc.tile_pool(name="shared", bufs=1))
        psum = ctx.enter_context(tc.psum_pool(name="psum", bufs=1))

        offsets = keep.tile([P, J // 16], U16, name="offsets")
        tab = shared.tile([P, T], I32, name="tab", align_bytes=64, offset=90112)
        tab_sc = keep.tile([P, T], U8, name="tab_sc", align_bytes=64)
        w_sc_raw = keep.tile([P, 2 * F], U8, name="w_sc_raw", align_bytes=64)
        joined = [shared.tile([P, 3 * W], U8, name="joined%d" % s, align_bytes=64, offset=(32256, 40448)[s]) for s in range(2)]
        planes = [keep.tile([P, PASSES, 3 * W], U8, name="planes%d" % s, align_bytes=64) for s in range(2)]
        gain = shared.tile([P, GROUPS, SLOTS], F32, name="gain", align_bytes=64, offset=20224)
        level = shared.tile([P, T], F32, name="level", align_bytes=64, offset=0)
        fb_raw = [shared.tile([P, SLOTS, N], F32, name="fb_raw%d" % g, align_bytes=64, offset=(16320, 28672)[g]) for g in range(GROUPS)]

        turns = []

        def next_bank(shape):
            turns.append(shape)
            return psum.tile(shape, F32, name="bank%d" % (len(turns) % 8))

        w_raw = {}

        def load_weight(w, g, passes, offset):
            raw = shared.tile([P, len(passes), W], I32, name="w_raw%d%d%d" % (w, g, passes[0]), align_bytes=64, offset=offset)
            words = w_words[w].rearrange("a p f b -> p a (f b)").bitcast(I32)
            nc.sync.dma_start(raw[:], words[:, passes[0] : passes[-1] + 1, g * W : (g + 1) * W])
            w_raw[w, g, passes[0]] = raw

        nc.sync.dma_start(gain[:], gn.rearrange("(g p t) -> p g t", g=GROUPS, t=SLOTS))
        nc.sync.dma_start(tab_sc[96:P, :].bitcast(I32), tab_scales.bitcast(I32).rearrange("a q t -> q a t"))
        nc.sync.dma_start(offsets[:], offs)
        nc.sync.dma_start(tab[:], tab_words.rearrange("e p t b -> p (e t b)").bitcast(I32))
        for w in range(2):
            nc.scalar.dma_start(
                w_sc_raw[96:P, w * F : (w + 1) * F].bitcast(I32), w_scales[w].bitcast(I32).rearrange("a q f -> q a f")
            )
        load_weight(0, 0, [0, 1], 86016)

        nc.vector.memset(tab_sc[0:96, :].bitcast(I32), 0)
        nc.vector.memset(w_sc_raw[0:96, :].bitcast(I32), 0)
        for s in range(2):
            nc.gpsimd.memset(planes[s][:].bitcast(I32), 0)

        def join_scales(s):
            picked_sc = shared.tile([P, (2 - s) * W], U8, name="picked_sc%d" % s, align_bytes=64, offset=(20160, 20352)[s])
            nc.vector.tensor_copy(picked_sc[:, 0:W], tab_sc[:].indirect(offsets[:, 32 * s : 32 * s + 32]))
            nc.vector.tensor_copy(
                joined[s][:, W:].rearrange("p (w t m) -> p w t m", w=2, t=SLOTS),
                w_sc_raw[:].rearrange("p (w g m t) -> p g w t m", w=2, g=GROUPS, t=SLOTS)[:, s],
            )
            nc.vector.tensor_copy(joined[s][96:P, 0:W].bitcast(I32), picked_sc[96:P, 0:W].bitcast(I32))

        def fill_planes(s, queue):
            for quad in range(4):
                queue.dma_start(
                    planes[s][32 * quad : 32 * quad + 4].bitcast(I32),
                    joined[s][96 + 8 * quad : 96 + 8 * quad + 8, :].bitcast(I32),
                )

        gn_abs = shared.tile([P, GROUPS, 16], F32, name="gn_abs", align_bytes=64, offset=63488 - 64)
        root = keep.tile([P, GROUPS, SLOTS], F32, name="root")
        nc.vector.scalar_tensor_tensor(gn_abs[:, :, 0:SLOTS], gain[:], -1.0, gain[:], ALU.mult, ALU.max)
        is_pos = keep.tile([P, GROUPS, SLOTS], F32, name="is_pos")
        nc.vector.tensor_scalar(is_pos[:], gain[:], 0.0, 2.0, ALU.is_ge, ALU.mult)
        nc.scalar.activation(root[:], gn_abs[:, :, 0:SLOTS], ACT.Sqrt)
        join_scales(0)
        fill_planes(0, nc.sync)
        load_weight(1, 0, [0, 1], 21120)

        sign = keep.tile([P, GROUPS, SLOTS], F32, name="sign")
        nc.gpsimd.tensor_scalar(sign[:], is_pos[:], 1.0, -1.0, ALU.mult, ALU.add)
        join_scales(1)

        fb_rows = fb.rearrange("(g p t) n -> g p (t n)", g=GROUPS, t=SLOTS)
        nc.sync.dma_start(fb_raw[0][:].rearrange("p t n -> p (t n)"), fb_rows[0])
        fill_planes(1, nc.sync)
        nc.sync.dma_start(fb_raw[1][:].rearrange("p t n -> p (t n)"), fb_rows[1])
        load_weight(0, 1, [0, 1], 32768)
        load_weight(1, 1, [0, 1], 90112 + 4096)
        nc.sync.dma_start(level[:], ts)

        v = [keep.tile([P, PASSES, 2 * W], U8, name="v%d" % jh, align_bytes=64) for jh in range(HALVES)]
        w_q = {}

        def gather_words(j0, cols, offset):
            pair = shared.tile([P, cols], U32, name="pair%d" % j0, align_bytes=64, offset=57344 + offset)
            nc.vector.tensor_copy(pair[:], tab[:].bitcast(U32).indirect(offsets[:, j0 // 16 : (j0 + cols) // 16]))
            return pair

        def part_words(j0, pair):
            jh, c0 = divmod(j0, W)
            halves = pair[:].bitcast(U16).rearrange("p (c d) -> p d c", d=2)
            nc.vector.tensor_copy(v[jh][:].bitcast(U16)[:, :, c0 : c0 + pair.shape[1]], halves)

        def order_weight(w, g, passes, copy, offset):
            tile = shared.tile([P, len(passes), SLOTS, P], U32, name="w_q%d%d%d" % (w, g, passes[0]), align_bytes=64, offset=offset)
            copy(
                tile[:].rearrange("p a t m -> p a m t"),
                w_raw[w, g, 0][:, passes[0] : passes[-1] + 1].bitcast(U32).rearrange("p a (m t) -> p a m t", t=SLOTS),
            )
            for i, a in enumerate(passes):
                w_q[w, g, a] = tile[:, i]

        def product(sums, g, t, w, a, j0, cols):
            jh, c0 = divmod(j0, W)
            f0 = (1 + w) * W + t * P
            nc.tensor.matmul_mx(
                out=sums,
                lhsT=w_q[w, g, a][:, t, :].bitcast(FP8X4),
                lhsT_scale=planes[g][:, a, f0 : f0 + P],
                rhs=v[jh][:, a, 2 * c0 : 2 * (c0 + cols)].bitcast(FP4X4),
                rhs_scale=planes[jh][:, a, c0 : c0 + cols],
                start=(a == 0),
                stop=(a == PASSES - 1),
            )

        def square(dst, src, roots, t):
            nc.scalar.activation(dst, src, ACT.Square, scale=roots[:, t : t + 1])

        def first_squares():
            sq_re = shared.tile([P, SLOTS, W], F32, name="sq_first_re", align_bytes=64, offset=69632)
            sq_im = [keep.tile([P, SLOTS, Q], F32, name="sq_first_im%d" % i, align_bytes=64) for i in range(2)]
            banks = [next_bank([P, W]) for t in range(SLOTS)]
            for t in range(SLOTS):
                for a in range(PASSES):
                    product(banks[t][:], 0, t, 0, a, 0, W)
            for t in range(SLOTS):
                square(sq_re[:, t, :], banks[t][:], root[:, 0, :], t)
            for j0 in range(0, W, Q):
                for t0 in range(0, SLOTS, 2):
                    sums = next_bank([P, 2, Q])
                    for t in range(t0, t0 + 2):
                        for a in range(PASSES):
                            product(sums[:, t - t0, :], 0, t, 1, a, j0, Q)
                    for t in range(t0, t0 + 2):
                        square(sq_im[j0 // Q][:, t, :], sums[:, t - t0, :], root[:, 0, :], t)
            return [(sq_re[:, :, i * Q : (i + 1) * Q], sq_im[i][:]) for i in range(2)]

        def paired_squares(g, j0, cols=Q):
            sq = ring.tile([P, SLOTS, 2, cols], F32, name="sq", align_bytes=64, bufs=7)
            per_bank = W // (2 * cols)
            for t0 in range(0, SLOTS, per_bank):
                sums = next_bank([P, per_bank, 2, cols])
                for t in range(t0, t0 + per_bank):
                    for w in range(2):
                        for a in range(PASSES):
                            product(sums[:, t - t0, w, :], g, t, w, a, j0, cols)
                for t in range(t0, t0 + per_bank):
                    square(sq[:, t], sums[:, t - t0], root[:, g, :], t)
            return sq[:, :, 0, :], sq[:, :, 1, :]

        def power(sq, h=None):
            cols = sq[0].shape[2]
            if h is None:
                h = ring.tile([P, cols, SLOTS], BF16, name="h%d" % cols, align_bytes=64)
            nc.vector.tensor_tensor(
                h[:].rearrange("p (c i) t -> p c t i", i=2),
                sq[0].rearrange("p t (c i) -> p c t i", i=2),
                sq[1].rearrange("p t (c i) -> p c t i", i=2),
                ALU.add,
            )
            return h

        h_mx = {}

        def quantize(h, g, j0):
            cols = h.shape[1]
            h_q = keep.tile([P, cols], U32, name="h_q%d_%d" % (g, j0), align_bytes=64)
            h_sc = keep.tile([P, cols], U8, name="h_sc%d_%d" % (g, j0), align_bytes=64)
            nc.vector.quantize_mx(out=h_q[:].bitcast(FP8X4), scales=h_sc[:], in_=h[:].rearrange("p c t -> p (c t)"))
            for c in range(0, cols, P):
                h_mx[g, j0 + c] = (h_q[:, c:], h_sc[:, c:])

        fb_b = shared.tile([P, GROUPS, N, SLOTS], BF16, name="fb_b", align_bytes=64, offset=57344)
        fb_q = shared.tile([P, GROUPS, N], U32, name="fb_q", align_bytes=64, offset=90112 + 4096 + 2048)
        fb_sc = keep.tile([P, GROUPS, N], U8, name="fb_sc", align_bytes=64)

        def round_filters(g):
            nc.vector.tensor_tensor(
                fb_b[:, g].rearrange("p (c i) t -> p c t i", i=2),
                fb_raw[g][:].rearrange("p t (c i) -> p c t i", i=2),
                sign[:, g, :].unsqueeze(1).unsqueeze(3).broadcast_to([P, N // 2, SLOTS, 2]),
                ALU.mult,
            )

        def quantize_filters():
            nc.vector.quantize_mx(
                out=fb_q[:].rearrange("p g n -> p (g n)").bitcast(FP8X4),
                scales=fb_sc[:].rearrange("p g n -> p (g n)"),
                in_=fb_b[:].rearrange("p g n t -> p (g n t)"),
            )

        picked_level = shared.tile([P, J], F32, name="picked_level", align_bytes=64, offset=69632)
        filtered = {}

        def filter_products(j0, cols=Q):
            sums = next_bank([P, N // P, cols])
            filtered[j0] = sums
            for nt in range(N // P):
                for g in range(GROUPS):
                    nc.tensor.matmul_mx(
                        out=sums[:, nt, :],
                        lhsT=fb_q[:, g, nt * P : (nt + 1) * P].bitcast(FP8X4),
                        lhsT_scale=fb_sc[:, g, nt * P : (nt + 1) * P],
                        rhs=h_mx[g, j0][0][:, 0:cols].bitcast(FP8X4),
                        rhs_scale=h_mx[g, j0][1][:, 0:cols],
                        start=(g == 0),
                        stop=(g == GROUPS - 1),
                    )

        def finish(j0):
            cols = filtered[j0].shape[2]
            y = keep.tile([P, N // P, cols], F32, name="y%d" % j0, align_bytes=64)
            nc.vector.tensor_tensor(
                y[:], filtered[j0][:], picked_level[:, j0 : j0 + cols].unsqueeze(1).broadcast_to([P, N // P, cols]), ALU.mult
            )
            nc.sync.dma_start(out.rearrange("(nt p) j -> p nt j", p=P)[:, :, j0 : j0 + cols], y[:])

        pair0 = gather_words(0, Q, 1024)
        pair1 = gather_words(Q, Q, 2048)
        part_words(0, pair0)
        part_words(Q, pair1)
        order_weight(0, 0, [0], nc.scalar.copy, 61440)
        order_weight(0, 0, [1], nc.scalar.copy, 63488)
        pair2 = gather_words(W, W, 0)
        order_weight(1, 0, [0, 1], nc.vector.tensor_copy, 90112)
        part_words(W, pair2)
        sq_a = first_squares()
        round_filters(0)
        round_filters(1)
        sq_b = paired_squares(0, 2 * Q)
        h_a0 = power(sq_a[0], shared.tile([P, Q, SLOTS], BF16, name="h_a0", align_bytes=64, offset=28672))
        order_weight(0, 1, [0, 1], nc.vector.tensor_copy, 65536)
        h_a1 = power(sq_a[1], shared.tile([P, Q, SLOTS], BF16, name="h_a1", align_bytes=64, offset=28672 + 2048))
        order_weight(1, 1, [0, 1], nc.vector.tensor_copy, 16384)
        quantize(h_a0, 0, 0)
        quantize_filters()
        sq_c = paired_squares(0, 3 * Q)
        quantize(h_a1, 0, Q)
        h_b = power(sq_b, shared.tile([P, Q, SLOTS], BF16, name="h_b", align_bytes=64, offset=90112 + 4096))
        h_c = power(sq_c, shared.tile([P, Q, SLOTS], BF16, name="h_c", align_bytes=64, offset=69632 + 4096 + 2048))
        quantize(h_b, 0, 2 * Q)
        nc.vector.tensor_copy(picked_level[:], level[:].indirect(offsets[:]))
        sq_0 = paired_squares(1, 0)
        h_0 = power(sq_0, shared.tile([P, Q, SLOTS], BF16, name="h_0", align_bytes=64, offset=0))
        quantize(h_c, 0, 3 * Q)
        sq_1 = paired_squares(1, Q)
        quantize(h_0, 1, 0)
        h_1 = power(sq_1, shared.tile([P, Q, SLOTS], BF16, name="h_1", align_bytes=64, offset=2048))
        sq_2 = paired_squares(1, 2 * Q)
        sq_3 = paired_squares(1, 3 * Q, P)
        sq_4 = paired_squares(1, 3 * Q + P, P)
        filter_products(0)
        quantize(h_1, 1, Q)
        filter_products(Q)
        h_2 = power(sq_2)
        finish(0)
        quantize(h_2, 1, 2 * Q)
        filter_products(2 * Q)
        h_3 = power(sq_3)
        h_4 = power(sq_4)
        quantize(h_3, 1, 3 * Q)
        filter_products(3 * Q, P)
        quantize(h_4, 1, 3 * Q + P)
        filter_products(3 * Q + P, P)
        finish(Q)
        finish(2 * Q)
        finish(3 * Q)
        finish(3 * Q + P)
